import numpy as np
import ml_dtypes


def mxq(x, axis, fmt="e4m3"):
    dtype, down = {"e4m3": (ml_dtypes.float8_e4m3fn, 7), "e5m2": (ml_dtypes.float8_e5m2, 14)}[fmt]
    v = np.moveaxis(np.asarray(x, np.float32).astype(ml_dtypes.bfloat16).astype(np.float64), axis, -1)
    blocks = v.reshape(v.shape[:-1] + (-1, 32))
    amax = np.abs(blocks).max(-1, keepdims=True)
    byte = np.maximum(np.where(amax > 0, np.frexp(amax)[1] - 1 + 127, 0) - down, 1)
    scale = np.exp2(byte - 127.0)
    codes = (blocks / scale).astype(np.float32).astype(dtype).astype(np.float64)
    return np.moveaxis((codes * scale).reshape(v.shape), -1, axis)


WIDE = False


def mx_kscale(k):
    if not WIDE:
        return np.ones(k)
    levels = np.array([18, -18])
    if k % 512:
        return np.exp2(np.random.permutation(np.resize(levels, k // 32))).repeat(32)
    a = np.empty((k // 512, 16))
    for p in range(k // 512):
        a[p, :8] = np.random.permutation(np.resize(levels, 8))
        for g in range(8):
            far = levels[np.abs(levels - a[p, g]) >= 10]
            a[p, g + 8] = far[np.random.randint(len(far))]
    return np.exp2(a.ravel()).repeat(32)


def f64(x):
    return np.asarray(x).astype(np.float64)


def striped(idx):
    return np.tile(np.asarray(idx).reshape(-1, 16).T, (8, 1)).astype(np.uint16)


def unstriped(offs):
    return offs[:16].T.reshape(-1).astype(np.int64)


E2M1 = np.array([0.0, 0.5, 1.0, 1.5, 2.0, 3.0, 4.0, 6.0, -0.0, -0.5, -1.0, -1.5, -2.0, -3.0, -4.0, -6.0])


def pack_weight(w, fmt):
    k, n = w.shape
    w = f64(np.asarray(w, np.float32).astype(ml_dtypes.bfloat16)).reshape(k // 32, 32, n)
    amax = np.abs(w).max(1)
    if fmt == "e4m3":
        byte = np.frexp(amax)[1] - 1 + 127 - 7
    else:
        mant, ex = np.frexp(amax / 6.0)
        byte = np.where(mant > 0.5, ex, ex - 1) + 127
    byte = np.clip(np.where(amax > 0, byte, 1), 1, 254)
    scaled = (w * np.exp2(127.0 - byte)[:, None, :]).reshape(k, n).astype(np.float32)
    by_word = np.ascontiguousarray(scaled.reshape(k // 512, 128, 4, n).transpose(0, 1, 3, 2))
    if fmt == "e4m3":
        words = by_word.astype(ml_dtypes.float8_e4m3fn).view(np.uint8)
    else:
        c = by_word.astype(ml_dtypes.float4_e2m1fn).view(np.uint8) & 0xF
        words = (c[..., 0::2] | (c[..., 1::2] << 4)).reshape(k // 512, 128, 2 * n)
    return np.ascontiguousarray(words), np.ascontiguousarray(byte.astype(np.uint8).reshape(k // 512, 16, n))


def unpack_weight(words, scales, fmt):
    g, _, n = scales.shape
    words = np.ascontiguousarray(words).reshape(g, 128, n, -1)
    if fmt == "e4m3":
        vals = words.view(ml_dtypes.float8_e4m3fn).astype(np.float64)
    else:
        nib = np.empty((g, 128, n, 4), np.uint8)
        nib[..., 0::2] = words & 0xF
        nib[..., 1::2] = words >> 4
        vals = E2M1[nib]
    vals = vals * np.repeat(np.exp2(scales.astype(np.float64) - 127.0), 8, axis=1)[..., None]
    return vals.transpose(0, 1, 3, 2).reshape(g * 512, n)


N, T, D, V = 512, 1024, 512, 1024


def setup_inputs():
    n = np.random.standard_normal
    idx = np.random.permutation(T)[:N]
    s = mx_kscale(D)[:, None]
    z = mx_kscale(V)[:, None]
    w = n((D, V)) / np.sqrt(D)
    wd, wv = pack_weight(w * s, "e4m3"), pack_weight(w.T / z, "e4m3")
    return {
        "xT": (n((D, T)) / s).astype(np.float32),
        "wd_words": wd[0],
        "wd_scales": wd[1],
        "wv_words": wv[0],
        "wv_scales": wv[1],
        "y": n((V, N)).astype(np.float32),
        "cw": (np.random.uniform(0.5, 1.5, (V, 1)) / np.sqrt(V) * z).astype(np.float32),
        "rw": np.tile(np.random.uniform(0.5, 1.5, N), (128, 1)).astype(np.float32),
        "offs": striped(idx),
    }


def reference(xT, wd_words, wd_scales, wv_words, wv_scales, y, cw, rw, offs):
    idx = unstriped(offs)
    a = unpack_weight(wd_words, wd_scales, "e4m3").T @ mxq(f64(xT)[:, idx], 0, "e4m3")
    g = f64(cw) * f64(rw)[:1] * (a - f64(y))
    dx = unpack_weight(wv_words, wv_scales, "e4m3").T @ mxq(g, 0, "e5m2")
    gx = np.zeros((D, T))
    gx[:, idx] = dx
    return gx

@@ -1,0 +1,229 @@
+from contextlib import ExitStack
+
+import concourse.mybir as mybir
+from concourse.masks import make_identity
+
+N, T, D, V = 512, 1024, 512, 1024
+FLOPS = 2 * 2 * N * D * V
+
+F32 = mybir.dt.float32
+BF16 = mybir.dt.bfloat16
+I32 = mybir.dt.int32
+U32 = mybir.dt.uint32
+U16 = mybir.dt.uint16
+U8 = mybir.dt.uint8
+E4M3 = mybir.dt.float8_e4m3fn_x4
+E5M2 = mybir.dt.float8_e5m2_x4
+COPY = mybir.ActivationFunctionType.Copy
+MULT = mybir.AluOpType.mult
+SUB = mybir.AluOpType.subtract
+
+P = 128
+LANES = 4
+PASSES = V // (P * LANES)
+CHUNK = 128
+CHUNKS = N // CHUNK
+HALF = N // 2
+LIST_COLS = CHUNK // 16
+
+
+def tile_attend_gml_sq_kernel(tc, xT, wd_words, wd_scales, wv_words, wv_scales, y, cw, rw, offs, out):
+    nc = tc.nc
+    with ExitStack() as ctx:
+        keep = ctx.enter_context(tc.tile_pool(name="keep", bufs=1))
+        work = ctx.enter_context(tc.tile_pool(name="work", bufs=2))
+        psum = ctx.enter_context(tc.psum_pool(name="psum", bufs=2))
+
+        offsets = keep.tile([P, N // 16], U16, name="offsets")
+        wd_raw = keep.tile([P, V], I32, name="wd_raw", align_bytes=64)
+        wd_raw_scale = keep.tile([P, V], U8, name="wd_raw_scale", align_bytes=64)
+        wd_codes = keep.tile([P, V], I32, name="wd_codes", align_bytes=64)
+        wd_scale = keep.tile([P, V], U8, name="wd_scale", align_bytes=64)
+        wv_codes = keep.tile([P, PASSES, D], I32, name="wv_codes", align_bytes=64)
+        wv_scale = keep.tile([P, PASSES, D], U8, name="wv_scale", align_bytes=64)
+        cw_sb = keep.tile([P, PASSES, LANES], F32, name="cw_sb")
+        rw_sb = [keep.tile([P, HALF], F32, name=f"rw_sb{h}") for h in range(2)]
+        x_raw = [[keep.tile([P, 2, T // 2], F32, name=f"x_raw{u}{h}") for h in range(2)] for u in range(2)]
+        x_pairs = [keep.tile([P, T], U32, name=f"x_pairs{u}") for u in range(2)]
+        x_listed = keep.tile([P, N, 2], U32, name="x_listed", align_bytes=64)
+        x_codes = keep.tile([P, N], U32, name="x_codes", align_bytes=64)
+        x_scale = keep.tile([P, N], U8, name="x_scale", align_bytes=64)
+        y_sb = [[keep.tile([P, LANES, HALF], F32, name=f"y_sb{h}{o}") for o in range(PASSES)] for h in range(2)]
+        weight = [keep.tile([P, PASSES, LANES, HALF], F32, name=f"weight{h}") for h in range(2)]
+        windows = [keep.tile([P, T], F32, name=f"window{j}") for j in range(D // P)]
+        dx_sb = [keep.tile([P, D // P, CHUNK], F32, name=f"dx_sb{c}") for c in range(CHUNKS)]
+        ident = keep.tile([P, P], F32, name="ident")
+
+        nc.vector.memset(wd_raw_scale[:].bitcast(I32), 0)
+        nc.vector.memset(wv_scale[:].rearrange("p o d -> p (o d)").bitcast(I32), 0)
+
+        x_rows = xT.rearrange("(p u e) c -> u p e c", u=2, e=2)
+        y_rows = y.rearrange("(o p t) i -> o p t i", o=PASSES, t=LANES)
+
+        def load_x(u, h):
+            nc.sync.dma_start(x_raw[u][h][:], x_rows[u][:, :, h * (T // 2) : (h + 1) * (T // 2)])
+
+        nc.sync.dma_start(wd_raw[:], wd_words[0].rearrange("p v t -> p (v t)").bitcast(I32))
+        for q in range(4):
+            nc.scalar.dma_start(wd_raw_scale[32 * q : 32 * q + 4, :].bitcast(I32), wd_scales[0, 4 * q : 4 * q + 4, :].bitcast(I32))
+        load_x(0, 0)
+        load_x(0, 1)
+        load_x(1, 0)
+        nc.sync.dma_start(offsets[:], offs)
+        nc.scalar.dma_start(cw_sb[:], cw.rearrange("(o p t) one -> p o (t one)", o=PASSES, t=LANES))
+        nc.scalar.dma_start(rw_sb[0][:], rw[:, 0:HALF])
+        load_x(1, 1)
+        for o in range(PASSES):
+            nc.sync.dma_start(y_sb[0][o][:], y_rows[o][:, :, 0:HALF])
+        for q in range(4):
+            nc.sync.dma_start(
+                wv_scale[32 * q : 32 * q + 4, :, :].bitcast(I32),
+                wv_scales[:, 4 * q : 4 * q + 4, :].rearrange("o f d -> f o d").bitcast(I32),
+            )
+        nc.sync.dma_start(wv_codes[:], wv_words.rearrange("o p d t -> p o (d t)").bitcast(I32))
+        nc.sync.dma_start(rw_sb[1][:], rw[:, HALF:N])
+        for o in range(PASSES):
+            nc.sync.dma_start(y_sb[1][o][:], y_rows[o][:, :, HALF:N])
+
+        for window in windows:
+            nc.vector.memset(window[:], 0.0)
+        make_identity(nc, ident[:])
+
+        nc.vector.tensor_copy(
+            wd_codes[:].rearrange("p (o t m) -> p o m t", o=PASSES, t=LANES),
+            wd_raw[:].rearrange("p (o m t) -> p o m t", o=PASSES, t=LANES),
+        )
+        nc.vector.tensor_copy(
+            wd_scale[:].rearrange("p (o t m) -> p o m t", o=PASSES, t=LANES),
+            wd_raw_scale[:].rearrange("p (o m t) -> p o m t", o=PASSES, t=LANES),
+        )
+
+        def cast_x(u, h):
+            dst = x_pairs[u][:, h * (T // 2) : (h + 1) * (T // 2)].bitcast(BF16).rearrange("p (c e) -> p c e", e=2)
+            src = x_raw[u][h][:].rearrange("p e c -> p c e")
+            if h == 0:
+                nc.scalar.activation(dst, src, COPY)
+            else:
+                nc.vector.tensor_copy(dst, src)
+
+        def make_weight(h):
+            for o in range(PASSES):
+                for t in range(LANES):
+                    nc.scalar.activation(weight[h][:, o, t, :], rw_sb[h][:], COPY, scale=cw_sb[:, o, t : t + 1])
+
+        def gather(u, c0, c1):
+            nc.vector.tensor_copy(
+                x_listed[:, c0 * CHUNK : c1 * CHUNK, u],
+                x_pairs[u][:].indirect(offsets[:, c0 * LIST_COLS : c1 * LIST_COLS]),
+            )
+
+        def quantize_x(c0, c1):
+            cols = slice(c0 * CHUNK, c1 * CHUNK)
+            nc.vector.quantize_mx(
+                out=x_codes[:, cols].bitcast(E4M3),
+                scales=x_scale[:, cols],
+                in_=x_listed[:, cols, :].rearrange("p i u -> p (i u)").bitcast(BF16),
+            )
+
+        residual = {}
+        grad = {}
+
+        def head_and_residual(c):
+            cols = slice(c * CHUNK, (c + 1) * CHUNK)
+            h, within = divmod(c * CHUNK, HALF)
+            for o in range(PASSES):
+                a_bank = psum.tile([P, LANES, CHUNK], F32, name=f"a_bank{o}")
+                for t in range(LANES):
+                    w_cols = slice((o * LANES + t) * P, (o * LANES + t + 1) * P)
+                    nc.tensor.matmul_mx(
+                        out=a_bank[:, t, :],
+                        lhsT=wd_codes[:, w_cols].bitcast(E4M3),
+                        lhsT_scale=wd_scale[:, w_cols],
+                        rhs=x_codes[:, cols].bitcast(E4M3),
+                        rhs_scale=x_scale[:, cols],
+                        start=True,
+                        stop=True,
+                    )
+                residual[c, o] = keep.tile([P, LANES, CHUNK], F32, name=f"residual{c}{o}")
+                nc.vector.tensor_tensor(residual[c, o][:], a_bank[:], y_sb[h][o][:, :, within : within + CHUNK], SUB)
+
+        def weigh(c):
+            h, within = divmod(c * CHUNK, HALF)
+            engine = nc.vector if c == 0 else nc.gpsimd
+            grad[c] = keep.tile([P, PASSES, CHUNK, LANES], BF16, name=f"grad{c}", align_bytes=64)
+            for o in range(PASSES):
+                engine.tensor_tensor(
+                    grad[c][:, o, :, :],
+                    residual[c, o][:].rearrange("p t i -> p i t"),
+                    weight[h][:, o, :, within : within + CHUNK].rearrange("p t i -> p i t"),
+                    MULT,
+                )
+
+        def back_through_head(c):
+            g_codes = work.tile([P, PASSES, CHUNK], U32, name="g_codes", align_bytes=64)
+            g_scale = work.tile([P, PASSES, CHUNK], U8, name="g_scale", align_bytes=64)
+            nc.vector.quantize_mx(
+                out=g_codes[:].rearrange("p o i -> p (o i)").bitcast(E5M2),
+                scales=g_scale[:].rearrange("p o i -> p (o i)"),
+                in_=grad[c][:].rearrange("p o i t -> p (o i t)"),
+            )
+            dxt_bank = psum.tile([P, D], F32, name="dxt_bank")
+            for o in range(PASSES):
+                nc.tensor.matmul_mx(
+                    out=dxt_bank[:],
+                    lhsT=g_codes[:, o, :].bitcast(E5M2),
+                    lhsT_scale=g_scale[:, o, :],
+                    rhs=wv_codes[:, o, :].bitcast(E4M3),
+                    rhs_scale=wv_scale[:, o, :],
+                    start=(o == 0),
+                    stop=(o == PASSES - 1),
+                )
+            dxt_sb = work.tile([P, D], F32, name="dxt_sb")
+            nc.scalar.copy(dxt_sb[:], dxt_bank[:])
+            dx_bank = psum.tile([P, D // P, CHUNK], F32, name="dx_bank")
+            for j in range(D // P):
+                nc.tensor.transpose(dx_bank[:, j, :], dxt_sb[:, j * P : (j + 1) * P], ident[:])
+            nc.scalar.copy(dx_sb[c][:], dx_bank[:])
+
+        def scatter(c, j):
+            nc.vector.tensor_copy(
+                windows[j][:].indirect(offsets[:, c * LIST_COLS : (c + 1) * LIST_COLS]),
+                dx_sb[c][:, j, :],
+            )
+            if c == CHUNKS - 1:
+                nc.sync.dma_start(out[j * P : (j + 1) * P, :], windows[j][:])
+
+        cast_x(0, 0)
+        cast_x(0, 1)
+        gather(0, 0, CHUNKS)
+        cast_x(1, 0)
+        cast_x(1, 1)
+        make_weight(0)
+        gather(1, 0, 1)
+        gather(1, 1, 2)
+        quantize_x(0, 1)
+        gather(1, 2, 4)
+        quantize_x(1, 2)
+        head_and_residual(0)
+        quantize_x(2, 4)
+        weigh(0)
+        head_and_residual(1)
+        back_through_head(0)
+        weigh(1)
+        make_weight(1)
+        head_and_residual(2)
+        weigh(2)
+        head_and_residual(3)
+        weigh(3)
+        scatter(0, 0)
+        back_through_head(1)
+        for j in range(1, 4):
+            scatter(0, j)
+        scatter(1, 0)
+        back_through_head(2)
+        for j in range(1, 4):
+            scatter(1, j)
+        back_through_head(3)
+        for j in range(4):
+            scatter(2, j)
+            scatter(3, j)

@@ -25,6 +25,7 @@ CHUNK = 128
 CHUNKS = N // CHUNK
 HALF = N // 2
 LIST_COLS = CHUNK // 16
+X_PIECES = (((0, 512), (512, 1024)), ((0, 512), (512, 768), (768, 1024)))
 
 
 def tile_attend_gml_sq_kernel(tc, xT, wd_words, wd_scales, wv_words, wv_scales, y, cw, rw, offs, out):
@@ -43,7 +44,7 @@ def tile_attend_gml_sq_kernel(tc, xT, wd_words, wd_scales, wv_words, wv_scales, 
         wv_scale = keep.tile([P, PASSES, D], U8, name="wv_scale", align_bytes=64)
         cw_sb = keep.tile([P, PASSES, LANES], F32, name="cw_sb")
         rw_sb = [keep.tile([P, HALF], F32, name=f"rw_sb{h}") for h in range(2)]
-        x_raw = [[keep.tile([P, 2, T // 2], F32, name=f"x_raw{u}{h}") for h in range(2)] for u in range(2)]
+        x_raw = [[keep.tile([P, 2, b - a], F32, name=f"x_raw{u}_{a}") for a, b in X_PIECES[u]] for u in range(2)]
         x_pairs = [keep.tile([P, T], U32, name=f"x_pairs{u}") for u in range(2)]
         x_listed = keep.tile([P, N, 2], U32, name="x_listed", align_bytes=64)
         x_codes = keep.tile([P, N], U32, name="x_codes", align_bytes=64)
@@ -60,8 +61,9 @@ def tile_attend_gml_sq_kernel(tc, xT, wd_words, wd_scales, wv_words, wv_scales, 
         x_rows = xT.rearrange("(p u e) c -> u p e c", u=2, e=2)
         y_rows = y.rearrange("(o p t) i -> o p t i", o=PASSES, t=LANES)
 
-        def load_x(u, h):
-            nc.sync.dma_start(x_raw[u][h][:], x_rows[u][:, :, h * (T // 2) : (h + 1) * (T // 2)])
+        def load_x(u, k):
+            a, b = X_PIECES[u][k]
+            nc.sync.dma_start(x_raw[u][k][:], x_rows[u][:, :, a:b])
 
         nc.sync.dma_start(wd_raw[:], wd_words[0].rearrange("p v t -> p (v t)").bitcast(I32))
         for q in range(4):
@@ -73,6 +75,7 @@ def tile_attend_gml_sq_kernel(tc, xT, wd_words, wd_scales, wv_words, wv_scales, 
         nc.scalar.dma_start(cw_sb[:], cw.rearrange("(o p t) one -> p o (t one)", o=PASSES, t=LANES))
         nc.scalar.dma_start(rw_sb[0][:], rw[:, 0:HALF])
         load_x(1, 1)
+        load_x(1, 2)
         for o in range(PASSES):
             nc.sync.dma_start(y_sb[0][o][:], y_rows[o][:, :, 0:HALF])
         for q in range(4):
@@ -86,7 +89,7 @@ def tile_attend_gml_sq_kernel(tc, xT, wd_words, wd_scales, wv_words, wv_scales, 
             nc.sync.dma_start(y_sb[1][o][:], y_rows[o][:, :, HALF:N])
 
         for window in windows:
-            nc.vector.memset(window[:], 0.0)
+            nc.vector.memset(window[:].bitcast(I32), 0)
         make_identity(nc, ident[:])
 
         nc.vector.tensor_copy(
@@ -98,10 +101,11 @@ def tile_attend_gml_sq_kernel(tc, xT, wd_words, wd_scales, wv_words, wv_scales, 
             wd_raw_scale[:].rearrange("p (o m t) -> p o m t", o=PASSES, t=LANES),
         )
 
-        def cast_x(u, h):
-            dst = x_pairs[u][:, h * (T // 2) : (h + 1) * (T // 2)].bitcast(BF16).rearrange("p (c e) -> p c e", e=2)
-            src = x_raw[u][h][:].rearrange("p e c -> p c e")
-            if h == 0:
+        def cast_x(u, k):
+            a, b = X_PIECES[u][k]
+            dst = x_pairs[u][:, a:b].bitcast(BF16).rearrange("p (c e) -> p c e", e=2)
+            src = x_raw[u][k][:].rearrange("p e c -> p c e")
+            if k == 0:
                 nc.scalar.activation(dst, src, COPY)
             else:
                 nc.vector.tensor_copy(dst, src)
@@ -149,7 +153,7 @@ def tile_attend_gml_sq_kernel(tc, xT, wd_words, wd_scales, wv_words, wv_scales, 
 
         def weigh(c):
             h, within = divmod(c * CHUNK, HALF)
-            engine = nc.vector if c == 0 else nc.gpsimd
+            engine = nc.vector if c == 0 else nc.vector
             grad[c] = keep.tile([P, PASSES, CHUNK, LANES], BF16, name=f"grad{c}", align_bytes=64)
             for o in range(PASSES):
                 engine.tensor_tensor(
@@ -198,6 +202,7 @@ def tile_attend_gml_sq_kernel(tc, xT, wd_words, wd_scales, wv_words, wv_scales, 
         gather(0, 0, CHUNKS)
         cast_x(1, 0)
         cast_x(1, 1)
+        cast_x(1, 2)
         make_weight(0)
         gather(1, 0, 1)
         gather(1, 1, 2)
@@ -209,21 +214,20 @@ def tile_attend_gml_sq_kernel(tc, xT, wd_words, wd_scales, wv_words, wv_scales, 
         weigh(0)
         head_and_residual(1)
         back_through_head(0)
-        weigh(1)
         make_weight(1)
+        weigh(1)
         head_and_residual(2)
+        back_through_head(1)
         weigh(2)
         head_and_residual(3)
+        back_through_head(2)
         weigh(3)
         scatter(0, 0)
-        back_through_head(1)
+        back_through_head(3)
         for j in range(1, 4):
             scatter(0, j)
-        scatter(1, 0)
-        back_through_head(2)
-        for j in range(1, 4):
+        for j in range(4):
             scatter(1, j)
-        back_through_head(3)
         for j in range(4):
             scatter(2, j)
             scatter(3, j)

@@ -21,10 +21,12 @@ SUB = mybir.AluOpType.subtract
 P = 128
 LANES = 4
 PASSES = V // (P * LANES)
+D_TILES = D // P
 CHUNK = 128
 CHUNKS = N // CHUNK
 HALF = N // 2
 LIST_COLS = CHUNK // 16
+RUN = 4
 X_PIECES = (((0, 512), (512, 1024)), ((0, 512), (512, 768), (768, 1024)))
 
 
@@ -32,8 +34,8 @@ def tile_attend_gml_sq_kernel(tc, xT, wd_words, wd_scales, wv_words, wv_scales, 
     nc = tc.nc
     with ExitStack() as ctx:
         keep = ctx.enter_context(tc.tile_pool(name="keep", bufs=1))
-        work = ctx.enter_context(tc.tile_pool(name="work", bufs=2))
-        psum = ctx.enter_context(tc.psum_pool(name="psum", bufs=2))
+        psum2 = ctx.enter_context(tc.psum_pool(name="psum2", bufs=2))
+        psum1 = ctx.enter_context(tc.psum_pool(name="psum1", bufs=1))
 
         offsets = keep.tile([P, N // 16], U16, name="offsets")
         wd_raw = keep.tile([P, V], I32, name="wd_raw", align_bytes=64)
@@ -51,8 +53,14 @@ def tile_attend_gml_sq_kernel(tc, xT, wd_words, wd_scales, wv_words, wv_scales, 
         x_scale = keep.tile([P, N], U8, name="x_scale", align_bytes=64)
         y_sb = [[keep.tile([P, LANES, HALF], F32, name=f"y_sb{h}{o}") for o in range(PASSES)] for h in range(2)]
         weight = [keep.tile([P, PASSES, LANES, HALF], F32, name=f"weight{h}") for h in range(2)]
-        windows = [keep.tile([P, T], F32, name=f"window{j}") for j in range(D // P)]
-        dx_sb = [keep.tile([P, D // P, CHUNK], F32, name=f"dx_sb{c}") for c in range(CHUNKS)]
+        residual = [[keep.tile([P, LANES, CHUNK], F32, name=f"residual{c}{o}") for o in range(PASSES)] for c in range(CHUNKS)]
+        grad = [keep.tile([P, N * LANES], BF16, name=f"grad{o}", align_bytes=64) for o in range(PASSES)]
+        g_codes = [keep.tile([P, N], U32, name=f"g_codes{o}", align_bytes=64) for o in range(PASSES)]
+        g_scale = [keep.tile([P, N], U8, name=f"g_scale{o}", align_bytes=64) for o in range(PASSES)]
+        first_turned = keep.tile([P, D], F32, name="first_turned")
+        dx_first = keep.tile([P, D_TILES, CHUNK], F32, name="dx_first")
+        dx_rest = [keep.tile([P, N - CHUNK], F32, name=f"dx_rest{j}") for j in range(D_TILES)]
+        windows = [keep.tile([P, T], F32, name=f"window{j}") for j in range(D_TILES)]
         ident = keep.tile([P, P], F32, name="ident")
 
         nc.vector.memset(wd_raw_scale[:].bitcast(I32), 0)
@@ -129,73 +137,78 @@ def tile_attend_gml_sq_kernel(tc, xT, wd_words, wd_scales, wv_words, wv_scales, 
                 in_=x_listed[:, cols, :].rearrange("p i u -> p (i u)").bitcast(BF16),
             )
 
-        residual = {}
-        grad = {}
-
-        def head_and_residual(c):
+        def subtract_targets(c, o):
             cols = slice(c * CHUNK, (c + 1) * CHUNK)
             h, within = divmod(c * CHUNK, HALF)
-            for o in range(PASSES):
-                a_bank = psum.tile([P, LANES, CHUNK], F32, name=f"a_bank{o}")
-                for t in range(LANES):
-                    w_cols = slice((o * LANES + t) * P, (o * LANES + t + 1) * P)
-                    nc.tensor.matmul_mx(
-                        out=a_bank[:, t, :],
-                        lhsT=wd_codes[:, w_cols].bitcast(E4M3),
-                        lhsT_scale=wd_scale[:, w_cols],
-                        rhs=x_codes[:, cols].bitcast(E4M3),
-                        rhs_scale=x_scale[:, cols],
-                        start=True,
-                        stop=True,
-                    )
-                residual[c, o] = keep.tile([P, LANES, CHUNK], F32, name=f"residual{c}{o}")
-                nc.vector.tensor_tensor(residual[c, o][:], a_bank[:], y_sb[h][o][:, :, within : within + CHUNK], SUB)
-
-        def weigh(c):
-            h, within = divmod(c * CHUNK, HALF)
-            engine = nc.vector if c == 0 else nc.vector
-            grad[c] = keep.tile([P, PASSES, CHUNK, LANES], BF16, name=f"grad{c}", align_bytes=64)
-            for o in range(PASSES):
-                engine.tensor_tensor(
-                    grad[c][:, o, :, :],
-                    residual[c, o][:].rearrange("p t i -> p i t"),
-                    weight[h][:, o, :, within : within + CHUNK].rearrange("p t i -> p i t"),
-                    MULT,
+            a_bank = psum2.tile([P, LANES, CHUNK], F32, name=f"a_bank{o}")
+            for t in range(LANES):
+                w_cols = slice((o * LANES + t) * P, (o * LANES + t + 1) * P)
+                nc.tensor.matmul_mx(
+                    out=a_bank[:, t, :],
+                    lhsT=wd_codes[:, w_cols].bitcast(E4M3),
+                    lhsT_scale=wd_scale[:, w_cols],
+                    rhs=x_codes[:, cols].bitcast(E4M3),
+                    rhs_scale=x_scale[:, cols],
+                    start=True,
+                    stop=True,
                 )
+            nc.vector.tensor_tensor(residual[c][o][:], a_bank[:], y_sb[h][o][:, :, within : within + CHUNK], SUB)
 
-        def back_through_head(c):
-            g_codes = work.tile([P, PASSES, CHUNK], U32, name="g_codes", align_bytes=64)
-            g_scale = work.tile([P, PASSES, CHUNK], U8, name="g_scale", align_bytes=64)
-            nc.vector.quantize_mx(
-                out=g_codes[:].rearrange("p o i -> p (o i)").bitcast(E5M2),
-                scales=g_scale[:].rearrange("p o i -> p (o i)"),
-                in_=grad[c][:].rearrange("p o i t -> p (o i t)"),
+        def weigh(c, o):
+            h, within = divmod(c * CHUNK, HALF)
+            nc.vector.tensor_tensor(
+                grad[o][:, c * CHUNK * LANES : (c + 1) * CHUNK * LANES].rearrange("p (r i t) -> p r t i", i=RUN, t=LANES),
+                residual[c][o][:].rearrange("p t (r i) -> p r t i", i=RUN),
+                weight[h][:, o, :, within : within + CHUNK].rearrange("p t (r i) -> p r t i", i=RUN),
+                MULT,
             )
-            dxt_bank = psum.tile([P, D], F32, name="dxt_bank")
+
+        def quantize_grad(c0, c1, o):
+            cols = slice(c0 * CHUNK, c1 * CHUNK)
+            nc.vector.quantize_mx(
+                out=g_codes[o][:, cols].bitcast(E5M2),
+                scales=g_scale[o][:, cols],
+                in_=grad[o][:, cols.start * LANES : cols.stop * LANES],
+            )
+
+        def back_first_chunk():
+            turned_bank = psum1.tile([P, D], F32, name="turned_bank")
             for o in range(PASSES):
                 nc.tensor.matmul_mx(
-                    out=dxt_bank[:],
-                    lhsT=g_codes[:, o, :].bitcast(E5M2),
-                    lhsT_scale=g_scale[:, o, :],
+                    out=turned_bank[:],
+                    lhsT=g_codes[o][:, 0:CHUNK].bitcast(E5M2),
+                    lhsT_scale=g_scale[o][:, 0:CHUNK],
                     rhs=wv_codes[:, o, :].bitcast(E4M3),
                     rhs_scale=wv_scale[:, o, :],
                     start=(o == 0),
                     stop=(o == PASSES - 1),
                 )
-            dxt_sb = work.tile([P, D], F32, name="dxt_sb")
-            nc.scalar.copy(dxt_sb[:], dxt_bank[:])
-            dx_bank = psum.tile([P, D // P, CHUNK], F32, name="dx_bank")
-            for j in range(D // P):
-                nc.tensor.transpose(dx_bank[:, j, :], dxt_sb[:, j * P : (j + 1) * P], ident[:])
-            nc.scalar.copy(dx_sb[c][:], dx_bank[:])
+            nc.scalar.copy(first_turned[:], turned_bank[:])
+            first_bank = psum1.tile([P, D_TILES, CHUNK], F32, name="first_bank")
+            for j in range(D_TILES):
+                nc.tensor.transpose(first_bank[:, j, :], first_turned[:, j * P : (j + 1) * P], ident[:])
+            nc.scalar.copy(dx_first[:], first_bank[:])
 
-        def scatter(c, j):
-            nc.vector.tensor_copy(
-                windows[j][:].indirect(offsets[:, c * LIST_COLS : (c + 1) * LIST_COLS]),
-                dx_sb[c][:, j, :],
-            )
-            if c == CHUNKS - 1:
-                nc.sync.dma_start(out[j * P : (j + 1) * P, :], windows[j][:])
+        def back_rest(j):
+            dx_bank = psum2.tile([P, N], F32, name="dx_bank")
+            for o in range(PASSES):
+                nc.tensor.matmul_mx(
+                    out=dx_bank[:],
+                    lhsT=wv_codes[:, o, j * P : (j + 1) * P].bitcast(E4M3),
+                    lhsT_scale=wv_scale[:, o, j * P : (j + 1) * P],
+                    rhs=g_codes[o][:].bitcast(E5M2),
+                    rhs_scale=g_scale[o][:],
+                    start=(o == 0),
+                    stop=(o == PASSES - 1),
+                )
+            nc.scalar.copy(dx_rest[j][:], dx_bank[:, CHUNK:N])
+
+        def scatter_first(j):
+            nc.vector.tensor_copy(windows[j][:].indirect(offsets[:, 0:LIST_COLS]), dx_first[:, j, :])
+
+        def scatter_rest(j):
+            nc.vector.tensor_copy(windows[j][:].indirect(offsets[:, LIST_COLS : CHUNKS * LIST_COLS]), dx_rest[j][:])
+            nc.sync.dma_start(out[j * P : (j + 1) * P, :], windows[j][:])
 
         cast_x(0, 0)
         cast_x(0, 1)
@@ -204,30 +217,41 @@ def tile_attend_gml_sq_kernel(tc, xT, wd_words, wd_scales, wv_words, wv_scales, 
         cast_x(1, 1)
         cast_x(1, 2)
         make_weight(0)
-        gather(1, 0, 1)
         gather(1, 1, 2)
-        quantize_x(0, 1)
-        gather(1, 2, 4)
         quantize_x(1, 2)
-        head_and_residual(0)
+        gather(1, 0, 1)
+        gather(1, 2, 4)
+        quantize_x(0, 1)
+        subtract_targets(1, 0)
         quantize_x(2, 4)
-        weigh(0)
-        head_and_residual(1)
-        back_through_head(0)
+        subtract_targets(1, 1)
         make_weight(1)
-        weigh(1)
-        head_and_residual(2)
-        back_through_head(1)
-        weigh(2)
-        head_and_residual(3)
-        back_through_head(2)
-        weigh(3)
-        scatter(0, 0)
-        back_through_head(3)
-        for j in range(1, 4):
-            scatter(0, j)
-        for j in range(4):
-            scatter(1, j)
-        for j in range(4):
-            scatter(2, j)
-            scatter(3, j)
+        weigh(1, 0)
+        weigh(1, 1)
+        subtract_targets(0, 0)
+        quantize_grad(1, 2, 0)
+        subtract_targets(0, 1)
+        quantize_grad(1, 2, 1)
+        weigh(0, 0)
+        weigh(0, 1)
+        quantize_grad(0, 1, 0)
+        subtract_targets(2, 0)
+        quantize_grad(0, 1, 1)
+        back_first_chunk()
+        subtract_targets(2, 1)
+        weigh(2, 0)
+        weigh(2, 1)
+        subtract_targets(3, 0)
+        quantize_grad(2, 3, 0)
+        subtract_targets(3, 1)
+        quantize_grad(2, 3, 1)
+        weigh(3, 0)
+        weigh(3, 1)
+        quantize_grad(3, 4, 0)
+        quantize_grad(3, 4, 1)
+        for j in range(D_TILES):
+            back_rest(j)
+        for j in range(D_TILES):
+            scatter_first(j)
+        for j in range(D_TILES):
+            scatter_rest(j)

@@ -20,7 +20,10 @@ SUB = mybir.AluOpType.subtract
 
 P = 128
 LANES = 4
-PASSES = V // (P * LANES)
+K_PASS = P * LANES
+PASSES = V // K_PASS
+PAIRS = 2
+QUADRANTS = 4
 D_TILES = D // P
 CHUNK = 128
 CHUNKS = N // CHUNK
@@ -38,17 +41,17 @@ def tile_attend_gml_sq_kernel(tc, xT, wd_words, wd_scales, wv_words, wv_scales, 
         psum1 = ctx.enter_context(tc.psum_pool(name="psum1", bufs=1))
 
         offsets = keep.tile([P, N // 16], U16, name="offsets")
-        wd_raw = keep.tile([P, V], I32, name="wd_raw", align_bytes=64)
+        wd_raw = [keep.tile([P, K_PASS], I32, name=f"wd_raw{o}") for o in range(PASSES)]
         wd_raw_scale = keep.tile([P, V], U8, name="wd_raw_scale", align_bytes=64)
-        wd_codes = keep.tile([P, V], I32, name="wd_codes", align_bytes=64)
+        wd_codes = [keep.tile([P, K_PASS], I32, name=f"wd_codes{o}", align_bytes=64) for o in range(PASSES)]
         wd_scale = keep.tile([P, V], U8, name="wd_scale", align_bytes=64)
         wv_codes = keep.tile([P, PASSES, D], I32, name="wv_codes", align_bytes=64)
         wv_scale = keep.tile([P, PASSES, D], U8, name="wv_scale", align_bytes=64)
         cw_sb = keep.tile([P, PASSES, LANES], F32, name="cw_sb")
         rw_sb = [keep.tile([P, HALF], F32, name=f"rw_sb{h}") for h in range(2)]
-        x_raw = [[keep.tile([P, 2, b - a], F32, name=f"x_raw{u}_{a}") for a, b in X_PIECES[u]] for u in range(2)]
-        x_pairs = [keep.tile([P, T], U32, name=f"x_pairs{u}") for u in range(2)]
-        x_listed = keep.tile([P, N, 2], U32, name="x_listed", align_bytes=64)
+        x_raw = [[keep.tile([P, 2, b - a], F32, name=f"x_raw{u}_{a}") for a, b in X_PIECES[u]] for u in range(PAIRS)]
+        x_pairs = [keep.tile([P, T], U32, name=f"x_pairs{u}") for u in range(PAIRS)]
+        x_listed = keep.tile([P, N, PAIRS], U32, name="x_listed", align_bytes=64)
         x_codes = keep.tile([P, N], U32, name="x_codes", align_bytes=64)
         x_scale = keep.tile([P, N], U8, name="x_scale", align_bytes=64)
         y_sb = [[keep.tile([P, LANES, HALF], F32, name=f"y_sb{h}{o}") for o in range(PASSES)] for h in range(2)]
@@ -63,30 +66,35 @@ def tile_attend_gml_sq_kernel(tc, xT, wd_words, wd_scales, wv_words, wv_scales, 
         windows = [keep.tile([P, T], F32, name=f"window{j}") for j in range(D_TILES)]
         ident = keep.tile([P, P], F32, name="ident")
 
-        nc.vector.memset(wd_raw_scale[:].bitcast(I32), 0)
-        nc.vector.memset(wv_scale[:].rearrange("p o d -> p (o d)").bitcast(I32), 0)
+        nc.gpsimd.memset(wd_raw_scale[:].bitcast(I32), 0)
+        nc.gpsimd.memset(wv_scale[:].rearrange("p o d -> p (o d)").bitcast(I32), 0)
 
-        x_rows = xT.rearrange("(p u e) c -> u p e c", u=2, e=2)
+        x_rows = xT.rearrange("(p u e) c -> u p e c", u=PAIRS, e=2)
         y_rows = y.rearrange("(o p t) i -> o p t i", o=PASSES, t=LANES)
 
         def load_x(u, k):
             a, b = X_PIECES[u][k]
             nc.sync.dma_start(x_raw[u][k][:], x_rows[u][:, :, a:b])
 
-        nc.sync.dma_start(wd_raw[:], wd_words[0].rearrange("p v t -> p (v t)").bitcast(I32))
-        for q in range(4):
+        def load_wd(o):
+            words = wd_words[0].rearrange("p v t -> p (v t)").bitcast(I32)
+            nc.sync.dma_start(wd_raw[o][:], words[:, o * K_PASS : (o + 1) * K_PASS])
+
+        nc.sync.dma_start(offsets[:], offs)
+        load_wd(0)
+        for q in range(QUADRANTS):
             nc.scalar.dma_start(wd_raw_scale[32 * q : 32 * q + 4, :].bitcast(I32), wd_scales[0, 4 * q : 4 * q + 4, :].bitcast(I32))
         load_x(0, 0)
         load_x(0, 1)
         load_x(1, 0)
-        nc.sync.dma_start(offsets[:], offs)
         nc.scalar.dma_start(cw_sb[:], cw.rearrange("(o p t) one -> p o (t one)", o=PASSES, t=LANES))
         nc.scalar.dma_start(rw_sb[0][:], rw[:, 0:HALF])
         load_x(1, 1)
         load_x(1, 2)
+        load_wd(1)
         for o in range(PASSES):
             nc.sync.dma_start(y_sb[0][o][:], y_rows[o][:, :, 0:HALF])
-        for q in range(4):
+        for q in range(QUADRANTS):
             nc.sync.dma_start(
                 wv_scale[32 * q : 32 * q + 4, :, :].bitcast(I32),
                 wv_scales[:, 4 * q : 4 * q + 4, :].rearrange("o f d -> f o d").bitcast(I32),
@@ -100,10 +108,13 @@ def tile_attend_gml_sq_kernel(tc, xT, wd_words, wd_scales, wv_words, wv_scales, 
             nc.vector.memset(window[:].bitcast(I32), 0)
         make_identity(nc, ident[:])
 
-        nc.vector.tensor_copy(
-            wd_codes[:].rearrange("p (o t m) -> p o m t", o=PASSES, t=LANES),
-            wd_raw[:].rearrange("p (o m t) -> p o m t", o=PASSES, t=LANES),
-        )
+        def reorder_wd(o):
+            nc.vector.tensor_copy(
+                wd_codes[o][:].rearrange("p (t m) -> p m t", t=LANES),
+                wd_raw[o][:].rearrange("p (m t) -> p m t", t=LANES),
+            )
+
+        reorder_wd(0)
         nc.vector.tensor_copy(
             wd_scale[:].rearrange("p (o t m) -> p o m t", o=PASSES, t=LANES),
             wd_raw_scale[:].rearrange("p (o m t) -> p o m t", o=PASSES, t=LANES),
@@ -142,11 +153,11 @@ def tile_attend_gml_sq_kernel(tc, xT, wd_words, wd_scales, wv_words, wv_scales, 
             h, within = divmod(c * CHUNK, HALF)
             a_bank = psum2.tile([P, LANES, CHUNK], F32, name=f"a_bank{o}")
             for t in range(LANES):
-                w_cols = slice((o * LANES + t) * P, (o * LANES + t + 1) * P)
+                scale_cols = slice((o * LANES + t) * P, (o * LANES + t + 1) * P)
                 nc.tensor.matmul_mx(
                     out=a_bank[:, t, :],
-                    lhsT=wd_codes[:, w_cols].bitcast(E4M3),
-                    lhsT_scale=wd_scale[:, w_cols],
+                    lhsT=wd_codes[o][:, t * P : (t + 1) * P].bitcast(E4M3),
+                    lhsT_scale=wd_scale[:, scale_cols],
                     rhs=x_codes[:, cols].bitcast(E4M3),
                     rhs_scale=x_scale[:, cols],
                     start=True,
@@ -163,8 +174,8 @@ def tile_attend_gml_sq_kernel(tc, xT, wd_words, wd_scales, wv_words, wv_scales, 
                 MULT,
             )
 
-        def quantize_grad(c0, c1, o):
-            cols = slice(c0 * CHUNK, c1 * CHUNK)
+        def quantize_grad(c, o):
+            cols = slice(c * CHUNK, (c + 1) * CHUNK)
             nc.vector.quantize_mx(
                 out=g_codes[o][:, cols].bitcast(E5M2),
                 scales=g_scale[o][:, cols],
@@ -206,52 +217,55 @@ def tile_attend_gml_sq_kernel(tc, xT, wd_words, wd_scales, wv_words, wv_scales, 
         def scatter_first(j):
             nc.vector.tensor_copy(windows[j][:].indirect(offsets[:, 0:LIST_COLS]), dx_first[:, j, :])
 
-        def scatter_rest(j):
+        def scatter_rest_and_store(j):
             nc.vector.tensor_copy(windows[j][:].indirect(offsets[:, LIST_COLS : CHUNKS * LIST_COLS]), dx_rest[j][:])
             nc.sync.dma_start(out[j * P : (j + 1) * P, :], windows[j][:])
 
         cast_x(0, 0)
         cast_x(0, 1)
         gather(0, 0, CHUNKS)
-        cast_x(1, 0)
-        cast_x(1, 1)
-        cast_x(1, 2)
+        for k in range(len(X_PIECES[1])):
+            cast_x(1, k)
         make_weight(0)
+
         gather(1, 1, 2)
         quantize_x(1, 2)
         gather(1, 0, 1)
         gather(1, 2, 4)
         quantize_x(0, 1)
+        reorder_wd(1)
         subtract_targets(1, 0)
         quantize_x(2, 4)
         subtract_targets(1, 1)
         make_weight(1)
+
         weigh(1, 0)
         weigh(1, 1)
         subtract_targets(0, 0)
-        quantize_grad(1, 2, 0)
+        quantize_grad(1, 0)
         subtract_targets(0, 1)
-        quantize_grad(1, 2, 1)
+        quantize_grad(1, 1)
         weigh(0, 0)
         weigh(0, 1)
-        quantize_grad(0, 1, 0)
+        quantize_grad(0, 0)
         subtract_targets(2, 0)
-        quantize_grad(0, 1, 1)
+        quantize_grad(0, 1)
         back_first_chunk()
         subtract_targets(2, 1)
         weigh(2, 0)
         weigh(2, 1)
         subtract_targets(3, 0)
-        quantize_grad(2, 3, 0)
+        quantize_grad(2, 0)
         subtract_targets(3, 1)
-        quantize_grad(2, 3, 1)
+        quantize_grad(2, 1)
         weigh(3, 0)
         weigh(3, 1)
-        quantize_grad(3, 4, 0)
-        quantize_grad(3, 4, 1)
+        quantize_grad(3, 0)
+        quantize_grad(3, 1)
+
         for j in range(D_TILES):
             back_rest(j)
         for j in range(D_TILES):
             scatter_first(j)
         for j in range(D_TILES):
-            scatter_rest(j)
+            scatter_rest_and_store(j)

@@ -31,14 +31,22 @@ HALF = N // 2
 LIST_COLS = CHUNK // 16
 RUN = 4
 X_PIECES = (((0, 512), (512, 1024)), ((0, 512), (512, 768), (768, 1024)))
+EARLY = (0,)
+LATE = (1, 2, 3)
+TURNED = ((1, 0), (1, 1))
+WEIGHTED = (0, 3, 2)
+G_COLS = {(0, 0): 0, (0, 1): 1, (1, 0): 2, (2, 0): 3, (3, 0): 4, (1, 1): 5, (2, 1): 6, (3, 1): 7}
+G_START = (CHUNK, N)
 
 
 def tile_attend_gml_sq_kernel(tc, xT, wd_words, wd_scales, wv_words, wv_scales, y, cw, rw, offs, out):
     nc = tc.nc
     with ExitStack() as ctx:
         keep = ctx.enter_context(tc.tile_pool(name="keep", bufs=1))
-        psum2 = ctx.enter_context(tc.psum_pool(name="psum2", bufs=2))
-        psum1 = ctx.enter_context(tc.psum_pool(name="psum1", bufs=1))
+        psum = ctx.enter_context(tc.psum_pool(name="psum", bufs=1))
+
+        def bank(b, shape, name):
+            return psum.tile(shape, F32, name=name, tag=f"bank{b}")
 
         offsets = keep.tile([P, N // 16], U16, name="offsets")
         wd_raw = [keep.tile([P, K_PASS], I32, name=f"wd_raw{o}") for o in range(PASSES)]
@@ -48,25 +56,32 @@ def tile_attend_gml_sq_kernel(tc, xT, wd_words, wd_scales, wv_words, wv_scales, 
         wv_codes = keep.tile([P, PASSES, D], I32, name="wv_codes", align_bytes=64)
         wv_scale = keep.tile([P, PASSES, D], U8, name="wv_scale", align_bytes=64)
         cw_sb = keep.tile([P, PASSES, LANES], F32, name="cw_sb")
-        rw_sb = [keep.tile([P, HALF], F32, name=f"rw_sb{h}") for h in range(2)]
+        cw_neg = keep.tile([P, PASSES, LANES], F32, name="cw_neg")
+        rw_rows = keep.tile([P, CHUNK], F32, name="rw_rows")
+        rw_col = keep.tile([P, CHUNKS], F32, name="rw_col")
         x_raw = [[keep.tile([P, 2, b - a], F32, name=f"x_raw{u}_{a}") for a, b in X_PIECES[u]] for u in range(PAIRS)]
         x_pairs = [keep.tile([P, T], U32, name=f"x_pairs{u}") for u in range(PAIRS)]
         x_listed = keep.tile([P, N, PAIRS], U32, name="x_listed", align_bytes=64)
         x_codes = keep.tile([P, N], U32, name="x_codes", align_bytes=64)
         x_scale = keep.tile([P, N], U8, name="x_scale", align_bytes=64)
         y_sb = [[keep.tile([P, LANES, HALF], F32, name=f"y_sb{h}{o}") for o in range(PASSES)] for h in range(2)]
-        weight = [keep.tile([P, PASSES, LANES, HALF], F32, name=f"weight{h}") for h in range(2)]
-        residual = [[keep.tile([P, LANES, CHUNK], F32, name=f"residual{c}{o}") for o in range(PASSES)] for c in range(CHUNKS)]
-        grad = [keep.tile([P, N * LANES], BF16, name=f"grad{o}", align_bytes=64) for o in range(PASSES)]
-        g_codes = [keep.tile([P, N], U32, name=f"g_codes{o}", align_bytes=64) for o in range(PASSES)]
-        g_scale = [keep.tile([P, N], U8, name=f"g_scale{o}", align_bytes=64) for o in range(PASSES)]
-        first_turned = keep.tile([P, D], F32, name="first_turned")
-        dx_first = keep.tile([P, D_TILES, CHUNK], F32, name="dx_first")
-        dx_rest = [keep.tile([P, N - CHUNK], F32, name=f"dx_rest{j}") for j in range(D_TILES)]
+        weight = keep.tile([P, len(WEIGHTED), LANES, PASSES, CHUNK], F32, name="weight")
+        residual = [keep.tile([P, LANES, PASSES, CHUNK], F32, name=f"residual{c}", tag=f"residual{c}") for c in range(CHUNKS)]
+        a_scaled = {(c, o): keep.tile([P, LANES, CHUNK], F32, name=f"a_scaled{c}{o}") for c, o in TURNED}
+        y_scaled = {(c, o): keep.tile([P, LANES, CHUNK], F32, name=f"y_scaled{c}{o}") for c, o in TURNED}
+        grad_turned = {(c, o): keep.tile([P, K_PASS], BF16, name=f"grad_turned{c}{o}", tag=f"grad_turned{c}{o}") for c, o in TURNED}
+        grad = {c: keep.tile([P, PASSES * CHUNK * LANES], BF16, name=f"grad{c}", align_bytes=64) for c in WEIGHTED}
+        grad_late = {(c, o): keep.tile([P, CHUNK * LANES], BF16, name=f"grad{c}{o}", align_bytes=64) for c, o in TURNED}
+        g_codes = keep.tile([P, PASSES * N], U32, name="g_codes", align_bytes=64)
+        g_scale = keep.tile([P, PASSES * N], U8, name="g_scale", align_bytes=64)
+        dx_turned = {c: keep.tile([P, D], F32, name=f"dx_turned{c}") for c in EARLY}
+        dx_early = {}
+        dx_rest = [keep.tile([P, len(LATE) * CHUNK], F32, name=f"dx_rest{j}") for j in range(D_TILES)]
         windows = [keep.tile([P, T], F32, name=f"window{j}") for j in range(D_TILES)]
         ident = keep.tile([P, P], F32, name="ident")
 
         nc.gpsimd.memset(wd_raw_scale[:].bitcast(I32), 0)
+        nc.gpsimd.memset(rw_rows[:], 0.0)
         nc.gpsimd.memset(wv_scale[:].rearrange("p o d -> p (o d)").bitcast(I32), 0)
 
         x_rows = xT.rearrange("(p u e) c -> u p e c", u=PAIRS, e=2)
@@ -84,29 +99,23 @@ def tile_attend_gml_sq_kernel(tc, xT, wd_words, wd_scales, wv_words, wv_scales, 
         load_wd(0)
         for q in range(QUADRANTS):
             nc.scalar.dma_start(wd_raw_scale[32 * q : 32 * q + 4, :].bitcast(I32), wd_scales[0, 4 * q : 4 * q + 4, :].bitcast(I32))
+        nc.scalar.dma_start(rw_rows[0:CHUNKS, :], rw[0:1, :].rearrange("one (c i) -> (one c) i", c=CHUNKS))
         load_x(0, 0)
         load_x(0, 1)
         load_x(1, 0)
-        nc.scalar.dma_start(cw_sb[:], cw.rearrange("(o p t) one -> p o (t one)", o=PASSES, t=LANES))
-        nc.scalar.dma_start(rw_sb[0][:], rw[:, 0:HALF])
         load_x(1, 1)
         load_x(1, 2)
+        nc.sync.dma_start(cw_sb[:], cw.rearrange("(o p t) one -> p o (t one)", o=PASSES, t=LANES))
         load_wd(1)
-        for o in range(PASSES):
-            nc.sync.dma_start(y_sb[0][o][:], y_rows[o][:, :, 0:HALF])
-        for q in range(QUADRANTS):
-            nc.sync.dma_start(
-                wv_scale[32 * q : 32 * q + 4, :, :].bitcast(I32),
-                wv_scales[:, 4 * q : 4 * q + 4, :].rearrange("o f d -> f o d").bitcast(I32),
-            )
+        nc.sync.dma_start(y_sb[0][0][:], y_rows[0][:, :, 0:HALF])
+        nc.sync.dma_start(y_sb[0][1][:], y_rows[1][:, :, 0:HALF])
+        nc.sync.dma_start(y_sb[1][0][:], y_rows[0][:, :, HALF:N])
         nc.sync.dma_start(wv_codes[:], wv_words.rearrange("o p d t -> p o (d t)").bitcast(I32))
-        nc.sync.dma_start(rw_sb[1][:], rw[:, HALF:N])
-        for o in range(PASSES):
-            nc.sync.dma_start(y_sb[1][o][:], y_rows[o][:, :, HALF:N])
+        nc.sync.dma_start(y_sb[1][1][:], y_rows[1][:, :, HALF:N])
 
-        for window in windows:
-            nc.vector.memset(window[:].bitcast(I32), 0)
         make_identity(nc, ident[:])
+        for j in range(D_TILES):
+            (nc.vector if j < 3 else nc.gpsimd).memset(windows[j][:].bitcast(I32), 0)
 
         def reorder_wd(o):
             nc.vector.tensor_copy(
@@ -120,6 +129,13 @@ def tile_attend_gml_sq_kernel(tc, xT, wd_words, wd_scales, wv_words, wv_scales, 
             wd_raw_scale[:].rearrange("p (o m t) -> p o m t", o=PASSES, t=LANES),
         )
 
+        def load_wv_scales():
+            for q in range(QUADRANTS):
+                nc.scalar.dma_start(
+                    wv_scale[32 * q : 32 * q + 4, :, :].bitcast(I32),
+                    wv_scales[:, 4 * q : 4 * q + 4, :].rearrange("o f d -> f o d").bitcast(I32),
+                )
+
         def cast_x(u, k):
             a, b = X_PIECES[u][k]
             dst = x_pairs[u][:, a:b].bitcast(BF16).rearrange("p (c e) -> p c e", e=2)
@@ -129,10 +145,17 @@ def tile_attend_gml_sq_kernel(tc, xT, wd_words, wd_scales, wv_words, wv_scales, 
             else:
                 nc.vector.tensor_copy(dst, src)
 
-        def make_weight(h):
+        def make_weight(b0, b):
+            col_bank = bank(b0, [P, P], "col_bank")
+            nc.tensor.transpose(col_bank[:], rw_rows[:], ident[:])
+            nc.scalar.copy(rw_col[:], col_bank[:, 0:CHUNKS])
+            rw_bank = bank(b, [P, len(WEIGHTED), CHUNK], "rw_bank")
+            for k, c in enumerate(WEIGHTED):
+                nc.tensor.transpose(rw_bank[:, k, :], rw_col[:, c : c + 1].to_broadcast([P, P]), ident[:])
             for o in range(PASSES):
                 for t in range(LANES):
-                    nc.scalar.activation(weight[h][:, o, t, :], rw_sb[h][:], COPY, scale=cw_sb[:, o, t : t + 1])
+                    k = len([c for c in WEIGHTED if (c, o) not in TURNED])
+                    nc.scalar.activation(weight[:, 0:k, t, o, :], rw_bank[:, 0:k, :], COPY, scale=cw_sb[:, o, t : t + 1])
 
         def gather(u, c0, c1):
             nc.vector.tensor_copy(
@@ -148,10 +171,9 @@ def tile_attend_gml_sq_kernel(tc, xT, wd_words, wd_scales, wv_words, wv_scales, 
                 in_=x_listed[:, cols, :].rearrange("p i u -> p (i u)").bitcast(BF16),
             )
 
-        def subtract_targets(c, o):
+        def product(c, o, b):
             cols = slice(c * CHUNK, (c + 1) * CHUNK)
-            h, within = divmod(c * CHUNK, HALF)
-            a_bank = psum2.tile([P, LANES, CHUNK], F32, name=f"a_bank{o}")
+            a_bank = bank(b, [P, LANES, CHUNK], f"a_bank{c}{o}")
             for t in range(LANES):
                 scale_cols = slice((o * LANES + t) * P, (o * LANES + t + 1) * P)
                 nc.tensor.matmul_mx(
@@ -163,62 +185,106 @@ def tile_attend_gml_sq_kernel(tc, xT, wd_words, wd_scales, wv_words, wv_scales, 
                     start=True,
                     stop=True,
                 )
-            nc.vector.tensor_tensor(residual[c][o][:], a_bank[:], y_sb[h][o][:, :, within : within + CHUNK], SUB)
+            return a_bank
 
-        def weigh(c, o):
+        def y_of(c, o):
             h, within = divmod(c * CHUNK, HALF)
+            return y_sb[h][o][:, :, within : within + CHUNK]
+
+        def subtract_targets(c, o, a_bank):
+            nc.vector.tensor_tensor(residual[c][:, :, o, :], a_bank[:], y_of(c, o), SUB)
+
+        def weigh(c, o0, o1, dst):
             nc.vector.tensor_tensor(
-                grad[o][:, c * CHUNK * LANES : (c + 1) * CHUNK * LANES].rearrange("p (r i t) -> p r t i", i=RUN, t=LANES),
-                residual[c][o][:].rearrange("p t (r i) -> p r t i", i=RUN),
-                weight[h][:, o, :, within : within + CHUNK].rearrange("p t (r i) -> p r t i", i=RUN),
+                dst.rearrange("p (r i t) -> p r t i", i=RUN, t=LANES),
+                residual[c][:, :, o0:o1, :].rearrange("p t o (r i) -> p (o r) t i", i=RUN),
+                weight[:, WEIGHTED.index(c), :, o0:o1, :].rearrange("p t o (r i) -> p (o r) t i", i=RUN),
                 MULT,
             )
 
-        def quantize_grad(c, o):
-            cols = slice(c * CHUNK, (c + 1) * CHUNK)
-            nc.vector.quantize_mx(
-                out=g_codes[o][:, cols].bitcast(E5M2),
-                scales=g_scale[o][:, cols],
-                in_=grad[o][:, cols.start * LANES : cols.stop * LANES],
+        def scale_targets(c, o):
+            for t in range(LANES):
+                nc.scalar.activation(y_scaled[c, o][:, t, :], y_of(c, o)[:, t, :], COPY, scale=cw_neg[:, o, t : t + 1])
+
+        def scale_product(c, o, a_bank):
+            for t in range(LANES):
+                nc.scalar.activation(a_scaled[c, o][:, t, :], a_bank[:, t, :], COPY, scale=cw_sb[:, o, t : t + 1])
+
+        def turn_and_weigh(c, o, b):
+            sum_bank = bank(b, [P, LANES, P], f"sum_bank{c}{o}")
+            for t in range(LANES):
+                nc.tensor.matmul(sum_bank[:, t, :], y_scaled[c, o][:, t, :], ident[:], start=True, stop=False, is_transpose=True)
+                nc.tensor.matmul(sum_bank[:, t, :], a_scaled[c, o][:, t, :], ident[:], start=False, stop=True, is_transpose=True)
+            nc.scalar.activation(
+                grad_turned[c, o][:].rearrange("i (u p e) -> i u p e", u=PAIRS, e=2),
+                sum_bank[:].rearrange("i (u e) p -> i u p e", u=PAIRS),
+                COPY,
+                scale=rw_col[:, c : c + 1],
             )
 
-        def back_first_chunk():
-            turned_bank = psum1.tile([P, D], F32, name="turned_bank")
+        def turn_back(c, o, b):
+            word_bank = bank(b, [P, PAIRS, CHUNK], f"word_bank{c}{o}")
+            words = grad_turned[c, o][:].bitcast(F32)
+            for u in range(PAIRS):
+                nc.tensor.transpose(word_bank[:, u, :], words[:, u * P : (u + 1) * P], ident[:])
+            nc.scalar.copy(
+                grad_late[c, o][:].bitcast(F32).rearrange("p (i u) -> p i u", u=PAIRS),
+                word_bank[:].rearrange("p u i -> p i u"),
+            )
+
+        def g_cols(c, o0, o1):
+            return slice(G_COLS[c, o0] * CHUNK, (G_COLS[c, o1 - 1] + 1) * CHUNK)
+
+        def quantize_grad(c, o0, o1, src):
+            cols = g_cols(c, o0, o1)
+            nc.vector.quantize_mx(out=g_codes[:, cols].bitcast(E5M2), scales=g_scale[:, cols], in_=src)
+
+        def back_early(c, b0):
+            turned_bank = bank(b0, [P, D], f"turned_bank{c}")
             for o in range(PASSES):
                 nc.tensor.matmul_mx(
                     out=turned_bank[:],
-                    lhsT=g_codes[o][:, 0:CHUNK].bitcast(E5M2),
-                    lhsT_scale=g_scale[o][:, 0:CHUNK],
+                    lhsT=g_codes[:, g_cols(c, o, o + 1)].bitcast(E5M2),
+                    lhsT_scale=g_scale[:, g_cols(c, o, o + 1)],
                     rhs=wv_codes[:, o, :].bitcast(E4M3),
                     rhs_scale=wv_scale[:, o, :],
                     start=(o == 0),
                     stop=(o == PASSES - 1),
                 )
-            nc.scalar.copy(first_turned[:], turned_bank[:])
-            first_bank = psum1.tile([P, D_TILES, CHUNK], F32, name="first_bank")
-            for j in range(D_TILES):
-                nc.tensor.transpose(first_bank[:, j, :], first_turned[:, j * P : (j + 1) * P], ident[:])
-            nc.scalar.copy(dx_first[:], first_bank[:])
+            return turned_bank
 
-        def back_rest(j):
-            dx_bank = psum2.tile([P, N], F32, name="dx_bank")
-            for o in range(PASSES):
+        def turn_early(c, j0, j1, turned_bank, b1):
+            nc.scalar.copy(dx_turned[c][:, j0 * P : j1 * P], turned_bank[:, j0 * P : j1 * P])
+            early_bank = bank(b1, [P, j1 - j0, CHUNK], f"early_bank{c}{j0}")
+            for j in range(j0, j1):
+                nc.tensor.transpose(early_bank[:, j - j0, :], dx_turned[c][:, j * P : (j + 1) * P], ident[:])
+            return early_bank
+
+        def fetch_early(c, j0, j1, early_bank, tag):
+            part = keep.tile([P, j1 - j0, CHUNK], F32, name=f"dx_early{c}{j0}", tag=tag)
+            nc.scalar.copy(part[:], early_bank[:])
+            for j in range(j0, j1):
+                dx_early[c, j] = part[:, j - j0, :]
+
+        def back_rest(j, b, passes):
+            dx_bank = bank(b, [P, N], f"dx_bank{j}")
+            for o in passes:
                 nc.tensor.matmul_mx(
                     out=dx_bank[:],
                     lhsT=wv_codes[:, o, j * P : (j + 1) * P].bitcast(E4M3),
                     lhsT_scale=wv_scale[:, o, j * P : (j + 1) * P],
-                    rhs=g_codes[o][:].bitcast(E5M2),
-                    rhs_scale=g_scale[o][:],
-                    start=(o == 0),
-                    stop=(o == PASSES - 1),
+                    rhs=g_codes[:, G_START[o] : G_START[o] + N].bitcast(E5M2),
+                    rhs_scale=g_scale[:, G_START[o] : G_START[o] + N],
+                    start=(o == passes[0]),
+                    stop=(o == passes[-1]),
                 )
             nc.scalar.copy(dx_rest[j][:], dx_bank[:, CHUNK:N])
 
-        def scatter_first(j):
-            nc.vector.tensor_copy(windows[j][:].indirect(offsets[:, 0:LIST_COLS]), dx_first[:, j, :])
+        def scatter_early(c, j):
+            nc.vector.tensor_copy(windows[j][:].indirect(offsets[:, c * LIST_COLS : (c + 1) * LIST_COLS]), dx_early[c, j])
 
         def scatter_rest_and_store(j):
-            nc.vector.tensor_copy(windows[j][:].indirect(offsets[:, LIST_COLS : CHUNKS * LIST_COLS]), dx_rest[j][:])
+            nc.vector.tensor_copy(windows[j][:].indirect(offsets[:, LATE[0] * LIST_COLS : (LATE[-1] + 1) * LIST_COLS]), dx_rest[j][:])
             nc.sync.dma_start(out[j * P : (j + 1) * P, :], windows[j][:])
 
         cast_x(0, 0)
@@ -226,46 +292,55 @@ def tile_attend_gml_sq_kernel(tc, xT, wd_words, wd_scales, wv_words, wv_scales, 
         gather(0, 0, CHUNKS)
         for k in range(len(X_PIECES[1])):
             cast_x(1, k)
-        make_weight(0)
+        nc.scalar.mul(cw_neg[:], cw_sb[:], -1.0)
+        make_weight(6, 7)
+        load_wv_scales()
 
-        gather(1, 1, 2)
-        quantize_x(1, 2)
         gather(1, 0, 1)
-        gather(1, 2, 4)
         quantize_x(0, 1)
+        a00 = product(0, 0, 0)
+        gather(1, 1, 2)
         reorder_wd(1)
-        subtract_targets(1, 0)
+        a01 = product(0, 1, 1)
+        quantize_x(1, 2)
+        a10 = product(1, 0, 2)
+        a11 = product(1, 1, 3)
+        gather(1, 2, 4)
+        scale_targets(1, 0)
+        scale_product(1, 0, a10)
+        subtract_targets(0, 0, a00)
         quantize_x(2, 4)
-        subtract_targets(1, 1)
-        make_weight(1)
-
-        weigh(1, 0)
-        weigh(1, 1)
-        subtract_targets(0, 0)
-        quantize_grad(1, 0)
-        subtract_targets(0, 1)
-        quantize_grad(1, 1)
-        weigh(0, 0)
-        weigh(0, 1)
-        quantize_grad(0, 0)
-        subtract_targets(2, 0)
-        quantize_grad(0, 1)
-        back_first_chunk()
-        subtract_targets(2, 1)
-        weigh(2, 0)
-        weigh(2, 1)
-        subtract_targets(3, 0)
-        quantize_grad(2, 0)
-        subtract_targets(3, 1)
-        quantize_grad(2, 1)
-        weigh(3, 0)
-        weigh(3, 1)
-        quantize_grad(3, 0)
-        quantize_grad(3, 1)
-
+        a30 = product(3, 0, 4)
+        a31 = product(3, 1, 5)
+        a20 = product(2, 0, 6)
+        a21 = product(2, 1, 7)
+        subtract_targets(0, 1, a01)
+        scale_targets(1, 1)
+        scale_product(1, 1, a11)
+        weigh(0, 0, 2, grad[0][:])
+        quantize_grad(0, 0, 2, grad[0][:])
+        turn_and_weigh(1, 0, 0)
+        turn_and_weigh(1, 1, 1)
+        subtract_targets(3, 0, a30)
+        subtract_targets(2, 0, a20)
+        t0 = back_early(0, 2)
+        e00 = turn_early(0, 0, 4, t0, 3)
+        subtract_targets(3, 1, a31)
+        subtract_targets(2, 1, a21)
+        weigh(3, 0, 2, grad[3][:])
+        weigh(2, 0, 2, grad[2][:])
+        turn_back(1, 0, 0)
+        turn_back(1, 1, 1)
+        fetch_early(0, 0, 4, e00, "dx_early0")
+        quantize_grad(3, 0, 1, grad[3][:, 0:K_PASS])
+        quantize_grad(3, 1, 2, grad[3][:, K_PASS:V])
+        quantize_grad(1, 0, 1, grad_late[1, 0][:])
+        quantize_grad(1, 1, 2, grad_late[1, 1][:])
+        quantize_grad(2, 0, 1, grad[2][:, 0:K_PASS])
+        quantize_grad(2, 1, 2, grad[2][:, K_PASS:V])
         for j in range(D_TILES):
-            back_rest(j)
+            back_rest(j, (4, 5, 6, 7)[j], (1, 0))
         for j in range(D_TILES):
-            scatter_first(j)
+            scatter_early(0, j)
         for j in range(D_TILES):
             scatter_rest_and_store(j)

@@ -59,13 +59,13 @@ def tile_attend_gml_sq_kernel(tc, xT, wd_words, wd_scales, wv_words, wv_scales, 
         cw_neg = keep.tile([P, PASSES, LANES], F32, name="cw_neg")
         rw_rows = keep.tile([P, CHUNK], F32, name="rw_rows")
         rw_col = keep.tile([P, CHUNKS], F32, name="rw_col")
-        x_raw = [[keep.tile([P, 2, b - a], F32, name=f"x_raw{u}_{a}") for a, b in X_PIECES[u]] for u in range(PAIRS)]
+        x_raw = [[keep.tile([P, 2, b - a], F32, name=f"x_raw{u}_{a}", tag=f"x_raw{u}_{a}") for a, b in X_PIECES[u]] for u in range(PAIRS)]
         x_pairs = [keep.tile([P, T], U32, name=f"x_pairs{u}") for u in range(PAIRS)]
         x_listed = keep.tile([P, N, PAIRS], U32, name="x_listed", align_bytes=64)
         x_codes = keep.tile([P, N], U32, name="x_codes", align_bytes=64)
         x_scale = keep.tile([P, N], U8, name="x_scale", align_bytes=64)
         y_sb = [[keep.tile([P, LANES, HALF], F32, name=f"y_sb{h}{o}") for o in range(PASSES)] for h in range(2)]
-        weight = keep.tile([P, len(WEIGHTED), LANES, PASSES, CHUNK], F32, name="weight")
+        weight = keep.tile([P, len(WEIGHTED), LANES, PASSES, CHUNK], F32, name="weight", tag="x_raw1_0")
         residual = [keep.tile([P, LANES, PASSES, CHUNK], F32, name=f"residual{c}", tag=f"residual{c}") for c in range(CHUNKS)]
         a_scaled = {(c, o): keep.tile([P, LANES, CHUNK], F32, name=f"a_scaled{c}{o}") for c, o in TURNED}
         y_scaled = {(c, o): keep.tile([P, LANES, CHUNK], F32, name=f"y_scaled{c}{o}") for c, o in TURNED}
@@ -95,23 +95,41 @@ def tile_attend_gml_sq_kernel(tc, xT, wd_words, wd_scales, wv_words, wv_scales, 
             words = wd_words[0].rearrange("p v t -> p (v t)").bitcast(I32)
             nc.sync.dma_start(wd_raw[o][:], words[:, o * K_PASS : (o + 1) * K_PASS])
 
-        nc.sync.dma_start(offsets[:], offs)
+        def load_y(h, o):
+            nc.sync.dma_start(y_sb[h][o][:], y_rows[o][:, :, h * HALF : (h + 1) * HALF])
+
+        def load_wd_scales(queue, q):
+            queue.dma_start(wd_raw_scale[32 * q : 32 * q + 4, :].bitcast(I32), wd_scales[0, 4 * q : 4 * q + 4, :].bitcast(I32))
+
+        def load_wv_scales(queue, q):
+            queue.dma_start(
+                wv_scale[32 * q : 32 * q + 4, :, :].bitcast(I32),
+                wv_scales[:, 4 * q : 4 * q + 4, :].rearrange("o f d -> f o d").bitcast(I32),
+            )
+
+        load_wd_scales(nc.scalar, 0)
+        load_wd_scales(nc.scalar, 1)
+        nc.scalar.dma_start(cw_sb[:], cw.rearrange("(o p t) one -> p o (t one)", o=PASSES, t=LANES))
+        load_wd_scales(nc.sync, 2)
+        load_wd_scales(nc.sync, 3)
         load_wd(0)
-        for q in range(QUADRANTS):
-            nc.scalar.dma_start(wd_raw_scale[32 * q : 32 * q + 4, :].bitcast(I32), wd_scales[0, 4 * q : 4 * q + 4, :].bitcast(I32))
-        nc.scalar.dma_start(rw_rows[0:CHUNKS, :], rw[0:1, :].rearrange("one (c i) -> (one c) i", c=CHUNKS))
         load_x(0, 0)
         load_x(0, 1)
+        nc.sync.dma_start(offsets[:], offs)
+        nc.sync.dma_start(rw_rows[0:CHUNKS, :], rw[0:1, :].rearrange("one (c i) -> (one c) i", c=CHUNKS))
         load_x(1, 0)
         load_x(1, 1)
         load_x(1, 2)
-        nc.sync.dma_start(cw_sb[:], cw.rearrange("(o p t) one -> p o (t one)", o=PASSES, t=LANES))
         load_wd(1)
-        nc.sync.dma_start(y_sb[0][0][:], y_rows[0][:, :, 0:HALF])
-        nc.sync.dma_start(y_sb[0][1][:], y_rows[1][:, :, 0:HALF])
-        nc.sync.dma_start(y_sb[1][0][:], y_rows[0][:, :, HALF:N])
+        load_y(0, 0)
+        load_y(0, 1)
+        load_wv_scales(nc.sync, 0)
+        load_wv_scales(nc.sync, 1)
+        load_wv_scales(nc.sync, 2)
+        load_wv_scales(nc.sync, 3)
+        load_y(1, 0)
         nc.sync.dma_start(wv_codes[:], wv_words.rearrange("o p d t -> p o (d t)").bitcast(I32))
-        nc.sync.dma_start(y_sb[1][1][:], y_rows[1][:, :, HALF:N])
+        load_y(1, 1)
 
         make_identity(nc, ident[:])
         for j in range(D_TILES):
@@ -128,13 +146,6 @@ def tile_attend_gml_sq_kernel(tc, xT, wd_words, wd_scales, wv_words, wv_scales, 
             wd_scale[:].rearrange("p (o t m) -> p o m t", o=PASSES, t=LANES),
             wd_raw_scale[:].rearrange("p (o m t) -> p o m t", o=PASSES, t=LANES),
         )
-
-        def load_wv_scales():
-            for q in range(QUADRANTS):
-                nc.scalar.dma_start(
-                    wv_scale[32 * q : 32 * q + 4, :, :].bitcast(I32),
-                    wv_scales[:, 4 * q : 4 * q + 4, :].rearrange("o f d -> f o d").bitcast(I32),
-                )
 
         def cast_x(u, k):
             a, b = X_PIECES[u][k]
@@ -294,7 +305,6 @@ def tile_attend_gml_sq_kernel(tc, xT, wd_words, wd_scales, wv_words, wv_scales, 
             cast_x(1, k)
         nc.scalar.mul(cw_neg[:], cw_sb[:], -1.0)
         make_weight(6, 7)
-        load_wv_scales()
 
         gather(1, 0, 1)
         quantize_x(0, 1)

@@ -30,7 +30,7 @@ CHUNKS = N // CHUNK
 HALF = N // 2
 LIST_COLS = CHUNK // 16
 RUN = 4
-X_PIECES = (((0, 512), (512, 1024)), ((0, 512), (512, 768), (768, 1024)))
+X_PIECES = (((0, 1024),), ((0, 512), (512, 768), (768, 1024)))
 EARLY = (0,)
 LATE = (1, 2, 3)
 TURNED = ((1, 0), (1, 1))
@@ -64,14 +64,13 @@ def tile_attend_gml_sq_kernel(tc, xT, wd_words, wd_scales, wv_words, wv_scales, 
         x_listed = keep.tile([P, N, PAIRS], U32, name="x_listed", align_bytes=64)
         x_codes = keep.tile([P, N], U32, name="x_codes", align_bytes=64)
         x_scale = keep.tile([P, N], U8, name="x_scale", align_bytes=64)
-        y_sb = [[keep.tile([P, LANES, HALF], F32, name=f"y_sb{h}{o}") for o in range(PASSES)] for h in range(2)]
+        y_sb = [[keep.tile([P, LANES, HALF], F32, name=f"y_sb{h}{o}", tag=f"y_sb{h}{o}", align_bytes=64) for o in range(PASSES)] for h in range(2)]
         weight = keep.tile([P, len(WEIGHTED), LANES, PASSES, CHUNK], F32, name="weight", tag="x_raw1_0")
-        residual = [keep.tile([P, LANES, PASSES, CHUNK], F32, name=f"residual{c}", tag=f"residual{c}") for c in range(CHUNKS)]
+        residual = [keep.tile([P, LANES, PASSES, CHUNK], F32, name=f"residual{c}") for c in range(CHUNKS)]
         a_scaled = {(c, o): keep.tile([P, LANES, CHUNK], F32, name=f"a_scaled{c}{o}") for c, o in TURNED}
         y_scaled = {(c, o): keep.tile([P, LANES, CHUNK], F32, name=f"y_scaled{c}{o}") for c, o in TURNED}
         grad_turned = {(c, o): keep.tile([P, K_PASS], BF16, name=f"grad_turned{c}{o}", tag=f"grad_turned{c}{o}") for c, o in TURNED}
         grad = {c: keep.tile([P, PASSES * CHUNK * LANES], BF16, name=f"grad{c}", align_bytes=64) for c in WEIGHTED}
-        grad_late = {(c, o): keep.tile([P, CHUNK * LANES], BF16, name=f"grad{c}{o}", align_bytes=64) for c, o in TURNED}
         g_codes = keep.tile([P, PASSES * N], U32, name="g_codes", align_bytes=64)
         g_scale = keep.tile([P, PASSES * N], U8, name="g_scale", align_bytes=64)
         dx_turned = {c: keep.tile([P, D], F32, name=f"dx_turned{c}") for c in EARLY}
@@ -113,20 +112,19 @@ def tile_attend_gml_sq_kernel(tc, xT, wd_words, wd_scales, wv_words, wv_scales, 
         load_wd_scales(nc.sync, 2)
         load_wd_scales(nc.sync, 3)
         load_wd(0)
-        load_x(0, 0)
-        load_x(0, 1)
         nc.sync.dma_start(offsets[:], offs)
+        load_x(0, 0)
         nc.sync.dma_start(rw_rows[0:CHUNKS, :], rw[0:1, :].rearrange("one (c i) -> (one c) i", c=CHUNKS))
+        load_wv_scales(nc.sync, 0)
+        load_wv_scales(nc.sync, 1)
+        load_wv_scales(nc.sync, 2)
+        load_wv_scales(nc.sync, 3)
         load_x(1, 0)
         load_x(1, 1)
         load_x(1, 2)
         load_wd(1)
         load_y(0, 0)
         load_y(0, 1)
-        load_wv_scales(nc.sync, 0)
-        load_wv_scales(nc.sync, 1)
-        load_wv_scales(nc.sync, 2)
-        load_wv_scales(nc.sync, 3)
         load_y(1, 0)
         nc.sync.dma_start(wv_codes[:], wv_words.rearrange("o p d t -> p o (d t)").bitcast(I32))
         load_y(1, 1)
@@ -147,11 +145,11 @@ def tile_attend_gml_sq_kernel(tc, xT, wd_words, wd_scales, wv_words, wv_scales, 
             wd_raw_scale[:].rearrange("p (o m t) -> p o m t", o=PASSES, t=LANES),
         )
 
-        def cast_x(u, k):
-            a, b = X_PIECES[u][k]
+        def cast_x(u, k, a, b, on_scalar):
+            first = X_PIECES[u][k][0]
             dst = x_pairs[u][:, a:b].bitcast(BF16).rearrange("p (c e) -> p c e", e=2)
-            src = x_raw[u][k][:].rearrange("p e c -> p c e")
-            if k == 0:
+            src = x_raw[u][k][:, :, a - first : b - first].rearrange("p e c -> p c e")
+            if on_scalar:
                 nc.scalar.activation(dst, src, COPY)
             else:
                 nc.vector.tensor_copy(dst, src)
@@ -224,8 +222,9 @@ def tile_attend_gml_sq_kernel(tc, xT, wd_words, wd_scales, wv_words, wv_scales, 
         def turn_and_weigh(c, o, b):
             sum_bank = bank(b, [P, LANES, P], f"sum_bank{c}{o}")
             for t in range(LANES):
-                nc.tensor.matmul(sum_bank[:, t, :], y_scaled[c, o][:, t, :], ident[:], start=True, stop=False, is_transpose=True)
-                nc.tensor.matmul(sum_bank[:, t, :], a_scaled[c, o][:, t, :], ident[:], start=False, stop=True, is_transpose=True)
+                nc.tensor.matmul(sum_bank[:, t, :], y_scaled[c, o][:, t, :], ident[:], start=(t == 0), stop=False, is_transpose=True)
+            for t in range(LANES):
+                nc.tensor.matmul(sum_bank[:, t, :], a_scaled[c, o][:, t, :], ident[:], start=False, stop=(t == LANES - 1), is_transpose=True)
             nc.scalar.activation(
                 grad_turned[c, o][:].rearrange("i (u p e) -> i u p e", u=PAIRS, e=2),
                 sum_bank[:].rearrange("i (u e) p -> i u p e", u=PAIRS),
@@ -233,13 +232,13 @@ def tile_attend_gml_sq_kernel(tc, xT, wd_words, wd_scales, wv_words, wv_scales, 
                 scale=rw_col[:, c : c + 1],
             )
 
-        def turn_back(c, o, b):
+        def turn_back(c, o, b, dst):
             word_bank = bank(b, [P, PAIRS, CHUNK], f"word_bank{c}{o}")
             words = grad_turned[c, o][:].bitcast(F32)
             for u in range(PAIRS):
                 nc.tensor.transpose(word_bank[:, u, :], words[:, u * P : (u + 1) * P], ident[:])
             nc.scalar.copy(
-                grad_late[c, o][:].bitcast(F32).rearrange("p (i u) -> p i u", u=PAIRS),
+                dst.bitcast(F32).rearrange("p (i u) -> p i u", u=PAIRS),
                 word_bank[:].rearrange("p u i -> p i u"),
             )
 
@@ -298,11 +297,12 @@ def tile_attend_gml_sq_kernel(tc, xT, wd_words, wd_scales, wv_words, wv_scales, 
             nc.vector.tensor_copy(windows[j][:].indirect(offsets[:, LATE[0] * LIST_COLS : (LATE[-1] + 1) * LIST_COLS]), dx_rest[j][:])
             nc.sync.dma_start(out[j * P : (j + 1) * P, :], windows[j][:])
 
-        cast_x(0, 0)
-        cast_x(0, 1)
+        cast_x(0, 0, 0, 320, True)
+        cast_x(0, 0, 320, 1024, False)
         gather(0, 0, CHUNKS)
-        for k in range(len(X_PIECES[1])):
-            cast_x(1, k)
+        cast_x(1, 0, 0, 512, True)
+        cast_x(1, 1, 512, 768, False)
+        cast_x(1, 2, 768, 1024, False)
         nc.scalar.mul(cw_neg[:], cw_sb[:], -1.0)
         make_weight(6, 7)
 
@@ -329,27 +329,28 @@ def tile_attend_gml_sq_kernel(tc, xT, wd_words, wd_scales, wv_words, wv_scales, 
         scale_product(1, 1, a11)
         weigh(0, 0, 2, grad[0][:])
         quantize_grad(0, 0, 2, grad[0][:])
+        t0 = back_early(0, 2)
+        e00 = turn_early(0, 0, 4, t0, 3)
         turn_and_weigh(1, 0, 0)
         turn_and_weigh(1, 1, 1)
         subtract_targets(3, 0, a30)
         subtract_targets(2, 0, a20)
-        t0 = back_early(0, 2)
-        e00 = turn_early(0, 0, 4, t0, 3)
         subtract_targets(3, 1, a31)
         subtract_targets(2, 1, a21)
         weigh(3, 0, 2, grad[3][:])
         weigh(2, 0, 2, grad[2][:])
-        turn_back(1, 0, 0)
-        turn_back(1, 1, 1)
-        fetch_early(0, 0, 4, e00, "dx_early0")
+        grad1 = keep.tile([P, V], BF16, name="grad1", tag="y_sb11", align_bytes=64)
+        turn_back(1, 0, 4, grad1[:, 0:K_PASS])
+        turn_back(1, 1, 6, grad1[:, K_PASS:V])
+        fetch_early(0, 0, 4, e00, "grad_turned11")
         quantize_grad(3, 0, 1, grad[3][:, 0:K_PASS])
         quantize_grad(3, 1, 2, grad[3][:, K_PASS:V])
-        quantize_grad(1, 0, 1, grad_late[1, 0][:])
-        quantize_grad(1, 1, 2, grad_late[1, 1][:])
+        quantize_grad(1, 0, 1, grad1[:, 0:K_PASS])
+        quantize_grad(1, 1, 2, grad1[:, K_PASS:V])
         quantize_grad(2, 0, 1, grad[2][:, 0:K_PASS])
         quantize_grad(2, 1, 2, grad[2][:, K_PASS:V])
         for j in range(D_TILES):
-            back_rest(j, (4, 5, 6, 7)[j], (1, 0))
+            back_rest(j, (5, 7, 0, 2)[j], (1, 0))
         for j in range(D_TILES):
             scatter_early(0, j)
         for j in range(D_TILES):

@@ -29,7 +29,7 @@ CHUNK = 128
 CHUNKS = N // CHUNK
 HALF = N // 2
 LIST_COLS = CHUNK // 16
-RUN = 4
+RUN = 2
 X_PIECES = (((0, 1024),), ((0, 512), (512, 768), (768, 1024)))
 EARLY = (0,)
 LATE = (1, 2, 3)

@@ -34,8 +34,9 @@ X_PIECES = (((0, 1024),), ((0, 512), (512, 768), (768, 1024)))
 EARLY = (0,)
 LATE = (1, 2, 3)
 TURNED = ((1, 0), (1, 1))
-WEIGHTED = (0, 3, 2)
+WEIGHTED = (0, 2, 3)
 G_COLS = {(0, 0): 0, (0, 1): 1, (1, 0): 2, (2, 0): 3, (3, 0): 4, (1, 1): 5, (2, 1): 6, (3, 1): 7}
+SIDE = 96
 G_START = (CHUNK, N)
 
 
@@ -65,12 +66,12 @@ def tile_attend_gml_sq_kernel(tc, xT, wd_words, wd_scales, wv_words, wv_scales, 
         x_codes = keep.tile([P, N], U32, name="x_codes", align_bytes=64)
         x_scale = keep.tile([P, N], U8, name="x_scale", align_bytes=64)
         y_sb = [[keep.tile([P, LANES, HALF], F32, name=f"y_sb{h}{o}", tag=f"y_sb{h}{o}", align_bytes=64) for o in range(PASSES)] for h in range(2)]
-        weight = keep.tile([P, len(WEIGHTED), LANES, PASSES, CHUNK], F32, name="weight", tag="x_raw1_0")
-        residual = [keep.tile([P, LANES, PASSES, CHUNK], F32, name=f"residual{c}") for c in range(CHUNKS)]
+        weight = keep.tile([P, LANES, PASSES, len(WEIGHTED) * CHUNK], F32, name="weight", tag="x_raw1_0")
+        residual = [keep.tile([P, LANES, len(WEIGHTED) * CHUNK], F32, name=f"residual{o}") for o in range(PASSES)]
         a_scaled = {(c, o): keep.tile([P, LANES, CHUNK], F32, name=f"a_scaled{c}{o}") for c, o in TURNED}
         y_scaled = {(c, o): keep.tile([P, LANES, CHUNK], F32, name=f"y_scaled{c}{o}") for c, o in TURNED}
         grad_turned = {(c, o): keep.tile([P, K_PASS], BF16, name=f"grad_turned{c}{o}", tag=f"grad_turned{c}{o}") for c, o in TURNED}
-        grad = {c: keep.tile([P, PASSES * CHUNK * LANES], BF16, name=f"grad{c}", align_bytes=64) for c in WEIGHTED}
+        grad_early = keep.tile([P, PASSES * K_PASS], BF16, name="grad_early", tag="grad_early", align_bytes=64)
         g_codes = keep.tile([P, PASSES * N], U32, name="g_codes", align_bytes=64)
         g_scale = keep.tile([P, PASSES * N], U8, name="g_scale", align_bytes=64)
         dx_turned = {c: keep.tile([P, D], F32, name=f"dx_turned{c}") for c in EARLY}
@@ -126,8 +127,8 @@ def tile_attend_gml_sq_kernel(tc, xT, wd_words, wd_scales, wv_words, wv_scales, 
         load_y(0, 0)
         load_y(0, 1)
         load_y(1, 0)
-        nc.sync.dma_start(wv_codes[:], wv_words.rearrange("o p d t -> p o (d t)").bitcast(I32))
         load_y(1, 1)
+        nc.sync.dma_start(wv_codes[:], wv_words.rearrange("o p d t -> p o (d t)").bitcast(I32))
 
         make_identity(nc, ident[:])
         for j in range(D_TILES):
@@ -163,8 +164,7 @@ def tile_attend_gml_sq_kernel(tc, xT, wd_words, wd_scales, wv_words, wv_scales, 
                 nc.tensor.transpose(rw_bank[:, k, :], rw_col[:, c : c + 1].to_broadcast([P, P]), ident[:])
             for o in range(PASSES):
                 for t in range(LANES):
-                    k = len([c for c in WEIGHTED if (c, o) not in TURNED])
-                    nc.scalar.activation(weight[:, 0:k, t, o, :], rw_bank[:, 0:k, :], COPY, scale=cw_sb[:, o, t : t + 1])
+                    nc.scalar.activation(weight[:, t, o, :], rw_bank[:].rearrange("p k i -> p (k i)"), COPY, scale=cw_sb[:, o, t : t + 1])
 
         def gather(u, c0, c1):
             nc.vector.tensor_copy(
@@ -201,13 +201,15 @@ def tile_attend_gml_sq_kernel(tc, xT, wd_words, wd_scales, wv_words, wv_scales, 
             return y_sb[h][o][:, :, within : within + CHUNK]
 
         def subtract_targets(c, o, a_bank):
-            nc.vector.tensor_tensor(residual[c][:, :, o, :], a_bank[:], y_of(c, o), SUB)
+            k = WEIGHTED.index(c)
+            nc.vector.tensor_tensor(residual[o][:, :, k * CHUNK : (k + 1) * CHUNK], a_bank[:], y_of(c, o), SUB)
 
-        def weigh(c, o0, o1, dst):
-            nc.vector.tensor_tensor(
+        def weigh(first, last, o, dst, engine):
+            cols = slice(first, last)
+            engine.tensor_tensor(
                 dst.rearrange("p (r i t) -> p r t i", i=RUN, t=LANES),
-                residual[c][:, :, o0:o1, :].rearrange("p t o (r i) -> p (o r) t i", i=RUN),
-                weight[:, WEIGHTED.index(c), :, o0:o1, :].rearrange("p t o (r i) -> p (o r) t i", i=RUN),
+                residual[o][:, :, cols].rearrange("p t (r i) -> p r t i", i=RUN),
+                weight[:, :, o, cols].rearrange("p t (r i) -> p r t i", i=RUN),
                 MULT,
             )
 
@@ -245,8 +247,7 @@ def tile_attend_gml_sq_kernel(tc, xT, wd_words, wd_scales, wv_words, wv_scales, 
         def g_cols(c, o0, o1):
             return slice(G_COLS[c, o0] * CHUNK, (G_COLS[c, o1 - 1] + 1) * CHUNK)
 
-        def quantize_grad(c, o0, o1, src):
-            cols = g_cols(c, o0, o1)
+        def quantize_grad(cols, src):
             nc.vector.quantize_mx(out=g_codes[:, cols].bitcast(E5M2), scales=g_scale[:, cols], in_=src)
 
         def back_early(c, b0):
@@ -270,11 +271,10 @@ def tile_attend_gml_sq_kernel(tc, xT, wd_words, wd_scales, wv_words, wv_scales, 
                 nc.tensor.transpose(early_bank[:, j - j0, :], dx_turned[c][:, j * P : (j + 1) * P], ident[:])
             return early_bank
 
-        def fetch_early(c, j0, j1, early_bank, tag):
-            part = keep.tile([P, j1 - j0, CHUNK], F32, name=f"dx_early{c}{j0}", tag=tag)
-            nc.scalar.copy(part[:], early_bank[:])
+        def fetch_early(c, j0, j1, early_bank, part):
+            nc.scalar.copy(part, early_bank[:].rearrange("p j i -> p (j i)"))
             for j in range(j0, j1):
-                dx_early[c, j] = part[:, j - j0, :]
+                dx_early[c, j] = part[:, (j - j0) * CHUNK : (j - j0 + 1) * CHUNK]
 
         def back_rest(j, b, passes):
             dx_bank = bank(b, [P, N], f"dx_bank{j}")
@@ -327,30 +327,34 @@ def tile_attend_gml_sq_kernel(tc, xT, wd_words, wd_scales, wv_words, wv_scales, 
         subtract_targets(0, 1, a01)
         scale_targets(1, 1)
         scale_product(1, 1, a11)
-        weigh(0, 0, 2, grad[0][:])
-        quantize_grad(0, 0, 2, grad[0][:])
+        weigh(0, CHUNK, 0, grad_early[:, 0:K_PASS], nc.vector)
+        weigh(0, CHUNK, 1, grad_early[:, K_PASS:V], nc.vector)
+        quantize_grad(g_cols(0, 0, 2), grad_early[:])
+        grad_late = [keep.tile([P, 2 * K_PASS], BF16, name=f"grad_late{o}", tag=("grad_early", "grad_late1")[o], align_bytes=64) for o in range(PASSES)]
         t0 = back_early(0, 2)
-        e00 = turn_early(0, 0, 4, t0, 3)
+        e00 = turn_early(0, 0, 2, t0, 3)
         turn_and_weigh(1, 0, 0)
         turn_and_weigh(1, 1, 1)
+        e02 = turn_early(0, 2, 4, t0, 0)
         subtract_targets(3, 0, a30)
+        weigh(3 * CHUNK - SIDE, 3 * CHUNK, 0, grad_late[0][:, V - LANES * SIDE : V], nc.gpsimd)
         subtract_targets(2, 0, a20)
         subtract_targets(3, 1, a31)
         subtract_targets(2, 1, a21)
-        weigh(3, 0, 2, grad[3][:])
-        weigh(2, 0, 2, grad[2][:])
-        grad1 = keep.tile([P, V], BF16, name="grad1", tag="y_sb11", align_bytes=64)
+        weigh(CHUNK, 3 * CHUNK - SIDE, 0, grad_late[0][:, 0 : V - LANES * SIDE], nc.vector)
+        weigh(CHUNK, 3 * CHUNK, 1, grad_late[1][:], nc.vector)
+        held = keep.tile([P, V], F32, name="held", tag="y_sb11", align_bytes=64)
+        grad1 = held[:, 0:K_PASS].bitcast(BF16)
         turn_back(1, 0, 4, grad1[:, 0:K_PASS])
         turn_back(1, 1, 6, grad1[:, K_PASS:V])
-        fetch_early(0, 0, 4, e00, "grad_turned11")
-        quantize_grad(3, 0, 1, grad[3][:, 0:K_PASS])
-        quantize_grad(3, 1, 2, grad[3][:, K_PASS:V])
-        quantize_grad(1, 0, 1, grad1[:, 0:K_PASS])
-        quantize_grad(1, 1, 2, grad1[:, K_PASS:V])
-        quantize_grad(2, 0, 1, grad[2][:, 0:K_PASS])
-        quantize_grad(2, 1, 2, grad[2][:, K_PASS:V])
+        fetch_early(0, 0, 2, e00, held[:, K_PASS : K_PASS + 2 * CHUNK])
+        fetch_early(0, 2, 4, e02, held[:, K_PASS + 2 * CHUNK : V])
+        quantize_grad(slice(G_COLS[2, 0] * CHUNK, (G_COLS[3, 0] + 1) * CHUNK), grad_late[0][:])
+        quantize_grad(g_cols(1, 0, 1), grad1[:, 0:K_PASS])
+        quantize_grad(g_cols(1, 1, 2), grad1[:, K_PASS:V])
+        quantize_grad(slice(G_COLS[2, 1] * CHUNK, (G_COLS[3, 1] + 1) * CHUNK), grad_late[1][:])
         for j in range(D_TILES):
-            back_rest(j, (5, 7, 0, 2)[j], (1, 0))
+            back_rest(j, (5, 7, 1, 2)[j], (1, 0))
         for j in range(D_TILES):
             scatter_early(0, j)
         for j in range(D_TILES):

@@ -36,7 +36,8 @@ LATE = (1, 2, 3)
 TURNED = ((1, 0), (1, 1))
 WEIGHTED = (0, 2, 3)
 G_COLS = {(0, 0): 0, (0, 1): 1, (1, 0): 2, (2, 0): 3, (3, 0): 4, (1, 1): 5, (2, 1): 6, (3, 1): 7}
-SIDE = 96
+SIDE_RUN = 4
+SIDE = 128
 G_START = (CHUNK, N)
 
 
@@ -204,12 +205,12 @@ def tile_attend_gml_sq_kernel(tc, xT, wd_words, wd_scales, wv_words, wv_scales, 
             k = WEIGHTED.index(c)
             nc.vector.tensor_tensor(residual[o][:, :, k * CHUNK : (k + 1) * CHUNK], a_bank[:], y_of(c, o), SUB)
 
-        def weigh(first, last, o, dst, engine):
+        def weigh(first, last, o, dst, engine, run=RUN):
             cols = slice(first, last)
             engine.tensor_tensor(
-                dst.rearrange("p (r i t) -> p r t i", i=RUN, t=LANES),
-                residual[o][:, :, cols].rearrange("p t (r i) -> p r t i", i=RUN),
-                weight[:, :, o, cols].rearrange("p t (r i) -> p r t i", i=RUN),
+                dst.rearrange("p (r i t) -> p r t i", i=run, t=LANES),
+                residual[o][:, :, cols].rearrange("p t (r i) -> p r t i", i=run),
+                weight[:, :, o, cols].rearrange("p t (r i) -> p r t i", i=run),
                 MULT,
             )
 
@@ -337,7 +338,7 @@ def tile_attend_gml_sq_kernel(tc, xT, wd_words, wd_scales, wv_words, wv_scales, 
         turn_and_weigh(1, 1, 1)
         e02 = turn_early(0, 2, 4, t0, 0)
         subtract_targets(3, 0, a30)
-        weigh(3 * CHUNK - SIDE, 3 * CHUNK, 0, grad_late[0][:, V - LANES * SIDE : V], nc.gpsimd)
+        weigh(3 * CHUNK - SIDE, 3 * CHUNK, 0, grad_late[0][:, V - LANES * SIDE : V], nc.gpsimd, SIDE_RUN)
         subtract_targets(2, 0, a20)
         subtract_targets(3, 1, a31)
         subtract_targets(2, 1, a21)

@@ -30,21 +30,22 @@ CHUNKS = N // CHUNK
 HALF = N // 2
 LIST_COLS = CHUNK // 16
 RUN = 2
-X_PIECES = (((0, 1024),), ((0, 512), (512, 768), (768, 1024)))
-EARLY = (0,)
-LATE = (1, 2, 3)
+X_PIECES = (((0, 1024),), ((0, 512), (512, 1024)))
+EARLY = (0, 3)
+LATE = (1, 2)
 TURNED = ((1, 0), (1, 1))
 WEIGHTED = (0, 2, 3)
-G_COLS = {(0, 0): 0, (0, 1): 1, (1, 0): 2, (2, 0): 3, (3, 0): 4, (1, 1): 5, (2, 1): 6, (3, 1): 7}
+G_COLS = {(0, 0): 0, (0, 1): 1, (3, 0): 2, (3, 1): 3, (1, 0): 4, (2, 0): 5, (1, 1): 6, (2, 1): 7}
 SIDE_RUN = 4
 SIDE = 128
-G_START = (CHUNK, N)
+G_START = (2 * CHUNK, N)
 
 
 def tile_attend_gml_sq_kernel(tc, xT, wd_words, wd_scales, wv_words, wv_scales, y, cw, rw, offs, out):
     nc = tc.nc
     with ExitStack() as ctx:
         keep = ctx.enter_context(tc.tile_pool(name="keep", bufs=1))
+        relay = ctx.enter_context(tc.tile_pool(name="relay", bufs=1))
         psum = ctx.enter_context(tc.psum_pool(name="psum", bufs=1))
 
         def bank(b, shape, name):
@@ -54,35 +55,38 @@ def tile_attend_gml_sq_kernel(tc, xT, wd_words, wd_scales, wv_words, wv_scales, 
         wd_raw = [keep.tile([P, K_PASS], I32, name=f"wd_raw{o}") for o in range(PASSES)]
         wd_raw_scale = keep.tile([P, V], U8, name="wd_raw_scale", align_bytes=64)
         wd_codes = [keep.tile([P, K_PASS], I32, name=f"wd_codes{o}", align_bytes=64) for o in range(PASSES)]
-        wd_scale = keep.tile([P, V], U8, name="wd_scale", align_bytes=64)
         wv_codes = keep.tile([P, PASSES, D], I32, name="wv_codes", align_bytes=64)
         wv_scale = keep.tile([P, PASSES, D], U8, name="wv_scale", align_bytes=64)
         cw_sb = keep.tile([P, PASSES, LANES], F32, name="cw_sb")
         cw_neg = keep.tile([P, PASSES, LANES], F32, name="cw_neg")
-        rw_rows = keep.tile([P, CHUNK], F32, name="rw_rows")
-        rw_col = keep.tile([P, CHUNKS], F32, name="rw_col")
-        x_raw = [[keep.tile([P, 2, b - a], F32, name=f"x_raw{u}_{a}", tag=f"x_raw{u}_{a}") for a, b in X_PIECES[u]] for u in range(PAIRS)]
+        rw_sb = keep.tile([P, CHUNKS, CHUNK], F32, name="rw_sb")
+        x_raw = [[keep.tile([P, 2, b - a], F32, name=f"x_raw{u}_{a}", tag=f"x_raw{u}_{a}", align_bytes=64) for a, b in X_PIECES[u]] for u in range(PAIRS)]
+        rw_col = keep.tile([P, 1], F32, name="rw_col")
+        wd_scale = [keep.tile([P, K_PASS], U8, name=f"wd_scale{o}", tag=("x_raw0_0", "x_raw1_512")[o], align_bytes=64) for o in range(PASSES)]
         x_pairs = [keep.tile([P, T], U32, name=f"x_pairs{u}") for u in range(PAIRS)]
-        x_listed = keep.tile([P, N, PAIRS], U32, name="x_listed", align_bytes=64)
+        x_first = keep.tile([P, PAIRS, HALF], U32, name="x_first")
+        x_shared = keep.tile([P, 3 * HALF], U32, name="x_shared", align_bytes=64)
+        x_second = x_shared[:, 0 : 2 * HALF].rearrange("p (u i) -> p u i", u=PAIRS)
+        listed_first = x_shared[:, HALF : 3 * HALF].rearrange("p (i u) -> p i u", u=PAIRS)
+        listed_second = keep.tile([P, HALF, PAIRS], U32, name="listed_second", align_bytes=64)
         x_codes = keep.tile([P, N], U32, name="x_codes", align_bytes=64)
         x_scale = keep.tile([P, N], U8, name="x_scale", align_bytes=64)
         y_sb = [[keep.tile([P, LANES, HALF], F32, name=f"y_sb{h}{o}", tag=f"y_sb{h}{o}", align_bytes=64) for o in range(PASSES)] for h in range(2)]
-        weight = keep.tile([P, LANES, PASSES, len(WEIGHTED) * CHUNK], F32, name="weight", tag="x_raw1_0")
-        residual = [keep.tile([P, LANES, len(WEIGHTED) * CHUNK], F32, name=f"residual{o}") for o in range(PASSES)]
+        weight = keep.tile([P, LANES, len(WEIGHTED), PASSES, CHUNK], F32, name="weight")
+        res_first = keep.tile([P, LANES, PASSES, CHUNK], F32, name="res_first", tag="grad_side", align_bytes=64)
+        res = {(0, o): res_first[:, :, o, :] for o in range(PASSES)}
         a_scaled = {(c, o): keep.tile([P, LANES, CHUNK], F32, name=f"a_scaled{c}{o}") for c, o in TURNED}
         y_scaled = {(c, o): keep.tile([P, LANES, CHUNK], F32, name=f"y_scaled{c}{o}") for c, o in TURNED}
-        grad_turned = {(c, o): keep.tile([P, K_PASS], BF16, name=f"grad_turned{c}{o}", tag=f"grad_turned{c}{o}") for c, o in TURNED}
-        grad_early = keep.tile([P, PASSES * K_PASS], BF16, name="grad_early", tag="grad_early", align_bytes=64)
+        grad_early = relay.tile([P, 5 * V], BF16, name="grad_early", offset=0, align_bytes=64)
         g_codes = keep.tile([P, PASSES * N], U32, name="g_codes", align_bytes=64)
         g_scale = keep.tile([P, PASSES * N], U8, name="g_scale", align_bytes=64)
-        dx_turned = {c: keep.tile([P, D], F32, name=f"dx_turned{c}") for c in EARLY}
+        dx_turned = {c: keep.tile([P, D], F32, name=f"dx_turned{c}", tag=f"dx_turned{c}") for c in EARLY}
         dx_early = {}
         dx_rest = [keep.tile([P, len(LATE) * CHUNK], F32, name=f"dx_rest{j}") for j in range(D_TILES)]
         windows = [keep.tile([P, T], F32, name=f"window{j}") for j in range(D_TILES)]
         ident = keep.tile([P, P], F32, name="ident")
 
         nc.gpsimd.memset(wd_raw_scale[:].bitcast(I32), 0)
-        nc.gpsimd.memset(rw_rows[:], 0.0)
         nc.gpsimd.memset(wv_scale[:].rearrange("p o d -> p (o d)").bitcast(I32), 0)
 
         x_rows = xT.rearrange("(p u e) c -> u p e c", u=PAIRS, e=2)
@@ -96,8 +100,8 @@ def tile_attend_gml_sq_kernel(tc, xT, wd_words, wd_scales, wv_words, wv_scales, 
             words = wd_words[0].rearrange("p v t -> p (v t)").bitcast(I32)
             nc.sync.dma_start(wd_raw[o][:], words[:, o * K_PASS : (o + 1) * K_PASS])
 
-        def load_y(h, o):
-            nc.sync.dma_start(y_sb[h][o][:], y_rows[o][:, :, h * HALF : (h + 1) * HALF])
+        def load_y(h, o, queue=nc.sync):
+            queue.dma_start(y_sb[h][o][:], y_rows[o][:, :, h * HALF : (h + 1) * HALF])
 
         def load_wd_scales(queue, q):
             queue.dma_start(wd_raw_scale[32 * q : 32 * q + 4, :].bitcast(I32), wd_scales[0, 4 * q : 4 * q + 4, :].bitcast(I32))
@@ -108,32 +112,27 @@ def tile_attend_gml_sq_kernel(tc, xT, wd_words, wd_scales, wv_words, wv_scales, 
                 wv_scales[:, 4 * q : 4 * q + 4, :].rearrange("o f d -> f o d").bitcast(I32),
             )
 
-        load_wd_scales(nc.scalar, 0)
-        load_wd_scales(nc.scalar, 1)
-        nc.scalar.dma_start(cw_sb[:], cw.rearrange("(o p t) one -> p o (t one)", o=PASSES, t=LANES))
-        load_wd_scales(nc.sync, 2)
-        load_wd_scales(nc.sync, 3)
-        load_wd(0)
         nc.sync.dma_start(offsets[:], offs)
+        nc.scalar.dma_start(cw_sb[:], cw.rearrange("(o p t) one -> p o (t one)", o=PASSES, t=LANES))
         load_x(0, 0)
-        nc.sync.dma_start(rw_rows[0:CHUNKS, :], rw[0:1, :].rearrange("one (c i) -> (one c) i", c=CHUNKS))
-        load_wv_scales(nc.sync, 0)
-        load_wv_scales(nc.sync, 1)
-        load_wv_scales(nc.sync, 2)
-        load_wv_scales(nc.sync, 3)
-        load_x(1, 0)
-        load_x(1, 1)
-        load_x(1, 2)
+        for q in range(QUADRANTS):
+            load_wd_scales(nc.scalar, q)
+        for k in range(len(X_PIECES[1])):
+            load_x(1, k)
+        nc.sync.dma_start(rw_sb[:], rw.rearrange("p (c i) -> p c i", c=CHUNKS))
+        load_wd(0)
         load_wd(1)
         load_y(0, 0)
         load_y(0, 1)
         load_y(1, 0)
-        load_y(1, 1)
         nc.sync.dma_start(wv_codes[:], wv_words.rearrange("o p d t -> p o (d t)").bitcast(I32))
+        for q in range(QUADRANTS):
+            load_wv_scales(nc.sync, q)
+        load_y(1, 1)
 
         make_identity(nc, ident[:])
         for j in range(D_TILES):
-            (nc.vector if j < 3 else nc.gpsimd).memset(windows[j][:].bitcast(I32), 0)
+            nc.vector.memset(windows[j][:].bitcast(I32), 0)
 
         def reorder_wd(o):
             nc.vector.tensor_copy(
@@ -141,11 +140,11 @@ def tile_attend_gml_sq_kernel(tc, xT, wd_words, wd_scales, wv_words, wv_scales, 
                 wd_raw[o][:].rearrange("p (m t) -> p m t", t=LANES),
             )
 
-        reorder_wd(0)
-        nc.vector.tensor_copy(
-            wd_scale[:].rearrange("p (o t m) -> p o m t", o=PASSES, t=LANES),
-            wd_raw_scale[:].rearrange("p (o m t) -> p o m t", o=PASSES, t=LANES),
-        )
+        def reorder_wd_scale(o):
+            nc.gpsimd.tensor_copy(
+                wd_scale[o][:].rearrange("p (t m) -> p t m", t=LANES),
+                wd_raw_scale[:, o * K_PASS : (o + 1) * K_PASS].rearrange("p (m t) -> p t m", t=LANES),
+            )
 
         def cast_x(u, k, a, b, on_scalar):
             first = X_PIECES[u][k][0]
@@ -156,40 +155,39 @@ def tile_attend_gml_sq_kernel(tc, xT, wd_words, wd_scales, wv_words, wv_scales, 
             else:
                 nc.vector.tensor_copy(dst, src)
 
-        def make_weight(b0, b):
-            col_bank = bank(b0, [P, P], "col_bank")
-            nc.tensor.transpose(col_bank[:], rw_rows[:], ident[:])
-            nc.scalar.copy(rw_col[:], col_bank[:, 0:CHUNKS])
-            rw_bank = bank(b, [P, len(WEIGHTED), CHUNK], "rw_bank")
-            for k, c in enumerate(WEIGHTED):
-                nc.tensor.transpose(rw_bank[:, k, :], rw_col[:, c : c + 1].to_broadcast([P, P]), ident[:])
+        def make_weight(c0, c1):
+            k = WEIGHTED.index(c0)
             for o in range(PASSES):
                 for t in range(LANES):
-                    nc.scalar.activation(weight[:, t, o, :], rw_bank[:].rearrange("p k i -> p (k i)"), COPY, scale=cw_sb[:, o, t : t + 1])
+                    nc.scalar.activation(weight[:, t, k : k + c1 - c0, o, :], rw_sb[:, c0:c1, :], COPY, scale=cw_sb[:, o, t : t + 1])
 
-        def gather(u, c0, c1):
-            nc.vector.tensor_copy(
-                x_listed[:, c0 * CHUNK : c1 * CHUNK, u],
-                x_pairs[u][:].indirect(offsets[:, c0 * LIST_COLS : c1 * LIST_COLS]),
-            )
+        def turn_rw(c, b):
+            col_bank = bank(b, [P, P], "col_bank")
+            nc.tensor.transpose(col_bank[:], rw_sb[:, c, :], ident[:])
+            nc.scalar.copy(rw_col[:], col_bank[:, 0:1])
 
-        def quantize_x(c0, c1):
+        def gather(dst, u, c0, c1):
+            nc.vector.tensor_copy(dst, x_pairs[u][:].indirect(offsets[:, c0 * LIST_COLS : c1 * LIST_COLS]))
+
+        def weave(dst, src):
+            nc.vector.tensor_copy(dst.bitcast(I32), src.bitcast(I32).rearrange("p u i -> p i u"))
+
+        def quantize_x(c0, c1, src):
             cols = slice(c0 * CHUNK, c1 * CHUNK)
             nc.vector.quantize_mx(
                 out=x_codes[:, cols].bitcast(E4M3),
                 scales=x_scale[:, cols],
-                in_=x_listed[:, cols, :].rearrange("p i u -> p (i u)").bitcast(BF16),
+                in_=src.rearrange("p i u -> p (i u)").bitcast(BF16),
             )
 
         def product(c, o, b):
             cols = slice(c * CHUNK, (c + 1) * CHUNK)
             a_bank = bank(b, [P, LANES, CHUNK], f"a_bank{c}{o}")
             for t in range(LANES):
-                scale_cols = slice((o * LANES + t) * P, (o * LANES + t + 1) * P)
                 nc.tensor.matmul_mx(
                     out=a_bank[:, t, :],
                     lhsT=wd_codes[o][:, t * P : (t + 1) * P].bitcast(E4M3),
-                    lhsT_scale=wd_scale[:, scale_cols],
+                    lhsT_scale=wd_scale[o][:, t * P : (t + 1) * P],
                     rhs=x_codes[:, cols].bitcast(E4M3),
                     rhs_scale=x_scale[:, cols],
                     start=True,
@@ -201,18 +199,22 @@ def tile_attend_gml_sq_kernel(tc, xT, wd_words, wd_scales, wv_words, wv_scales, 
             h, within = divmod(c * CHUNK, HALF)
             return y_sb[h][o][:, :, within : within + CHUNK]
 
-        def subtract_targets(c, o, a_bank):
-            k = WEIGHTED.index(c)
-            nc.vector.tensor_tensor(residual[o][:, :, k * CHUNK : (k + 1) * CHUNK], a_bank[:], y_of(c, o), SUB)
+        def residual(c0, c1, o):
+            return res[c0, o][:]
 
-        def weigh(first, last, o, dst, engine, run=RUN):
-            cols = slice(first, last)
+        def subtract_targets(c, o, a_bank):
+            nc.vector.tensor_tensor(residual(c, c + 1, o), a_bank[:], y_of(c, o), SUB)
+
+        def weigh(dst, residuals, weights, engine, run):
             engine.tensor_tensor(
                 dst.rearrange("p (r i t) -> p r t i", i=run, t=LANES),
-                residual[o][:, :, cols].rearrange("p t (r i) -> p r t i", i=run),
-                weight[:, :, o, cols].rearrange("p t (r i) -> p r t i", i=run),
+                residuals.rearrange("p t (r i) -> p r t i", i=run),
+                weights.rearrange("p t (r i) -> p r t i", i=run),
                 MULT,
             )
+
+        def weigh_side(c, o, dst):
+            weigh(dst, res[c, o][:], weight[:, :, WEIGHTED.index(c), o, :], nc.gpsimd, SIDE_RUN)
 
         def scale_targets(c, o):
             for t in range(LANES):
@@ -232,7 +234,7 @@ def tile_attend_gml_sq_kernel(tc, xT, wd_words, wd_scales, wv_words, wv_scales, 
                 grad_turned[c, o][:].rearrange("i (u p e) -> i u p e", u=PAIRS, e=2),
                 sum_bank[:].rearrange("i (u e) p -> i u p e", u=PAIRS),
                 COPY,
-                scale=rw_col[:, c : c + 1],
+                scale=rw_col[:],
             )
 
         def turn_back(c, o, b, dst):
@@ -265,8 +267,10 @@ def tile_attend_gml_sq_kernel(tc, xT, wd_words, wd_scales, wv_words, wv_scales, 
                 )
             return turned_bank
 
-        def turn_early(c, j0, j1, turned_bank, b1):
+        def copy_early(c, j0, j1, turned_bank):
             nc.scalar.copy(dx_turned[c][:, j0 * P : j1 * P], turned_bank[:, j0 * P : j1 * P])
+
+        def turn_early(c, j0, j1, b1):
             early_bank = bank(b1, [P, j1 - j0, CHUNK], f"early_bank{c}{j0}")
             for j in range(j0, j1):
                 nc.tensor.transpose(early_bank[:, j - j0, :], dx_turned[c][:, j * P : (j + 1) * P], ident[:])
@@ -289,7 +293,7 @@ def tile_attend_gml_sq_kernel(tc, xT, wd_words, wd_scales, wv_words, wv_scales, 
                     start=(o == passes[0]),
                     stop=(o == passes[-1]),
                 )
-            nc.scalar.copy(dx_rest[j][:], dx_bank[:, CHUNK:N])
+            nc.scalar.copy(dx_rest[j][:], dx_bank[:, N - len(LATE) * CHUNK : N])
 
         def scatter_early(c, j):
             nc.vector.tensor_copy(windows[j][:].indirect(offsets[:, c * LIST_COLS : (c + 1) * LIST_COLS]), dx_early[c, j])
@@ -300,63 +304,92 @@ def tile_attend_gml_sq_kernel(tc, xT, wd_words, wd_scales, wv_words, wv_scales, 
 
         cast_x(0, 0, 0, 320, True)
         cast_x(0, 0, 320, 1024, False)
-        gather(0, 0, CHUNKS)
+        reorder_wd_scale(0)
+        gather(x_first[:, 0, :], 0, 0, 2)
+        gather(x_second[:, 0, :], 0, 2, 4)
         cast_x(1, 0, 0, 512, True)
-        cast_x(1, 1, 512, 768, False)
-        cast_x(1, 2, 768, 1024, False)
+        cast_x(1, 1, 512, 704, True)
+        cast_x(1, 1, 704, 1024, False)
+        reorder_wd_scale(1)
         nc.scalar.mul(cw_neg[:], cw_sb[:], -1.0)
-        make_weight(6, 7)
+        make_weight(0, 1)
+        turn_rw(1, 7)
+        make_weight(2, 4)
 
-        gather(1, 0, 1)
-        quantize_x(0, 1)
+        for c in range(2):
+            gather(x_first[:, 1, c * CHUNK : (c + 1) * CHUNK], 1, c, c + 1)
+        for c in range(2):
+            weave(listed_first[:, c * CHUNK : (c + 1) * CHUNK, :], x_first[:, :, c * CHUNK : (c + 1) * CHUNK])
+        reorder_wd(0)
+        quantize_x(0, 1, listed_first[:, 0:CHUNK, :])
         a00 = product(0, 0, 0)
-        gather(1, 1, 2)
+        quantize_x(1, 2, listed_first[:, CHUNK:HALF, :])
+        a10 = product(1, 0, 2)
+        gather(x_second[:, 1, :], 1, 2, 4)
         reorder_wd(1)
         a01 = product(0, 1, 1)
-        quantize_x(1, 2)
-        a10 = product(1, 0, 2)
         a11 = product(1, 1, 3)
-        gather(1, 2, 4)
-        scale_targets(1, 0)
-        scale_product(1, 0, a10)
+        weave(listed_second[:], x_second)
         subtract_targets(0, 0, a00)
-        quantize_x(2, 4)
+        quantize_x(2, 4, listed_second[:])
         a30 = product(3, 0, 4)
         a31 = product(3, 1, 5)
         a20 = product(2, 0, 6)
         a21 = product(2, 1, 7)
         subtract_targets(0, 1, a01)
-        scale_targets(1, 1)
-        scale_product(1, 1, a11)
-        weigh(0, CHUNK, 0, grad_early[:, 0:K_PASS], nc.vector)
-        weigh(0, CHUNK, 1, grad_early[:, K_PASS:V], nc.vector)
-        quantize_grad(g_cols(0, 0, 2), grad_early[:])
-        grad_late = [keep.tile([P, 2 * K_PASS], BF16, name=f"grad_late{o}", tag=("grad_early", "grad_late1")[o], align_bytes=64) for o in range(PASSES)]
-        t0 = back_early(0, 2)
-        e00 = turn_early(0, 0, 2, t0, 3)
-        turn_and_weigh(1, 0, 0)
-        turn_and_weigh(1, 1, 1)
-        e02 = turn_early(0, 2, 4, t0, 0)
+        weigh(grad_early[:, 0:V], res_first[:].rearrange("p t o i -> p t (o i)"), weight[:, :, 0, :, :].rearrange("p t o i -> p t (o i)"), nc.vector, RUN)
+        quantize_grad(g_cols(0, 0, 2), grad_early[:, 0:V])
+        res[3, 0] = keep.tile([P, LANES, CHUNK], F32, name="res30")
+        res[3, 1] = relay.tile([P, 2 * LANES, CHUNK], F32, name="res31", offset=2048)[:, 0:LANES, :]
+        res[2, 1] = relay.tile([P, LANES, CHUNK], F32, name="res21", offset=6144)
+        res[2, 0] = relay.tile([P, LANES, CHUNK], F32, name="res20", offset=8192)
+        for o in range(PASSES):
+            scale_targets(1, o)
+            scale_product(1, o, (a10, a11)[o])
+        grad_second = keep.tile([P, V], BF16, name="grad_second", tag="grad_side", align_bytes=64)
+        t0 = back_early(0, 0)
+        copy_early(0, 0, 1, t0)
+        copy_early(0, 1, 4, t0)
+        e0a = turn_early(0, 0, 1, 1)
         subtract_targets(3, 0, a30)
-        weigh(3 * CHUNK - SIDE, 3 * CHUNK, 0, grad_late[0][:, V - LANES * SIDE : V], nc.gpsimd, SIDE_RUN)
-        subtract_targets(2, 0, a20)
+        weigh_side(3, 0, grad_second[:, 0:K_PASS])
         subtract_targets(3, 1, a31)
+        e0b = turn_early(0, 1, 4, 3)
+        subtract_targets(2, 0, a20)
         subtract_targets(2, 1, a21)
-        weigh(CHUNK, 3 * CHUNK - SIDE, 0, grad_late[0][:, 0 : V - LANES * SIDE], nc.vector)
-        weigh(CHUNK, 3 * CHUNK, 1, grad_late[1][:], nc.vector)
-        held = keep.tile([P, V], F32, name="held", tag="y_sb11", align_bytes=64)
-        grad1 = held[:, 0:K_PASS].bitcast(BF16)
-        turn_back(1, 0, 4, grad1[:, 0:K_PASS])
-        turn_back(1, 1, 6, grad1[:, K_PASS:V])
-        fetch_early(0, 0, 2, e00, held[:, K_PASS : K_PASS + 2 * CHUNK])
-        fetch_early(0, 2, 4, e02, held[:, K_PASS + 2 * CHUNK : V])
-        quantize_grad(slice(G_COLS[2, 0] * CHUNK, (G_COLS[3, 0] + 1) * CHUNK), grad_late[0][:])
-        quantize_grad(g_cols(1, 0, 1), grad1[:, 0:K_PASS])
-        quantize_grad(g_cols(1, 1, 2), grad1[:, K_PASS:V])
-        quantize_grad(slice(G_COLS[2, 1] * CHUNK, (G_COLS[3, 1] + 1) * CHUNK), grad_late[1][:])
-        for j in range(D_TILES):
-            back_rest(j, (5, 7, 1, 2)[j], (1, 0))
-        for j in range(D_TILES):
+        weigh(grad_second[:, K_PASS:V], res[3, 1], weight[:, :, 2, 1, :], nc.vector, RUN)
+        quantize_grad(g_cols(3, 0, 2), grad_second[:])
+        grad_turned = {
+            (1, 0): relay.tile([P, K_PASS], BF16, name="grad_turned10", offset=4096),
+            (1, 1): relay.tile([P, K_PASS], BF16, name="grad_turned11", offset=5120),
+        }
+        part_a = {0: relay.tile([P, CHUNK], F32, name="part_a0", offset=2048), 3: keep.tile([P, CHUNK], F32, name="part_a3")}
+        fetch_early(0, 0, 1, e0a, part_a[0][:])
+        part_b0 = relay.tile([P, 3 * CHUNK], F32, name="part_b0", offset=2560)
+        fetch_early(0, 1, 4, e0b, part_b0[:])
+        scatter_early(0, 0)
+        grad_late = keep.tile([P, 4 * K_PASS], BF16, name="grad_late", tag="grad_side", align_bytes=64)
+        weigh_side(2, 0, grad_late[:, K_PASS : 2 * K_PASS])
+        weigh_side(2, 1, grad_late[:, 3 * K_PASS : 4 * K_PASS])
+        t1 = back_early(3, 0)
+        copy_early(3, 0, 1, t1)
+        copy_early(3, 1, 4, t1)
+        e1a = turn_early(3, 0, 1, 1)
+        fetch_early(3, 0, 1, e1a, part_a[3][:])
+        e1b = turn_early(3, 1, 4, 3)
+        turn_and_weigh(1, 0, 2)
+        turn_and_weigh(1, 1, 5)
+        turn_back(1, 0, 4, grad_late[:, 0:K_PASS])
+        turn_back(1, 1, 6, grad_late[:, 2 * K_PASS : 3 * K_PASS])
+        part_b1 = relay.tile([P, 3 * CHUNK], F32, name="part_b1", offset=5632)
+        fetch_early(3, 1, 4, e1b, part_b1[:])
+        for j in range(1, D_TILES):
             scatter_early(0, j)
+        scatter_early(3, 0)
+        quantize_grad(slice(G_COLS[1, 0] * CHUNK, (G_COLS[2, 1] + 1) * CHUNK), grad_late[:])
+        for j in range(D_TILES):
+            back_rest(j, (7, 2, 5, 4)[j], (1, 0))
+        for j in range(1, D_TILES):
+            scatter_early(3, j)
         for j in range(D_TILES):
             scatter_rest_and_store(j)

@@ -52,7 +52,7 @@ def tile_attend_gml_sq_kernel(tc, xT, wd_words, wd_scales, wv_words, wv_scales, 
             return psum.tile(shape, F32, name=name, tag=f"bank{b}")
 
         offsets = keep.tile([P, N // 16], U16, name="offsets")
-        wd_raw = [keep.tile([P, K_PASS], I32, name=f"wd_raw{o}") for o in range(PASSES)]
+        wd_raw = [keep.tile([P, K_PASS], I32, name=f"wd_raw{o}", tag=f"wd_raw{o}") for o in range(PASSES)]
         wd_raw_scale = keep.tile([P, V], U8, name="wd_raw_scale", align_bytes=64)
         wd_codes = [keep.tile([P, K_PASS], I32, name=f"wd_codes{o}", align_bytes=64) for o in range(PASSES)]
         wv_codes = keep.tile([P, PASSES, D], I32, name="wv_codes", align_bytes=64)
@@ -67,17 +67,18 @@ def tile_attend_gml_sq_kernel(tc, xT, wd_words, wd_scales, wv_words, wv_scales, 
         x_first = keep.tile([P, PAIRS, HALF], U32, name="x_first")
         x_shared = keep.tile([P, 3 * HALF], U32, name="x_shared", align_bytes=64)
         x_second = x_shared[:, 0 : 2 * HALF].rearrange("p (u i) -> p u i", u=PAIRS)
-        listed_first = x_shared[:, HALF : 3 * HALF].rearrange("p (i u) -> p i u", u=PAIRS)
+        listed_first = [x_shared[:, (2 - c) * HALF : (3 - c) * HALF].rearrange("p (i u) -> p i u", u=PAIRS) for c in range(2)]
         listed_second = keep.tile([P, HALF, PAIRS], U32, name="listed_second", align_bytes=64)
         x_codes = keep.tile([P, N], U32, name="x_codes", align_bytes=64)
         x_scale = keep.tile([P, N], U8, name="x_scale", align_bytes=64)
         y_sb = [[keep.tile([P, LANES, HALF], F32, name=f"y_sb{h}{o}", tag=f"y_sb{h}{o}", align_bytes=64) for o in range(PASSES)] for h in range(2)]
-        weight = keep.tile([P, LANES, len(WEIGHTED), PASSES, CHUNK], F32, name="weight")
+        weight_early = {c: keep.tile([P, LANES, PASSES, CHUNK], F32, name=f"weight{c}") for c in EARLY}
+        weight = {(c, o): weight_early[c][:, :, o, :] for c in EARLY for o in range(PASSES)}
         res_first = keep.tile([P, LANES, PASSES, CHUNK], F32, name="res_first", tag="grad_side", align_bytes=64)
         res = {(0, o): res_first[:, :, o, :] for o in range(PASSES)}
         a_scaled = {(c, o): keep.tile([P, LANES, CHUNK], F32, name=f"a_scaled{c}{o}") for c, o in TURNED}
         y_scaled = {(c, o): keep.tile([P, LANES, CHUNK], F32, name=f"y_scaled{c}{o}") for c, o in TURNED}
-        grad_early = relay.tile([P, 5 * V], BF16, name="grad_early", offset=0, align_bytes=64)
+        grad_early = relay.tile([P, 7 * V], BF16, name="grad_early", offset=0, align_bytes=64)
         g_codes = keep.tile([P, PASSES * N], U32, name="g_codes", align_bytes=64)
         g_scale = keep.tile([P, PASSES * N], U8, name="g_scale", align_bytes=64)
         dx_turned = {c: keep.tile([P, D], F32, name=f"dx_turned{c}", tag=f"dx_turned{c}") for c in EARLY}
@@ -155,11 +156,9 @@ def tile_attend_gml_sq_kernel(tc, xT, wd_words, wd_scales, wv_words, wv_scales, 
             else:
                 nc.vector.tensor_copy(dst, src)
 
-        def make_weight(c0, c1):
-            k = WEIGHTED.index(c0)
-            for o in range(PASSES):
-                for t in range(LANES):
-                    nc.scalar.activation(weight[:, t, k : k + c1 - c0, o, :], rw_sb[:, c0:c1, :], COPY, scale=cw_sb[:, o, t : t + 1])
+        def make_weight(c, o):
+            for t in range(LANES):
+                nc.scalar.activation(weight[c, o][:, t, :], rw_sb[:, c, :], COPY, scale=cw_sb[:, o, t : t + 1])
 
         def turn_rw(c, b):
             col_bank = bank(b, [P, P], "col_bank")
@@ -170,7 +169,7 @@ def tile_attend_gml_sq_kernel(tc, xT, wd_words, wd_scales, wv_words, wv_scales, 
             nc.vector.tensor_copy(dst, x_pairs[u][:].indirect(offsets[:, c0 * LIST_COLS : c1 * LIST_COLS]))
 
         def weave(dst, src):
-            nc.vector.tensor_copy(dst.bitcast(I32), src.bitcast(I32).rearrange("p u i -> p i u"))
+            nc.scalar.copy(dst, src.rearrange("p u i -> p i u"))
 
         def quantize_x(c0, c1, src):
             cols = slice(c0 * CHUNK, c1 * CHUNK)
@@ -214,7 +213,7 @@ def tile_attend_gml_sq_kernel(tc, xT, wd_words, wd_scales, wv_words, wv_scales, 
             )
 
         def weigh_side(c, o, dst):
-            weigh(dst, res[c, o][:], weight[:, :, WEIGHTED.index(c), o, :], nc.gpsimd, SIDE_RUN)
+            weigh(dst, res[c, o][:], weight[c, o], nc.gpsimd, SIDE_RUN)
 
         def scale_targets(c, o):
             for t in range(LANES):
@@ -312,24 +311,31 @@ def tile_attend_gml_sq_kernel(tc, xT, wd_words, wd_scales, wv_words, wv_scales, 
         cast_x(1, 1, 704, 1024, False)
         reorder_wd_scale(1)
         nc.scalar.mul(cw_neg[:], cw_sb[:], -1.0)
-        make_weight(0, 1)
-        turn_rw(1, 7)
-        make_weight(2, 4)
 
         for c in range(2):
             gather(x_first[:, 1, c * CHUNK : (c + 1) * CHUNK], 1, c, c + 1)
         for c in range(2):
-            weave(listed_first[:, c * CHUNK : (c + 1) * CHUNK, :], x_first[:, :, c * CHUNK : (c + 1) * CHUNK])
+            weave(listed_first[c], x_first[:, :, c * CHUNK : (c + 1) * CHUNK])
         reorder_wd(0)
-        quantize_x(0, 1, listed_first[:, 0:CHUNK, :])
+        quantize_x(0, 1, listed_first[0])
         a00 = product(0, 0, 0)
-        quantize_x(1, 2, listed_first[:, CHUNK:HALF, :])
-        a10 = product(1, 0, 2)
-        gather(x_second[:, 1, :], 1, 2, 4)
         reorder_wd(1)
         a01 = product(0, 1, 1)
+        quantize_x(1, 2, listed_first[1])
+        a10 = product(1, 0, 2)
         a11 = product(1, 1, 3)
+        gather(x_second[:, 1, :], 1, 2, 4)
         weave(listed_second[:], x_second)
+        weight[2, 0] = keep.tile([P, LANES, CHUNK], F32, name="weight20", tag="wd_raw1")[:]
+        nc.gpsimd.tensor_tensor(
+            weight[2, 0],
+            rw_sb[:, 2:3, :].to_broadcast([P, LANES, CHUNK]),
+            cw_sb[:, 0, :].unsqueeze(2).to_broadcast([P, LANES, CHUNK]),
+            MULT,
+        )
+        make_weight(0, 0)
+        make_weight(0, 1)
+        turn_rw(1, 7)
         subtract_targets(0, 0, a00)
         quantize_x(2, 4, listed_second[:])
         a30 = product(3, 0, 4)
@@ -337,15 +343,17 @@ def tile_attend_gml_sq_kernel(tc, xT, wd_words, wd_scales, wv_words, wv_scales, 
         a20 = product(2, 0, 6)
         a21 = product(2, 1, 7)
         subtract_targets(0, 1, a01)
-        weigh(grad_early[:, 0:V], res_first[:].rearrange("p t o i -> p t (o i)"), weight[:, :, 0, :, :].rearrange("p t o i -> p t (o i)"), nc.vector, RUN)
+        weigh(grad_early[:, 0:V], res_first[:].rearrange("p t o i -> p t (o i)"), weight_early[0][:].rearrange("p t o i -> p t (o i)"), nc.vector, RUN)
         quantize_grad(g_cols(0, 0, 2), grad_early[:, 0:V])
         res[3, 0] = keep.tile([P, LANES, CHUNK], F32, name="res30")
-        res[3, 1] = relay.tile([P, 2 * LANES, CHUNK], F32, name="res31", offset=2048)[:, 0:LANES, :]
-        res[2, 1] = relay.tile([P, LANES, CHUNK], F32, name="res21", offset=6144)
-        res[2, 0] = relay.tile([P, LANES, CHUNK], F32, name="res20", offset=8192)
+        res[3, 1] = relay.tile([P, 4 * LANES, CHUNK], F32, name="res31", offset=2048)[:, 0:LANES, :]
+        res[2, 1] = relay.tile([P, LANES, CHUNK], F32, name="res21", offset=10240)
+        res[2, 0] = relay.tile([P, LANES, CHUNK], F32, name="res20", offset=12288)
         for o in range(PASSES):
             scale_targets(1, o)
             scale_product(1, o, (a10, a11)[o])
+        make_weight(3, 0)
+        make_weight(3, 1)
         grad_second = keep.tile([P, V], BF16, name="grad_second", tag="grad_side", align_bytes=64)
         t0 = back_early(0, 0)
         copy_early(0, 0, 1, t0)
@@ -354,19 +362,20 @@ def tile_attend_gml_sq_kernel(tc, xT, wd_words, wd_scales, wv_words, wv_scales, 
         subtract_targets(3, 0, a30)
         weigh_side(3, 0, grad_second[:, 0:K_PASS])
         subtract_targets(3, 1, a31)
-        e0b = turn_early(0, 1, 4, 3)
+        e0b = turn_early(0, 1, 4, 4)
         subtract_targets(2, 0, a20)
         subtract_targets(2, 1, a21)
-        weigh(grad_second[:, K_PASS:V], res[3, 1], weight[:, :, 2, 1, :], nc.vector, RUN)
+        weigh(grad_second[:, K_PASS:V], res[3, 1], weight[3, 1], nc.vector, RUN)
         quantize_grad(g_cols(3, 0, 2), grad_second[:])
-        grad_turned = {
-            (1, 0): relay.tile([P, K_PASS], BF16, name="grad_turned10", offset=4096),
-            (1, 1): relay.tile([P, K_PASS], BF16, name="grad_turned11", offset=5120),
-        }
+        grad_turned = {(1, o): keep.tile([P, K_PASS], BF16, name=f"grad_turned{o}") for o in range(PASSES)}
         part_a = {0: relay.tile([P, CHUNK], F32, name="part_a0", offset=2048), 3: keep.tile([P, CHUNK], F32, name="part_a3")}
         fetch_early(0, 0, 1, e0a, part_a[0][:])
         part_b0 = relay.tile([P, 3 * CHUNK], F32, name="part_b0", offset=2560)
         fetch_early(0, 1, 4, e0b, part_b0[:])
+        turn_and_weigh(1, 0, 2)
+        turn_and_weigh(1, 1, 3)
+        weight[2, 1] = relay.tile([P, LANES, CHUNK], F32, name="weight21", offset=4096)[:]
+        make_weight(2, 1)
         scatter_early(0, 0)
         grad_late = keep.tile([P, 4 * K_PASS], BF16, name="grad_late", tag="grad_side", align_bytes=64)
         weigh_side(2, 0, grad_late[:, K_PASS : 2 * K_PASS])
@@ -374,21 +383,19 @@ def tile_attend_gml_sq_kernel(tc, xT, wd_words, wd_scales, wv_words, wv_scales, 
         t1 = back_early(3, 0)
         copy_early(3, 0, 1, t1)
         copy_early(3, 1, 4, t1)
-        e1a = turn_early(3, 0, 1, 1)
+        e1a = turn_early(3, 0, 1, 2)
         fetch_early(3, 0, 1, e1a, part_a[3][:])
         e1b = turn_early(3, 1, 4, 3)
-        turn_and_weigh(1, 0, 2)
-        turn_and_weigh(1, 1, 5)
-        turn_back(1, 0, 4, grad_late[:, 0:K_PASS])
-        turn_back(1, 1, 6, grad_late[:, 2 * K_PASS : 3 * K_PASS])
-        part_b1 = relay.tile([P, 3 * CHUNK], F32, name="part_b1", offset=5632)
+        turn_back(1, 0, 1, grad_late[:, 0:K_PASS])
+        turn_back(1, 1, 4, grad_late[:, 2 * K_PASS : 3 * K_PASS])
+        part_b1 = relay.tile([P, 3 * CHUNK], F32, name="part_b1", offset=10240)
         fetch_early(3, 1, 4, e1b, part_b1[:])
         for j in range(1, D_TILES):
             scatter_early(0, j)
         scatter_early(3, 0)
         quantize_grad(slice(G_COLS[1, 0] * CHUNK, (G_COLS[2, 1] + 1) * CHUNK), grad_late[:])
         for j in range(D_TILES):
-            back_rest(j, (7, 2, 5, 4)[j], (1, 0))
+            back_rest(j, (5, 6, 7, 0)[j], (1, 0))
         for j in range(1, D_TILES):
             scatter_early(3, j)
         for j in range(D_TILES):

@@ -46,13 +46,14 @@ def tile_attend_gml_sq_kernel(tc, xT, wd_words, wd_scales, wv_words, wv_scales, 
     with ExitStack() as ctx:
         keep = ctx.enter_context(tc.tile_pool(name="keep", bufs=1))
         relay = ctx.enter_context(tc.tile_pool(name="relay", bufs=1))
+        front = ctx.enter_context(tc.tile_pool(name="front", bufs=1))
         psum = ctx.enter_context(tc.psum_pool(name="psum", bufs=1))
 
         def bank(b, shape, name):
             return psum.tile(shape, F32, name=name, tag=f"bank{b}")
 
         offsets = keep.tile([P, N // 16], U16, name="offsets")
-        wd_raw = [keep.tile([P, K_PASS], I32, name=f"wd_raw{o}", tag=f"wd_raw{o}") for o in range(PASSES)]
+        wd_raw = [keep.tile([P, K_PASS], I32, name="wd_raw0"), front.tile([P, 3 * K_PASS], I32, name="wd_raw1", offset=0)[:, 0:K_PASS]]
         wd_raw_scale = keep.tile([P, V], U8, name="wd_raw_scale", align_bytes=64)
         wd_codes = [keep.tile([P, K_PASS], I32, name=f"wd_codes{o}", align_bytes=64) for o in range(PASSES)]
         wv_codes = keep.tile([P, PASSES, D], I32, name="wv_codes", align_bytes=64)
@@ -62,20 +63,17 @@ def tile_attend_gml_sq_kernel(tc, xT, wd_words, wd_scales, wv_words, wv_scales, 
         rw_sb = keep.tile([P, CHUNKS, CHUNK], F32, name="rw_sb")
         x_raw = [[keep.tile([P, 2, b - a], F32, name=f"x_raw{u}_{a}", tag=f"x_raw{u}_{a}", align_bytes=64) for a, b in X_PIECES[u]] for u in range(PAIRS)]
         rw_col = keep.tile([P, 1], F32, name="rw_col")
-        wd_scale = [keep.tile([P, K_PASS], U8, name=f"wd_scale{o}", tag=("x_raw0_0", "x_raw1_512")[o], align_bytes=64) for o in range(PASSES)]
         x_pairs = [keep.tile([P, T], U32, name=f"x_pairs{u}") for u in range(PAIRS)]
-        x_first = keep.tile([P, PAIRS, HALF], U32, name="x_first")
+        x_first = keep.tile([P, PAIRS, HALF], U32, name="x_first", tag="x_first", align_bytes=64)
+        wd_scale = [keep.tile([P, K_PASS], U8, name=f"wd_scale{o}", tag=("x_raw0_0", "x_first")[o], align_bytes=64) for o in range(PASSES)]
         x_shared = keep.tile([P, 3 * HALF], U32, name="x_shared", align_bytes=64)
         x_second = x_shared[:, 0 : 2 * HALF].rearrange("p (u i) -> p u i", u=PAIRS)
         listed_first = [x_shared[:, (2 - c) * HALF : (3 - c) * HALF].rearrange("p (i u) -> p i u", u=PAIRS) for c in range(2)]
-        listed_second = keep.tile([P, HALF, PAIRS], U32, name="listed_second", align_bytes=64)
         x_codes = keep.tile([P, N], U32, name="x_codes", align_bytes=64)
         x_scale = keep.tile([P, N], U8, name="x_scale", align_bytes=64)
         y_sb = [[keep.tile([P, LANES, HALF], F32, name=f"y_sb{h}{o}", tag=f"y_sb{h}{o}", align_bytes=64) for o in range(PASSES)] for h in range(2)]
         weight_early = {c: keep.tile([P, LANES, PASSES, CHUNK], F32, name=f"weight{c}") for c in EARLY}
         weight = {(c, o): weight_early[c][:, :, o, :] for c in EARLY for o in range(PASSES)}
-        res_first = keep.tile([P, LANES, PASSES, CHUNK], F32, name="res_first", tag="grad_side", align_bytes=64)
-        res = {(0, o): res_first[:, :, o, :] for o in range(PASSES)}
         a_scaled = {(c, o): keep.tile([P, LANES, CHUNK], F32, name=f"a_scaled{c}{o}") for c, o in TURNED}
         y_scaled = {(c, o): keep.tile([P, LANES, CHUNK], F32, name=f"y_scaled{c}{o}") for c, o in TURNED}
         grad_early = relay.tile([P, 7 * V], BF16, name="grad_early", offset=0, align_bytes=64)
@@ -122,8 +120,8 @@ def tile_attend_gml_sq_kernel(tc, xT, wd_words, wd_scales, wv_words, wv_scales, 
             load_x(1, k)
         nc.sync.dma_start(rw_sb[:], rw.rearrange("p (c i) -> p c i", c=CHUNKS))
         load_wd(0)
-        load_wd(1)
         load_y(0, 0)
+        load_wd(1)
         load_y(0, 1)
         load_y(1, 0)
         nc.sync.dma_start(wv_codes[:], wv_words.rearrange("o p d t -> p o (d t)").bitcast(I32))
@@ -142,7 +140,7 @@ def tile_attend_gml_sq_kernel(tc, xT, wd_words, wd_scales, wv_words, wv_scales, 
             )
 
         def reorder_wd_scale(o):
-            nc.gpsimd.tensor_copy(
+            (nc.gpsimd, nc.vector)[o].tensor_copy(
                 wd_scale[o][:].rearrange("p (t m) -> p t m", t=LANES),
                 wd_raw_scale[:, o * K_PASS : (o + 1) * K_PASS].rearrange("p (m t) -> p t m", t=LANES),
             )
@@ -168,8 +166,11 @@ def tile_attend_gml_sq_kernel(tc, xT, wd_words, wd_scales, wv_words, wv_scales, 
         def gather(dst, u, c0, c1):
             nc.vector.tensor_copy(dst, x_pairs[u][:].indirect(offsets[:, c0 * LIST_COLS : c1 * LIST_COLS]))
 
-        def weave(dst, src):
-            nc.scalar.copy(dst, src.rearrange("p u i -> p i u"))
+        def weave(dst, src, on_scalar=True):
+            if on_scalar:
+                nc.scalar.copy(dst, src.rearrange("p u i -> p i u"))
+            else:
+                nc.vector.tensor_copy(dst.bitcast(I32), src.bitcast(I32).rearrange("p u i -> p i u"))
 
         def quantize_x(c0, c1, src):
             cols = slice(c0 * CHUNK, c1 * CHUNK)
@@ -309,7 +310,6 @@ def tile_attend_gml_sq_kernel(tc, xT, wd_words, wd_scales, wv_words, wv_scales, 
         cast_x(1, 0, 0, 512, True)
         cast_x(1, 1, 512, 704, True)
         cast_x(1, 1, 704, 1024, False)
-        reorder_wd_scale(1)
         nc.scalar.mul(cw_neg[:], cw_sb[:], -1.0)
 
         for c in range(2):
@@ -319,20 +319,17 @@ def tile_attend_gml_sq_kernel(tc, xT, wd_words, wd_scales, wv_words, wv_scales, 
         reorder_wd(0)
         quantize_x(0, 1, listed_first[0])
         a00 = product(0, 0, 0)
-        reorder_wd(1)
-        a01 = product(0, 1, 1)
         quantize_x(1, 2, listed_first[1])
         a10 = product(1, 0, 2)
-        a11 = product(1, 1, 3)
         gather(x_second[:, 1, :], 1, 2, 4)
-        weave(listed_second[:], x_second)
-        weight[2, 0] = keep.tile([P, LANES, CHUNK], F32, name="weight20", tag="wd_raw1")[:]
-        nc.gpsimd.tensor_tensor(
-            weight[2, 0],
-            rw_sb[:, 2:3, :].to_broadcast([P, LANES, CHUNK]),
-            cw_sb[:, 0, :].unsqueeze(2).to_broadcast([P, LANES, CHUNK]),
-            MULT,
-        )
+        reorder_wd_scale(1)
+        reorder_wd(1)
+        a01 = product(0, 1, 1)
+        a11 = product(1, 1, 3)
+        listed_second = front.tile([P, HALF, PAIRS], U32, name="listed_second", offset=4096, align_bytes=64)
+        res_first = front.tile([P, LANES, PASSES, CHUNK], F32, name="res_first", offset=0)
+        res = {(0, o): res_first[:, :, o, :] for o in range(PASSES)}
+        weave(listed_second[:], x_second, False)
         make_weight(0, 0)
         make_weight(0, 1)
         turn_rw(1, 7)
@@ -354,7 +351,9 @@ def tile_attend_gml_sq_kernel(tc, xT, wd_words, wd_scales, wv_words, wv_scales, 
             scale_product(1, o, (a10, a11)[o])
         make_weight(3, 0)
         make_weight(3, 1)
-        grad_second = keep.tile([P, V], BF16, name="grad_second", tag="grad_side", align_bytes=64)
+        weight[2, 0] = keep.tile([P, LANES, CHUNK], F32, name="weight20")[:]
+        make_weight(2, 0)
+        grad_second = front.tile([P, V], BF16, name="grad_second", offset=0, align_bytes=64)
         t0 = back_early(0, 0)
         copy_early(0, 0, 1, t0)
         copy_early(0, 1, 4, t0)
@@ -367,7 +366,10 @@ def tile_attend_gml_sq_kernel(tc, xT, wd_words, wd_scales, wv_words, wv_scales, 
         subtract_targets(2, 1, a21)
         weigh(grad_second[:, K_PASS:V], res[3, 1], weight[3, 1], nc.vector, RUN)
         quantize_grad(g_cols(3, 0, 2), grad_second[:])
-        grad_turned = {(1, o): keep.tile([P, K_PASS], BF16, name=f"grad_turned{o}") for o in range(PASSES)}
+        grad_turned = {
+            (1, 0): keep.tile([P, K_PASS], BF16, name="grad_turned0"),
+            (1, 1): relay.tile([P, K_PASS], BF16, name="grad_turned1", offset=6144),
+        }
         part_a = {0: relay.tile([P, CHUNK], F32, name="part_a0", offset=2048), 3: keep.tile([P, CHUNK], F32, name="part_a3")}
         fetch_early(0, 0, 1, e0a, part_a[0][:])
         part_b0 = relay.tile([P, 3 * CHUNK], F32, name="part_b0", offset=2560)
@@ -377,7 +379,7 @@ def tile_attend_gml_sq_kernel(tc, xT, wd_words, wd_scales, wv_words, wv_scales, 
         weight[2, 1] = relay.tile([P, LANES, CHUNK], F32, name="weight21", offset=4096)[:]
         make_weight(2, 1)
         scatter_early(0, 0)
-        grad_late = keep.tile([P, 4 * K_PASS], BF16, name="grad_late", tag="grad_side", align_bytes=64)
+        grad_late = front.tile([P, 4 * K_PASS], BF16, name="grad_late", offset=0, align_bytes=64)
         weigh_side(2, 0, grad_late[:, K_PASS : 2 * K_PASS])
         weigh_side(2, 1, grad_late[:, 3 * K_PASS : 4 * K_PASS])
         t1 = back_early(3, 0)
@@ -385,7 +387,7 @@ def tile_attend_gml_sq_kernel(tc, xT, wd_words, wd_scales, wv_words, wv_scales, 
         copy_early(3, 1, 4, t1)
         e1a = turn_early(3, 0, 1, 2)
         fetch_early(3, 0, 1, e1a, part_a[3][:])
-        e1b = turn_early(3, 1, 4, 3)
+        e1b = turn_early(3, 1, 4, 5)
         turn_back(1, 0, 1, grad_late[:, 0:K_PASS])
         turn_back(1, 1, 4, grad_late[:, 2 * K_PASS : 3 * K_PASS])
         part_b1 = relay.tile([P, 3 * CHUNK], F32, name="part_b1", offset=10240)
@@ -395,7 +397,7 @@ def tile_attend_gml_sq_kernel(tc, xT, wd_words, wd_scales, wv_words, wv_scales, 
         scatter_early(3, 0)
         quantize_grad(slice(G_COLS[1, 0] * CHUNK, (G_COLS[2, 1] + 1) * CHUNK), grad_late[:])
         for j in range(D_TILES):
-            back_rest(j, (5, 6, 7, 0)[j], (1, 0))
+            back_rest(j, (6, 7, 3, 0)[j], (1, 0))
         for j in range(1, D_TILES):
             scatter_early(3, j)
         for j in range(D_TILES):

@@ -53,7 +53,7 @@ def tile_attend_gml_sq_kernel(tc, xT, wd_words, wd_scales, wv_words, wv_scales, 
             return psum.tile(shape, F32, name=name, tag=f"bank{b}")
 
         offsets = keep.tile([P, N // 16], U16, name="offsets")
-        wd_raw = [keep.tile([P, K_PASS], I32, name="wd_raw0"), front.tile([P, 3 * K_PASS], I32, name="wd_raw1", offset=0)[:, 0:K_PASS]]
+        wd_raw = [keep.tile([P, K_PASS], I32, name=f"wd_raw{o}", tag=f"wd_raw{o}", align_bytes=64) for o in range(PASSES)]
         wd_raw_scale = keep.tile([P, V], U8, name="wd_raw_scale", align_bytes=64)
         wd_codes = [keep.tile([P, K_PASS], I32, name=f"wd_codes{o}", align_bytes=64) for o in range(PASSES)]
         wv_codes = keep.tile([P, PASSES, D], I32, name="wv_codes", align_bytes=64)
@@ -65,10 +65,9 @@ def tile_attend_gml_sq_kernel(tc, xT, wd_words, wd_scales, wv_words, wv_scales, 
         rw_col = keep.tile([P, 1], F32, name="rw_col")
         x_pairs = [keep.tile([P, T], U32, name=f"x_pairs{u}") for u in range(PAIRS)]
         x_first = keep.tile([P, PAIRS, HALF], U32, name="x_first", tag="x_first", align_bytes=64)
-        wd_scale = [keep.tile([P, K_PASS], U8, name=f"wd_scale{o}", tag=("x_raw0_0", "x_first")[o], align_bytes=64) for o in range(PASSES)]
-        x_shared = keep.tile([P, 3 * HALF], U32, name="x_shared", align_bytes=64)
-        x_second = x_shared[:, 0 : 2 * HALF].rearrange("p (u i) -> p u i", u=PAIRS)
-        listed_first = [x_shared[:, (2 - c) * HALF : (3 - c) * HALF].rearrange("p (i u) -> p i u", u=PAIRS) for c in range(2)]
+        wd_scale = [keep.tile([P, K_PASS], U8, name=f"wd_scale{o}", tag=("x_raw0_0", "x_raw1_512")[o], align_bytes=64) for o in range(PASSES)]
+        x_second = keep.tile([P, PAIRS, HALF], U32, name="x_second")
+        listed_first = [keep.tile([P, CHUNK, PAIRS], U32, name=f"listed{c}", align_bytes=64) for c in range(2)]
         x_codes = keep.tile([P, N], U32, name="x_codes", align_bytes=64)
         x_scale = keep.tile([P, N], U8, name="x_scale", align_bytes=64)
         y_sb = [[keep.tile([P, LANES, HALF], F32, name=f"y_sb{h}{o}", tag=f"y_sb{h}{o}", align_bytes=64) for o in range(PASSES)] for h in range(2)]
@@ -76,7 +75,7 @@ def tile_attend_gml_sq_kernel(tc, xT, wd_words, wd_scales, wv_words, wv_scales, 
         weight = {(c, o): weight_early[c][:, :, o, :] for c in EARLY for o in range(PASSES)}
         a_scaled = {(c, o): keep.tile([P, LANES, CHUNK], F32, name=f"a_scaled{c}{o}") for c, o in TURNED}
         y_scaled = {(c, o): keep.tile([P, LANES, CHUNK], F32, name=f"y_scaled{c}{o}") for c, o in TURNED}
-        grad_early = relay.tile([P, 7 * V], BF16, name="grad_early", offset=0, align_bytes=64)
+        grad_early = keep.tile([P, V], BF16, name="grad_early", align_bytes=64)
         g_codes = keep.tile([P, PASSES * N], U32, name="g_codes", align_bytes=64)
         g_scale = keep.tile([P, PASSES * N], U8, name="g_scale", align_bytes=64)
         dx_turned = {c: keep.tile([P, D], F32, name=f"dx_turned{c}", tag=f"dx_turned{c}") for c in EARLY}
@@ -120,8 +119,8 @@ def tile_attend_gml_sq_kernel(tc, xT, wd_words, wd_scales, wv_words, wv_scales, 
             load_x(1, k)
         nc.sync.dma_start(rw_sb[:], rw.rearrange("p (c i) -> p c i", c=CHUNKS))
         load_wd(0)
-        load_y(0, 0)
         load_wd(1)
+        load_y(0, 0)
         load_y(0, 1)
         load_y(1, 0)
         nc.sync.dma_start(wv_codes[:], wv_words.rearrange("o p d t -> p o (d t)").bitcast(I32))
@@ -140,7 +139,7 @@ def tile_attend_gml_sq_kernel(tc, xT, wd_words, wd_scales, wv_words, wv_scales, 
             )
 
         def reorder_wd_scale(o):
-            (nc.gpsimd, nc.vector)[o].tensor_copy(
+            nc.gpsimd.tensor_copy(
                 wd_scale[o][:].rearrange("p (t m) -> p t m", t=LANES),
                 wd_raw_scale[:, o * K_PASS : (o + 1) * K_PASS].rearrange("p (m t) -> p t m", t=LANES),
             )
@@ -310,42 +309,42 @@ def tile_attend_gml_sq_kernel(tc, xT, wd_words, wd_scales, wv_words, wv_scales, 
         cast_x(1, 0, 0, 512, True)
         cast_x(1, 1, 512, 704, True)
         cast_x(1, 1, 704, 1024, False)
+        reorder_wd_scale(1)
         nc.scalar.mul(cw_neg[:], cw_sb[:], -1.0)
 
         for c in range(2):
             gather(x_first[:, 1, c * CHUNK : (c + 1) * CHUNK], 1, c, c + 1)
-        for c in range(2):
-            weave(listed_first[c], x_first[:, :, c * CHUNK : (c + 1) * CHUNK])
-        reorder_wd(0)
-        quantize_x(0, 1, listed_first[0])
-        a00 = product(0, 0, 0)
-        quantize_x(1, 2, listed_first[1])
-        a10 = product(1, 0, 2)
         gather(x_second[:, 1, :], 1, 2, 4)
-        reorder_wd_scale(1)
+        for c in range(2):
+            weave(listed_first[c][:], x_first[:, :, c * CHUNK : (c + 1) * CHUNK])
+        reorder_wd(0)
+        quantize_x(0, 1, listed_first[0][:])
+        a00 = product(0, 0, 0)
         reorder_wd(1)
         a01 = product(0, 1, 1)
+        quantize_x(1, 2, listed_first[1][:])
+        listed_second = keep.tile([P, HALF, PAIRS], U32, name="listed_second", tag="wd_raw1", align_bytes=64)
+        weave(listed_second[:], x_second[:], False)
+        a10 = product(1, 0, 2)
         a11 = product(1, 1, 3)
-        listed_second = front.tile([P, HALF, PAIRS], U32, name="listed_second", offset=4096, align_bytes=64)
-        res_first = front.tile([P, LANES, PASSES, CHUNK], F32, name="res_first", offset=0)
+        res_first = front.tile([P, 2 * LANES, PASSES, CHUNK], F32, name="res_first", offset=0)[:, 0:LANES, :, :]
         res = {(0, o): res_first[:, :, o, :] for o in range(PASSES)}
-        weave(listed_second[:], x_second, False)
         make_weight(0, 0)
         make_weight(0, 1)
         turn_rw(1, 7)
-        subtract_targets(0, 0, a00)
         quantize_x(2, 4, listed_second[:])
+        subtract_targets(0, 0, a00)
         a30 = product(3, 0, 4)
         a31 = product(3, 1, 5)
         a20 = product(2, 0, 6)
         a21 = product(2, 1, 7)
         subtract_targets(0, 1, a01)
-        weigh(grad_early[:, 0:V], res_first[:].rearrange("p t o i -> p t (o i)"), weight_early[0][:].rearrange("p t o i -> p t (o i)"), nc.vector, RUN)
+        weigh(grad_early[:, 0:V], res_first.rearrange("p t o i -> p t (o i)"), weight_early[0][:].rearrange("p t o i -> p t (o i)"), nc.vector, RUN)
         quantize_grad(g_cols(0, 0, 2), grad_early[:, 0:V])
         res[3, 0] = keep.tile([P, LANES, CHUNK], F32, name="res30")
         res[3, 1] = relay.tile([P, 4 * LANES, CHUNK], F32, name="res31", offset=2048)[:, 0:LANES, :]
         res[2, 1] = relay.tile([P, LANES, CHUNK], F32, name="res21", offset=10240)
-        res[2, 0] = relay.tile([P, LANES, CHUNK], F32, name="res20", offset=12288)
+        res[2, 0] = front.tile([P, LANES, CHUNK], F32, name="res20", offset=4096)
         for o in range(PASSES):
             scale_targets(1, o)
             scale_product(1, o, (a10, a11)[o])
@@ -368,7 +367,7 @@ def tile_attend_gml_sq_kernel(tc, xT, wd_words, wd_scales, wv_words, wv_scales, 
         quantize_grad(g_cols(3, 0, 2), grad_second[:])
         grad_turned = {
             (1, 0): keep.tile([P, K_PASS], BF16, name="grad_turned0"),
-            (1, 1): relay.tile([P, K_PASS], BF16, name="grad_turned1", offset=6144),
+            (1, 1): relay.tile([P, K_PASS], BF16, name="grad_turned1", offset=9216),
         }
         part_a = {0: relay.tile([P, CHUNK], F32, name="part_a0", offset=2048), 3: keep.tile([P, CHUNK], F32, name="part_a3")}
         fetch_early(0, 0, 1, e0a, part_a[0][:])
@@ -389,15 +388,15 @@ def tile_attend_gml_sq_kernel(tc, xT, wd_words, wd_scales, wv_words, wv_scales, 
         fetch_early(3, 0, 1, e1a, part_a[3][:])
         e1b = turn_early(3, 1, 4, 5)
         turn_back(1, 0, 1, grad_late[:, 0:K_PASS])
-        turn_back(1, 1, 4, grad_late[:, 2 * K_PASS : 3 * K_PASS])
-        part_b1 = relay.tile([P, 3 * CHUNK], F32, name="part_b1", offset=10240)
+        turn_back(1, 1, 0, grad_late[:, 2 * K_PASS : 3 * K_PASS])
+        part_b1 = relay.tile([P, 3 * CHUNK], F32, name="part_b1", offset=9728)
         fetch_early(3, 1, 4, e1b, part_b1[:])
         for j in range(1, D_TILES):
             scatter_early(0, j)
         scatter_early(3, 0)
         quantize_grad(slice(G_COLS[1, 0] * CHUNK, (G_COLS[2, 1] + 1) * CHUNK), grad_late[:])
         for j in range(D_TILES):
-            back_rest(j, (6, 7, 3, 0)[j], (1, 0))
+            back_rest(j, (6, 7, 4, 2)[j], (1, 0))
         for j in range(1, D_TILES):
             scatter_early(3, j)
         for j in range(D_TILES):

@@ -111,7 +111,7 @@ def tile_attend_gml_sq_kernel(tc, xT, wd_words, wd_scales, wv_words, wv_scales, 
             )
 
         nc.sync.dma_start(offsets[:], offs)
-        nc.scalar.dma_start(cw_sb[:], cw.rearrange("(o p t) one -> p o (t one)", o=PASSES, t=LANES))
+        nc.sync.dma_start(cw_sb[:], cw.rearrange("(o p t) one -> p o (t one)", o=PASSES, t=LANES))
         load_x(0, 0)
         for q in range(QUADRANTS):
             load_wd_scales(nc.scalar, q)

@@ -320,11 +320,11 @@ def tile_attend_gml_sq_kernel(tc, xT, wd_words, wd_scales, wv_words, wv_scales, 
         reorder_wd(0)
         quantize_x(0, 1, listed_first[0][:])
         a00 = product(0, 0, 0)
+        listed_second = keep.tile([P, HALF, PAIRS], U32, name="listed_second", tag="wd_raw0", align_bytes=64)
+        weave(listed_second[:], x_second[:], False)
         reorder_wd(1)
         a01 = product(0, 1, 1)
         quantize_x(1, 2, listed_first[1][:])
-        listed_second = keep.tile([P, HALF, PAIRS], U32, name="listed_second", tag="wd_raw1", align_bytes=64)
-        weave(listed_second[:], x_second[:], False)
         a10 = product(1, 0, 2)
         a11 = product(1, 1, 3)
         res_first = front.tile([P, 2 * LANES, PASSES, CHUNK], F32, name="res_first", offset=0)[:, 0:LANES, :, :]

@@ -386,9 +386,9 @@ def tile_attend_gml_sq_kernel(tc, xT, wd_words, wd_scales, wv_words, wv_scales, 
         copy_early(3, 1, 4, t1)
         e1a = turn_early(3, 0, 1, 2)
         fetch_early(3, 0, 1, e1a, part_a[3][:])
-        e1b = turn_early(3, 1, 4, 5)
         turn_back(1, 0, 1, grad_late[:, 0:K_PASS])
         turn_back(1, 1, 0, grad_late[:, 2 * K_PASS : 3 * K_PASS])
+        e1b = turn_early(3, 1, 4, 5)
         part_b1 = relay.tile([P, 3 * CHUNK], F32, name="part_b1", offset=9728)
         fetch_early(3, 1, 4, e1b, part_b1[:])
         for j in range(1, D_TILES):

@@ -111,10 +111,10 @@ def tile_attend_gml_sq_kernel(tc, xT, wd_words, wd_scales, wv_words, wv_scales, 
             )
 
         nc.sync.dma_start(offsets[:], offs)
-        nc.sync.dma_start(cw_sb[:], cw.rearrange("(o p t) one -> p o (t one)", o=PASSES, t=LANES))
         load_x(0, 0)
+        nc.sync.dma_start(cw_sb[:], cw.rearrange("(o p t) one -> p o (t one)", o=PASSES, t=LANES))
         for q in range(QUADRANTS):
-            load_wd_scales(nc.scalar, q)
+            load_wd_scales(nc.sync, q)
         for k in range(len(X_PIECES[1])):
             load_x(1, k)
         nc.sync.dma_start(rw_sb[:], rw.rearrange("p (c i) -> p c i", c=CHUNKS))

@@ -30,7 +30,7 @@ CHUNKS = N // CHUNK
 HALF = N // 2
 LIST_COLS = CHUNK // 16
 RUN = 2
-X_PIECES = (((0, 1024),), ((0, 512), (512, 1024)))
+X_PIECES = (((0, 512), (512, 1024)), ((0, 512), (512, 1024)))
 EARLY = (0, 3)
 LATE = (1, 2)
 TURNED = ((1, 0), (1, 1))
@@ -47,6 +47,11 @@ def tile_attend_gml_sq_kernel(tc, xT, wd_words, wd_scales, wv_words, wv_scales, 
         keep = ctx.enter_context(tc.tile_pool(name="keep", bufs=1))
         relay = ctx.enter_context(tc.tile_pool(name="relay", bufs=1))
         front = ctx.enter_context(tc.tile_pool(name="front", bufs=1))
+        mid = ctx.enter_context(tc.tile_pool(name="mid", bufs=1))
+        neg = ctx.enter_context(tc.tile_pool(name="neg", bufs=1))
+        ys = ctx.enter_context(tc.tile_pool(name="ys", bufs=1))
+        dts = ctx.enter_context(tc.tile_pool(name="dts", bufs=1))
+        grads = ctx.enter_context(tc.tile_pool(name="grads", bufs=1))
         psum = ctx.enter_context(tc.psum_pool(name="psum", bufs=1))
 
         def bank(b, shape, name):
@@ -58,27 +63,30 @@ def tile_attend_gml_sq_kernel(tc, xT, wd_words, wd_scales, wv_words, wv_scales, 
         wd_codes = [keep.tile([P, K_PASS], I32, name=f"wd_codes{o}", align_bytes=64) for o in range(PASSES)]
         wv_codes = keep.tile([P, PASSES, D], I32, name="wv_codes", align_bytes=64)
         wv_scale = keep.tile([P, PASSES, D], U8, name="wv_scale", align_bytes=64)
-        cw_sb = keep.tile([P, PASSES, LANES], F32, name="cw_sb")
-        cw_neg = keep.tile([P, PASSES, LANES], F32, name="cw_neg")
-        rw_sb = keep.tile([P, CHUNKS, CHUNK], F32, name="rw_sb")
+        cw_sb = keep.tile([P, PASSES, 2 * LANES], F32, name="cw_sb")[:, :, 0:LANES]
+        cw_neg = [neg.tile([P, LANES], F32, name="cw_neg0", offset=0, align_bytes=64), ys.tile([P, LANES], F32, name="cw_neg1", offset=0)]
+        rw_head = keep.tile([P, 2, CHUNK], F32, name="rw_head")
+        rw_mid = keep.tile([P, 2, CHUNK], F32, name="rw_mid")
         x_raw = [[keep.tile([P, 2, b - a], F32, name=f"x_raw{u}_{a}", tag=f"x_raw{u}_{a}", align_bytes=64) for a, b in X_PIECES[u]] for u in range(PAIRS)]
         rw_col = keep.tile([P, 1], F32, name="rw_col")
         x_pairs = [keep.tile([P, T], U32, name=f"x_pairs{u}") for u in range(PAIRS)]
-        x_first = keep.tile([P, PAIRS, HALF], U32, name="x_first", tag="x_first", align_bytes=64)
-        wd_scale = [keep.tile([P, K_PASS], U8, name=f"wd_scale{o}", tag=("x_raw0_0", "x_raw1_512")[o], align_bytes=64) for o in range(PASSES)]
-        x_second = keep.tile([P, PAIRS, HALF], U32, name="x_second")
-        listed_first = [keep.tile([P, CHUNK, PAIRS], U32, name=f"listed{c}", align_bytes=64) for c in range(2)]
+        stage = mid.tile([P, 4 * HALF], U32, name="stage", offset=2048, align_bytes=64)
+        x_first = stage[:, 2 * CHUNK : 4 * CHUNK].rearrange("p (u i) -> p u i", u=PAIRS)
+        wd_scale = [keep.tile([P, K_PASS], U8, name=f"wd_scale{o}", tag=("x_raw0_512", "wd_raw1")[o], align_bytes=64) for o in range(PASSES)]
+        x_second = stage[:].rearrange("p (u i) -> p u i", u=PAIRS)[:, :, 0:HALF]
+        listed_first = [stage[:, 3 * CHUNK : 5 * CHUNK].rearrange("p (i u) -> p i u", u=PAIRS), keep.tile([P, CHUNK, PAIRS], U32, name="listed1", align_bytes=64)]
         x_codes = keep.tile([P, N], U32, name="x_codes", align_bytes=64)
         x_scale = keep.tile([P, N], U8, name="x_scale", align_bytes=64)
         y_sb = [[keep.tile([P, LANES, HALF], F32, name=f"y_sb{h}{o}", tag=f"y_sb{h}{o}", align_bytes=64) for o in range(PASSES)] for h in range(2)]
-        weight_early = {c: keep.tile([P, LANES, PASSES, CHUNK], F32, name=f"weight{c}") for c in EARLY}
-        weight = {(c, o): weight_early[c][:, :, o, :] for c in EARLY for o in range(PASSES)}
-        a_scaled = {(c, o): keep.tile([P, LANES, CHUNK], F32, name=f"a_scaled{c}{o}") for c, o in TURNED}
-        y_scaled = {(c, o): keep.tile([P, LANES, CHUNK], F32, name=f"y_scaled{c}{o}") for c, o in TURNED}
-        grad_early = keep.tile([P, V], BF16, name="grad_early", align_bytes=64)
+        weight_first = keep.tile([P, LANES, PASSES, CHUNK], F32, name="weight_first")
+        weight = {(0, o): weight_first[:, :, o, :] for o in range(PASSES)}
+        weight_second = keep.tile([P, PASSES, K_PASS], F32, name="weight_second")
+        a_scaled = {(1, o): mid.tile([P, LANES, CHUNK], F32, name=f"a_scaled{o}", offset=1024 + 4096 * o) for o in range(PASSES)}
+        y_scaled = {(1, 0): keep.tile([P, LANES, CHUNK], F32, name="y_scaled0"), (1, 1): keep.tile([P, LANES, CHUNK], F32, name="y_scaled1")}
+        grad_early = front.tile([P, V], BF16, name="grad_early", offset=1024, align_bytes=64)
         g_codes = keep.tile([P, PASSES * N], U32, name="g_codes", align_bytes=64)
         g_scale = keep.tile([P, PASSES * N], U8, name="g_scale", align_bytes=64)
-        dx_turned = {c: keep.tile([P, D], F32, name=f"dx_turned{c}", tag=f"dx_turned{c}") for c in EARLY}
+        dx_turned = {0: dts.tile([P, D], F32, name="dx_turned0", offset=0), 3: keep.tile([P, D], F32, name="dx_turned3")}
         dx_early = {}
         dx_rest = [keep.tile([P, len(LATE) * CHUNK], F32, name=f"dx_rest{j}") for j in range(D_TILES)]
         windows = [keep.tile([P, T], F32, name=f"window{j}") for j in range(D_TILES)]
@@ -111,26 +119,30 @@ def tile_attend_gml_sq_kernel(tc, xT, wd_words, wd_scales, wv_words, wv_scales, 
             )
 
         nc.sync.dma_start(offsets[:], offs)
+        rw_chunks = rw.rearrange("p (c i) -> p c i", c=CHUNKS)
+        nc.sync.dma_start(cw_sb, cw.rearrange("(o p t) one -> p o (t one)", o=PASSES, t=LANES))
+        nc.sync.dma_start(rw_head[:], rw_chunks[:, 0:CHUNKS:3, :])
         load_x(0, 0)
-        nc.sync.dma_start(cw_sb[:], cw.rearrange("(o p t) one -> p o (t one)", o=PASSES, t=LANES))
+        load_x(0, 1)
         for q in range(QUADRANTS):
             load_wd_scales(nc.sync, q)
         for k in range(len(X_PIECES[1])):
             load_x(1, k)
-        nc.sync.dma_start(rw_sb[:], rw.rearrange("p (c i) -> p c i", c=CHUNKS))
         load_wd(0)
         load_wd(1)
         load_y(0, 0)
         load_y(0, 1)
+        nc.sync.dma_start(rw_mid[:], rw_chunks[:, 1:3, :])
         load_y(1, 0)
-        nc.sync.dma_start(wv_codes[:], wv_words.rearrange("o p d t -> p o (d t)").bitcast(I32))
         for q in range(QUADRANTS):
             load_wv_scales(nc.sync, q)
+        nc.sync.dma_start(wv_codes[:], wv_words.rearrange("o p d t -> p o (d t)").bitcast(I32))
         load_y(1, 1)
 
         make_identity(nc, ident[:])
-        for j in range(D_TILES):
+        for j in range(D_TILES - 1):
             nc.vector.memset(windows[j][:].bitcast(I32), 0)
+        nc.gpsimd.memset(windows[D_TILES - 1][:].bitcast(I32), 0)
 
         def reorder_wd(o):
             nc.vector.tensor_copy(
@@ -153,13 +165,22 @@ def tile_attend_gml_sq_kernel(tc, xT, wd_words, wd_scales, wv_words, wv_scales, 
             else:
                 nc.vector.tensor_copy(dst, src)
 
-        def make_weight(c, o):
+        def make_weight(c, o, src):
             for t in range(LANES):
-                nc.scalar.activation(weight[c, o][:, t, :], rw_sb[:, c, :], COPY, scale=cw_sb[:, o, t : t + 1])
+                nc.scalar.activation(weight[c, o][:, t, :], src, COPY, scale=cw_sb[:, o, t : t + 1])
+
+        def make_weight_woven(o, src):
+            shape = [P, CHUNK, LANES]
+            nc.vector.tensor_tensor(
+                weight_second[:, o, :].rearrange("p (i t) -> p i t", t=LANES),
+                src.unsqueeze(2).broadcast_to(shape),
+                cw_sb[:, o, :].unsqueeze(1).broadcast_to(shape),
+                MULT,
+            )
 
         def turn_rw(c, b):
             col_bank = bank(b, [P, P], "col_bank")
-            nc.tensor.transpose(col_bank[:], rw_sb[:, c, :], ident[:])
+            nc.tensor.transpose(col_bank[:], rw_mid[:, c - 1, :], ident[:])
             nc.scalar.copy(rw_col[:], col_bank[:, 0:1])
 
         def gather(dst, u, c0, c1):
@@ -204,6 +225,14 @@ def tile_attend_gml_sq_kernel(tc, xT, wd_words, wd_scales, wv_words, wv_scales, 
         def subtract_targets(c, o, a_bank):
             nc.vector.tensor_tensor(residual(c, c + 1, o), a_bank[:], y_of(c, o), SUB)
 
+        def subtract_woven(c, o, a_bank):
+            nc.vector.tensor_tensor(
+                res[c, o][:].rearrange("p (r i t) -> p r t i", i=SIDE_RUN, t=LANES),
+                a_bank[:].rearrange("p t (r i) -> p r t i", i=SIDE_RUN),
+                y_of(c, o).rearrange("p t (r i) -> p r t i", i=SIDE_RUN),
+                SUB,
+            )
+
         def weigh(dst, residuals, weights, engine, run):
             engine.tensor_tensor(
                 dst.rearrange("p (r i t) -> p r t i", i=run, t=LANES),
@@ -213,11 +242,16 @@ def tile_attend_gml_sq_kernel(tc, xT, wd_words, wd_scales, wv_words, wv_scales, 
             )
 
         def weigh_side(c, o, dst):
-            weigh(dst, res[c, o][:], weight[c, o], nc.gpsimd, SIDE_RUN)
+            nc.gpsimd.tensor_tensor(
+                dst.rearrange("p (i t) -> p i t", t=LANES),
+                res[c, o][:].rearrange("p (i t) -> p i t", t=LANES),
+                weight[c, o].rearrange("p t i -> p i t"),
+                MULT,
+            )
 
         def scale_targets(c, o):
             for t in range(LANES):
-                nc.scalar.activation(y_scaled[c, o][:, t, :], y_of(c, o)[:, t, :], COPY, scale=cw_neg[:, o, t : t + 1])
+                nc.scalar.activation(y_scaled[c, o][:, t, :], y_of(c, o)[:, t, :], COPY, scale=cw_neg[o][:, t : t + 1])
 
         def scale_product(c, o, a_bank):
             for t in range(LANES):
@@ -301,102 +335,108 @@ def tile_attend_gml_sq_kernel(tc, xT, wd_words, wd_scales, wv_words, wv_scales, 
             nc.vector.tensor_copy(windows[j][:].indirect(offsets[:, LATE[0] * LIST_COLS : (LATE[-1] + 1) * LIST_COLS]), dx_rest[j][:])
             nc.sync.dma_start(out[j * P : (j + 1) * P, :], windows[j][:])
 
-        cast_x(0, 0, 0, 320, True)
-        cast_x(0, 0, 320, 1024, False)
+        for o in range(PASSES):
+            nc.scalar.mul(cw_neg[o][:], cw_sb[:, o, :], -1.0)
+        for o in range(PASSES):
+            make_weight(0, o, rw_head[:, 0, :])
+        for o in range(PASSES):
+            make_weight_woven(o, rw_head[:, 1, :])
+        cast_x(0, 0, 0, 512, True)
+        cast_x(0, 1, 512, 640, True)
+        cast_x(0, 1, 640, 1024, False)
         reorder_wd_scale(0)
-        gather(x_first[:, 0, :], 0, 0, 2)
+        gather(listed_first[0][:, :, 0], 0, 0, 1)
+        gather(x_first[:, 0, :], 0, 1, 2)
         gather(x_second[:, 0, :], 0, 2, 4)
         cast_x(1, 0, 0, 512, True)
         cast_x(1, 1, 512, 704, True)
         cast_x(1, 1, 704, 1024, False)
-        reorder_wd_scale(1)
-        nc.scalar.mul(cw_neg[:], cw_sb[:], -1.0)
 
-        for c in range(2):
-            gather(x_first[:, 1, c * CHUNK : (c + 1) * CHUNK], 1, c, c + 1)
-        gather(x_second[:, 1, :], 1, 2, 4)
-        for c in range(2):
-            weave(listed_first[c][:], x_first[:, :, c * CHUNK : (c + 1) * CHUNK])
+        gather(listed_first[0][:, :, 1], 1, 0, 1)
         reorder_wd(0)
-        quantize_x(0, 1, listed_first[0][:])
+        quantize_x(0, 1, listed_first[0])
         a00 = product(0, 0, 0)
-        listed_second = keep.tile([P, HALF, PAIRS], U32, name="listed_second", tag="wd_raw0", align_bytes=64)
-        weave(listed_second[:], x_second[:], False)
         reorder_wd(1)
+        reorder_wd_scale(1)
         a01 = product(0, 1, 1)
+        gather(x_first[:, 1, :], 1, 1, 2)
+        weave(listed_first[1][:], x_first)
+        gather(x_second[:, 1, :], 1, 2, 4)
         quantize_x(1, 2, listed_first[1][:])
         a10 = product(1, 0, 2)
         a11 = product(1, 1, 3)
-        res_first = front.tile([P, 2 * LANES, PASSES, CHUNK], F32, name="res_first", offset=0)[:, 0:LANES, :, :]
+        res_first = keep.tile([P, LANES, PASSES, CHUNK], F32, name="res_first")
         res = {(0, o): res_first[:, :, o, :] for o in range(PASSES)}
-        make_weight(0, 0)
-        make_weight(0, 1)
-        turn_rw(1, 7)
-        quantize_x(2, 4, listed_second[:])
+        scale_targets(1, 0)
+        listed_second = neg.tile([P, HALF, PAIRS], U32, name="listed_second", offset=0, align_bytes=64)
+        weave(listed_second[:], x_second)
         subtract_targets(0, 0, a00)
-        a30 = product(3, 0, 4)
-        a31 = product(3, 1, 5)
-        a20 = product(2, 0, 6)
-        a21 = product(2, 1, 7)
         subtract_targets(0, 1, a01)
-        weigh(grad_early[:, 0:V], res_first.rearrange("p t o i -> p t (o i)"), weight_early[0][:].rearrange("p t o i -> p t (o i)"), nc.vector, RUN)
+        quantize_x(2, 4, listed_second[:])
+        turn_rw(1, 7)
+        a30 = product(3, 0, 4)
+        a20 = product(2, 0, 5)
+        a31 = product(3, 1, 6)
+        a21 = product(2, 1, 7)
+        scale_product(1, 0, a10)
+        scale_targets(1, 1)
+        scale_product(1, 1, a11)
+        weigh(grad_early[:, 0:V], res_first[:].rearrange("p t o i -> p t (o i)"), weight_first[:].rearrange("p t o i -> p t (o i)"), nc.vector, RUN)
         quantize_grad(g_cols(0, 0, 2), grad_early[:, 0:V])
-        res[3, 0] = keep.tile([P, LANES, CHUNK], F32, name="res30")
-        res[3, 1] = relay.tile([P, 4 * LANES, CHUNK], F32, name="res31", offset=2048)[:, 0:LANES, :]
-        res[2, 1] = relay.tile([P, LANES, CHUNK], F32, name="res21", offset=10240)
-        res[2, 0] = front.tile([P, LANES, CHUNK], F32, name="res20", offset=4096)
-        for o in range(PASSES):
-            scale_targets(1, o)
-            scale_product(1, o, (a10, a11)[o])
-        make_weight(3, 0)
-        make_weight(3, 1)
-        weight[2, 0] = keep.tile([P, LANES, CHUNK], F32, name="weight20")[:]
-        make_weight(2, 0)
-        grad_second = front.tile([P, V], BF16, name="grad_second", offset=0, align_bytes=64)
+        res[3, 0] = front.tile([P, K_PASS], F32, name="res30", offset=0)
+        res[2, 0] = front.tile([P, K_PASS], F32, name="res20", offset=2048)
+        res[3, 1] = relay.tile([P, K_PASS], F32, name="res31", offset=2048)
+        res[2, 1] = relay.tile([P, K_PASS], F32, name="res21", offset=6144)
+        rw_third = rw_mid[:, 1, :]
+        weight[2, 0] = ys.tile([P, LANES, CHUNK], F32, name="weight20", offset=0)[:]
+        make_weight(2, 0, rw_third)
+        grad_second = grads.tile([P, V], BF16, name="grad_second", offset=0, align_bytes=64)
         t0 = back_early(0, 0)
         copy_early(0, 0, 1, t0)
         copy_early(0, 1, 4, t0)
         e0a = turn_early(0, 0, 1, 1)
-        subtract_targets(3, 0, a30)
-        weigh_side(3, 0, grad_second[:, 0:K_PASS])
-        subtract_targets(3, 1, a31)
-        e0b = turn_early(0, 1, 4, 4)
-        subtract_targets(2, 0, a20)
-        subtract_targets(2, 1, a21)
-        weigh(grad_second[:, K_PASS:V], res[3, 1], weight[3, 1], nc.vector, RUN)
-        quantize_grad(g_cols(3, 0, 2), grad_second[:])
-        grad_turned = {
-            (1, 0): keep.tile([P, K_PASS], BF16, name="grad_turned0"),
-            (1, 1): relay.tile([P, K_PASS], BF16, name="grad_turned1", offset=9216),
-        }
-        part_a = {0: relay.tile([P, CHUNK], F32, name="part_a0", offset=2048), 3: keep.tile([P, CHUNK], F32, name="part_a3")}
+        subtract_woven(3, 0, a30)
+        nc.gpsimd.tensor_tensor(grad_second[:, 0:K_PASS], res[3, 0][:], weight_second[:, 0, :], MULT)
+        subtract_woven(2, 0, a20)
+        subtract_woven(3, 1, a31)
+        nc.gpsimd.tensor_tensor(grad_second[:, K_PASS:V], res[3, 1][:], weight_second[:, 1, :], MULT)
+        subtract_woven(2, 1, a21)
+        part_a = {c: keep.tile([P, CHUNK], F32, name=f"part_a{c}") for c in EARLY}
         fetch_early(0, 0, 1, e0a, part_a[0][:])
-        part_b0 = relay.tile([P, 3 * CHUNK], F32, name="part_b0", offset=2560)
-        fetch_early(0, 1, 4, e0b, part_b0[:])
-        turn_and_weigh(1, 0, 2)
-        turn_and_weigh(1, 1, 3)
-        weight[2, 1] = relay.tile([P, LANES, CHUNK], F32, name="weight21", offset=4096)[:]
-        make_weight(2, 1)
+        e0b = turn_early(0, 1, 4, 4)
+        weight[2, 1] = dts.tile([P, LANES, CHUNK], F32, name="weight21", offset=0)[:]
+        make_weight(2, 1, rw_third)
         scatter_early(0, 0)
-        grad_late = front.tile([P, 4 * K_PASS], BF16, name="grad_late", offset=0, align_bytes=64)
+        quantize_grad(g_cols(3, 0, 2), grad_second[:])
+        part_b0 = relay.tile([P, CHUNK], F32, name="part_b0", offset=2112)
+        part_c0 = relay.tile([P, 2 * CHUNK], F32, name="part_c0", offset=2624)
+        nc.scalar.copy(part_b0[:], e0b[:, 0, :])
+        nc.scalar.copy(part_c0[:], e0b[:, 1:3, :].rearrange("p j i -> p (j i)"))
+        dx_early[0, 1] = part_b0[:]
+        dx_early[0, 2] = part_c0[:, 0:CHUNK]
+        dx_early[0, 3] = part_c0[:, CHUNK : 2 * CHUNK]
+        grad_turned = {(1, o): relay.tile([P, K_PASS], BF16, name=f"grad_turned{o}", offset=(1088, 3648)[o]) for o in range(PASSES)}
+        turn_and_weigh(1, 0, 0)
+        turn_and_weigh(1, 1, 1)
+        grad_late = grads.tile([P, 4 * K_PASS], BF16, name="grad_late", offset=0, align_bytes=64)
         weigh_side(2, 0, grad_late[:, K_PASS : 2 * K_PASS])
         weigh_side(2, 1, grad_late[:, 3 * K_PASS : 4 * K_PASS])
-        t1 = back_early(3, 0)
+        t1 = back_early(3, 3)
         copy_early(3, 0, 1, t1)
         copy_early(3, 1, 4, t1)
         e1a = turn_early(3, 0, 1, 2)
         fetch_early(3, 0, 1, e1a, part_a[3][:])
-        turn_back(1, 0, 1, grad_late[:, 0:K_PASS])
-        turn_back(1, 1, 0, grad_late[:, 2 * K_PASS : 3 * K_PASS])
+        turn_back(1, 1, 3, grad_late[:, 2 * K_PASS : 3 * K_PASS])
+        turn_back(1, 0, 2, grad_late[:, 0:K_PASS])
         e1b = turn_early(3, 1, 4, 5)
-        part_b1 = relay.tile([P, 3 * CHUNK], F32, name="part_b1", offset=9728)
+        part_b1 = relay.tile([P, 3 * CHUNK], F32, name="part_b1", offset=6144)
         fetch_early(3, 1, 4, e1b, part_b1[:])
         for j in range(1, D_TILES):
             scatter_early(0, j)
         scatter_early(3, 0)
         quantize_grad(slice(G_COLS[1, 0] * CHUNK, (G_COLS[2, 1] + 1) * CHUNK), grad_late[:])
         for j in range(D_TILES):
-            back_rest(j, (6, 7, 4, 2)[j], (1, 0))
+            back_rest(j, (6, 7, 4, 0)[j], (1, 0))
         for j in range(1, D_TILES):
             scatter_early(3, j)
         for j in range(D_TILES):

@@ -59,31 +59,37 @@ def tile_attend_gml_sq_kernel(tc, xT, wd_words, wd_scales, wv_words, wv_scales, 
 
         offsets = keep.tile([P, N // 16], U16, name="offsets")
         wd_raw = [keep.tile([P, K_PASS], I32, name=f"wd_raw{o}", tag=f"wd_raw{o}", align_bytes=64) for o in range(PASSES)]
-        wd_raw_scale = keep.tile([P, V], U8, name="wd_raw_scale", align_bytes=64)
-        wd_codes = [keep.tile([P, K_PASS], I32, name=f"wd_codes{o}", align_bytes=64) for o in range(PASSES)]
+        wd_raw_scale = keep.tile([P, K_PASS], U8, name="wd_raw_scale", align_bytes=64)
+        wd_codes = [keep.tile([P, K_PASS], I32, name="wd_codes0", align_bytes=64)]
         wv_codes = keep.tile([P, PASSES, D], I32, name="wv_codes", align_bytes=64)
         wv_scale = keep.tile([P, PASSES, D], U8, name="wv_scale", align_bytes=64)
         cw_sb = keep.tile([P, PASSES, 2 * LANES], F32, name="cw_sb")[:, :, 0:LANES]
-        cw_neg = [neg.tile([P, LANES], F32, name="cw_neg0", offset=0, align_bytes=64), ys.tile([P, LANES], F32, name="cw_neg1", offset=0)]
+        cw_neg = [
+            neg.tile([P, LANES], F32, name="cw_neg0", offset=0, align_bytes=64),
+            front.tile([P, PAIRS], F32, name="cw_neg1", offset=1536),
+            ys.tile([P, PAIRS], F32, name="cw_neg2", offset=0),
+        ]
+        neg_col = {(0, t): cw_neg[0][:, t : t + 1] for t in range(LANES)}
+        for t in range(LANES):
+            neg_col[1, t] = cw_neg[1 + t // 2][:, t % 2 : t % 2 + 1]
         rw_head = keep.tile([P, 2, CHUNK], F32, name="rw_head")
         rw_mid = keep.tile([P, 2, CHUNK], F32, name="rw_mid")
         x_raw = [[keep.tile([P, 2, b - a], F32, name=f"x_raw{u}_{a}", tag=f"x_raw{u}_{a}", align_bytes=64) for a, b in X_PIECES[u]] for u in range(PAIRS)]
         rw_col = keep.tile([P, 1], F32, name="rw_col")
         x_pairs = [keep.tile([P, T], U32, name=f"x_pairs{u}") for u in range(PAIRS)]
-        stage = mid.tile([P, 4 * HALF], U32, name="stage", offset=2048, align_bytes=64)
-        x_first = stage[:, 2 * CHUNK : 4 * CHUNK].rearrange("p (u i) -> p u i", u=PAIRS)
-        wd_scale = [keep.tile([P, K_PASS], U8, name=f"wd_scale{o}", tag=("x_raw0_512", "wd_raw1")[o], align_bytes=64) for o in range(PASSES)]
-        x_second = stage[:].rearrange("p (u i) -> p u i", u=PAIRS)[:, :, 0:HALF]
-        listed_first = [stage[:, 3 * CHUNK : 5 * CHUNK].rearrange("p (i u) -> p i u", u=PAIRS), keep.tile([P, CHUNK, PAIRS], U32, name="listed1", align_bytes=64)]
+        stage = mid.tile([P, 2 * HALF], U32, name="stage", offset=2048, align_bytes=64)
+        x_first = [keep.tile([P, PAIRS, CHUNK], U32, name=f"x_first{c}", tag=f"x_first{c}", align_bytes=64) for c in range(2)]
+        wd_scale = keep.tile([P, K_PASS], U8, name="wd_scale", tag="x_raw0_512", align_bytes=64)
+        x_second = stage[:].rearrange("p (u i) -> p u i", u=PAIRS)
+        listed_first = [stage[:, HALF:].rearrange("p (i u) -> p i u", u=PAIRS), keep.tile([P, CHUNK, PAIRS], U32, name="listed1", align_bytes=64)]
         x_codes = keep.tile([P, N], U32, name="x_codes", align_bytes=64)
         x_scale = keep.tile([P, N], U8, name="x_scale", align_bytes=64)
         y_sb = [[keep.tile([P, LANES, HALF], F32, name=f"y_sb{h}{o}", tag=f"y_sb{h}{o}", align_bytes=64) for o in range(PASSES)] for h in range(2)]
         weight_first = keep.tile([P, LANES, PASSES, CHUNK], F32, name="weight_first")
         weight = {(0, o): weight_first[:, :, o, :] for o in range(PASSES)}
         weight_second = keep.tile([P, PASSES, K_PASS], F32, name="weight_second")
-        a_scaled = {(1, o): mid.tile([P, LANES, CHUNK], F32, name=f"a_scaled{o}", offset=1024 + 4096 * o) for o in range(PASSES)}
+        a_scaled = {(1, o): mid.tile([P, LANES, CHUNK], F32, name=f"a_scaled{o}", offset=1024 + 2048 * o) for o in range(PASSES)}
         y_scaled = {(1, 0): keep.tile([P, LANES, CHUNK], F32, name="y_scaled0"), (1, 1): keep.tile([P, LANES, CHUNK], F32, name="y_scaled1")}
-        grad_early = front.tile([P, V], BF16, name="grad_early", offset=1024, align_bytes=64)
         g_codes = keep.tile([P, PASSES * N], U32, name="g_codes", align_bytes=64)
         g_scale = keep.tile([P, PASSES * N], U8, name="g_scale", align_bytes=64)
         dx_turned = {0: dts.tile([P, D], F32, name="dx_turned0", offset=0), 3: keep.tile([P, D], F32, name="dx_turned3")}
@@ -110,7 +116,10 @@ def tile_attend_gml_sq_kernel(tc, xT, wd_words, wd_scales, wv_words, wv_scales, 
             queue.dma_start(y_sb[h][o][:], y_rows[o][:, :, h * HALF : (h + 1) * HALF])
 
         def load_wd_scales(queue, q):
-            queue.dma_start(wd_raw_scale[32 * q : 32 * q + 4, :].bitcast(I32), wd_scales[0, 4 * q : 4 * q + 4, :].bitcast(I32))
+            queue.dma_start(
+                wd_raw_scale[32 * q : 32 * q + 4 * PASSES, :].bitcast(I32),
+                wd_scales[0, 4 * q : 4 * q + 4, :].bitcast(I32).rearrange("f (o c) -> o f c", o=PASSES),
+            )
 
         def load_wv_scales(queue, q):
             queue.dma_start(
@@ -150,10 +159,10 @@ def tile_attend_gml_sq_kernel(tc, xT, wd_words, wd_scales, wv_words, wv_scales, 
                 wd_raw[o][:].rearrange("p (m t) -> p m t", t=LANES),
             )
 
-        def reorder_wd_scale(o):
+        def reorder_wd_scale():
             nc.gpsimd.tensor_copy(
-                wd_scale[o][:].rearrange("p (t m) -> p t m", t=LANES),
-                wd_raw_scale[:, o * K_PASS : (o + 1) * K_PASS].rearrange("p (m t) -> p t m", t=LANES),
+                wd_scale[:].rearrange("p (t m) -> p t m", t=LANES),
+                wd_raw_scale[:].rearrange("p (m t) -> p t m", t=LANES),
             )
 
         def cast_x(u, k, a, b, on_scalar):
@@ -207,7 +216,7 @@ def tile_attend_gml_sq_kernel(tc, xT, wd_words, wd_scales, wv_words, wv_scales, 
                 nc.tensor.matmul_mx(
                     out=a_bank[:, t, :],
                     lhsT=wd_codes[o][:, t * P : (t + 1) * P].bitcast(E4M3),
-                    lhsT_scale=wd_scale[o][:, t * P : (t + 1) * P],
+                    lhsT_scale=wd_scale[4 * o : P, t * P : (t + 1) * P],
                     rhs=x_codes[:, cols].bitcast(E4M3),
                     rhs_scale=x_scale[:, cols],
                     start=True,
@@ -242,16 +251,11 @@ def tile_attend_gml_sq_kernel(tc, xT, wd_words, wd_scales, wv_words, wv_scales, 
             )
 
         def weigh_side(c, o, dst):
-            nc.gpsimd.tensor_tensor(
-                dst.rearrange("p (i t) -> p i t", t=LANES),
-                res[c, o][:].rearrange("p (i t) -> p i t", t=LANES),
-                weight[c, o].rearrange("p t i -> p i t"),
-                MULT,
-            )
+            weigh(dst, res[c, o][:], weight[c, o], nc.gpsimd, SIDE_RUN)
 
         def scale_targets(c, o):
             for t in range(LANES):
-                nc.scalar.activation(y_scaled[c, o][:, t, :], y_of(c, o)[:, t, :], COPY, scale=cw_neg[o][:, t : t + 1])
+                nc.scalar.activation(y_scaled[c, o][:, t, :], y_of(c, o)[:, t, :], COPY, scale=neg_col[o, t])
 
         def scale_product(c, o, a_bank):
             for t in range(LANES):
@@ -335,32 +339,34 @@ def tile_attend_gml_sq_kernel(tc, xT, wd_words, wd_scales, wv_words, wv_scales, 
             nc.vector.tensor_copy(windows[j][:].indirect(offsets[:, LATE[0] * LIST_COLS : (LATE[-1] + 1) * LIST_COLS]), dx_rest[j][:])
             nc.sync.dma_start(out[j * P : (j + 1) * P, :], windows[j][:])
 
-        for o in range(PASSES):
-            nc.scalar.mul(cw_neg[o][:], cw_sb[:, o, :], -1.0)
+        nc.scalar.mul(cw_neg[0][:], cw_sb[:, 0, :], -1.0)
+        for u in range(PAIRS):
+            nc.scalar.mul(cw_neg[1 + u][:], cw_sb[:, 1, 2 * u : 2 * u + 2], -1.0)
         for o in range(PASSES):
             make_weight(0, o, rw_head[:, 0, :])
         for o in range(PASSES):
             make_weight_woven(o, rw_head[:, 1, :])
-        cast_x(0, 0, 0, 512, True)
-        cast_x(0, 1, 512, 640, True)
-        cast_x(0, 1, 640, 1024, False)
-        reorder_wd_scale(0)
-        gather(listed_first[0][:, :, 0], 0, 0, 1)
-        gather(x_first[:, 0, :], 0, 1, 2)
+        cast_x(0, 0, 0, 512, False)
+        cast_x(0, 1, 512, 704, True)
+        cast_x(0, 1, 704, 1024, False)
+        reorder_wd_scale()
+        for c in range(2):
+            gather(x_first[c][:, 0, :], 0, c, c + 1)
         gather(x_second[:, 0, :], 0, 2, 4)
         cast_x(1, 0, 0, 512, True)
         cast_x(1, 1, 512, 704, True)
         cast_x(1, 1, 704, 1024, False)
 
-        gather(listed_first[0][:, :, 1], 1, 0, 1)
+        gather(x_first[0][:, 1, :], 1, 0, 1)
+        weave(listed_first[0], x_first[0][:])
         reorder_wd(0)
+        gather(x_first[1][:, 1, :], 1, 1, 2)
+        weave(listed_first[1][:], x_first[1][:])
         quantize_x(0, 1, listed_first[0])
         a00 = product(0, 0, 0)
+        wd_codes.append(keep.tile([P, K_PASS], I32, name="wd_codes1", tag="x_first0", align_bytes=64))
         reorder_wd(1)
-        reorder_wd_scale(1)
         a01 = product(0, 1, 1)
-        gather(x_first[:, 1, :], 1, 1, 2)
-        weave(listed_first[1][:], x_first)
         gather(x_second[:, 1, :], 1, 2, 4)
         quantize_x(1, 2, listed_first[1][:])
         a10 = product(1, 0, 2)
@@ -381,12 +387,15 @@ def tile_attend_gml_sq_kernel(tc, xT, wd_words, wd_scales, wv_words, wv_scales, 
         scale_product(1, 0, a10)
         scale_targets(1, 1)
         scale_product(1, 1, a11)
-        weigh(grad_early[:, 0:V], res_first[:].rearrange("p t o i -> p t (o i)"), weight_first[:].rearrange("p t o i -> p t (o i)"), nc.vector, RUN)
-        quantize_grad(g_cols(0, 0, 2), grad_early[:, 0:V])
+        grad_early = [front.tile([P, K_PASS], BF16, name="grad_early0", offset=1536, align_bytes=64), keep.tile([P, K_PASS], BF16, name="grad_early1", align_bytes=64)]
+        for o in range(PASSES):
+            weigh(grad_early[o][:], res[0, o], weight[0, o], nc.vector, RUN)
+        for o in range(PASSES):
+            quantize_grad(g_cols(0, o, o + 1), grad_early[o][:])
         res[3, 0] = front.tile([P, K_PASS], F32, name="res30", offset=0)
-        res[2, 0] = front.tile([P, K_PASS], F32, name="res20", offset=2048)
+        res[2, 0] = front.tile([P, LANES, CHUNK], F32, name="res20", offset=2048)
         res[3, 1] = relay.tile([P, K_PASS], F32, name="res31", offset=2048)
-        res[2, 1] = relay.tile([P, K_PASS], F32, name="res21", offset=6144)
+        res[2, 1] = relay.tile([P, LANES, CHUNK], F32, name="res21", offset=6144)
         rw_third = rw_mid[:, 1, :]
         weight[2, 0] = ys.tile([P, LANES, CHUNK], F32, name="weight20", offset=0)[:]
         make_weight(2, 0, rw_third)
@@ -397,10 +406,10 @@ def tile_attend_gml_sq_kernel(tc, xT, wd_words, wd_scales, wv_words, wv_scales, 
         e0a = turn_early(0, 0, 1, 1)
         subtract_woven(3, 0, a30)
         nc.gpsimd.tensor_tensor(grad_second[:, 0:K_PASS], res[3, 0][:], weight_second[:, 0, :], MULT)
-        subtract_woven(2, 0, a20)
+        subtract_targets(2, 0, a20)
         subtract_woven(3, 1, a31)
         nc.gpsimd.tensor_tensor(grad_second[:, K_PASS:V], res[3, 1][:], weight_second[:, 1, :], MULT)
-        subtract_woven(2, 1, a21)
+        subtract_targets(2, 1, a21)
         part_a = {c: keep.tile([P, CHUNK], F32, name=f"part_a{c}") for c in EARLY}
         fetch_early(0, 0, 1, e0a, part_a[0][:])
         e0b = turn_early(0, 1, 4, 4)

@@ -30,7 +30,7 @@ CHUNKS = N // CHUNK
 HALF = N // 2
 LIST_COLS = CHUNK // 16
 RUN = 2
-X_PIECES = (((0, 512), (512, 1024)), ((0, 512), (512, 1024)))
+X_PIECES = (((0, 1024),), ((0, 512), (512, 1024)))
 EARLY = (0, 3)
 LATE = (1, 2)
 TURNED = ((1, 0), (1, 1))
@@ -73,18 +73,19 @@ def tile_attend_gml_sq_kernel(tc, xT, wd_words, wd_scales, wv_words, wv_scales, 
         for t in range(LANES):
             neg_col[1, t] = cw_neg[1 + t // 2][:, t % 2 : t % 2 + 1]
         rw_head = keep.tile([P, 2, CHUNK], F32, name="rw_head")
-        rw_mid = keep.tile([P, 2, CHUNK], F32, name="rw_mid")
+        rw_mid = keep.tile([P, CHUNK], F32, name="rw_mid")
         x_raw = [[keep.tile([P, 2, b - a], F32, name=f"x_raw{u}_{a}", tag=f"x_raw{u}_{a}", align_bytes=64) for a, b in X_PIECES[u]] for u in range(PAIRS)]
         rw_col = keep.tile([P, 1], F32, name="rw_col")
         x_pairs = [keep.tile([P, T], U32, name=f"x_pairs{u}") for u in range(PAIRS)]
         stage = mid.tile([P, 2 * HALF], U32, name="stage", offset=2048, align_bytes=64)
         x_first = [keep.tile([P, PAIRS, CHUNK], U32, name=f"x_first{c}", tag=f"x_first{c}", align_bytes=64) for c in range(2)]
-        wd_scale = keep.tile([P, K_PASS], U8, name="wd_scale", tag="x_raw0_512", align_bytes=64)
+        wd_scale = keep.tile([P, K_PASS], U8, name="wd_scale", tag="x_raw0_0", align_bytes=64)
         x_second = stage[:].rearrange("p (u i) -> p u i", u=PAIRS)
         listed_first = [stage[:, HALF:].rearrange("p (i u) -> p i u", u=PAIRS), keep.tile([P, CHUNK, PAIRS], U32, name="listed1", align_bytes=64)]
         x_codes = keep.tile([P, N], U32, name="x_codes", align_bytes=64)
         x_scale = keep.tile([P, N], U8, name="x_scale", align_bytes=64)
-        y_sb = [[keep.tile([P, LANES, HALF], F32, name=f"y_sb{h}{o}", tag=f"y_sb{h}{o}", align_bytes=64) for o in range(PASSES)] for h in range(2)]
+        y_sb = [[keep.tile([P, LANES, HALF], F32, name=f"y_sb{h}{o}", tag=f"y_sb{h}{o}", align_bytes=64) for o in range(PASSES - h)] for h in range(2)]
+        y_last = {c: keep.tile([P, LANES, CHUNK], F32, name=f"y_last{c}") for c in (2, 3)}
         weight_first = keep.tile([P, LANES, PASSES, CHUNK], F32, name="weight_first")
         weight = {(0, o): weight_first[:, :, o, :] for o in range(PASSES)}
         weight_second = keep.tile([P, PASSES, K_PASS], F32, name="weight_second")
@@ -132,7 +133,6 @@ def tile_attend_gml_sq_kernel(tc, xT, wd_words, wd_scales, wv_words, wv_scales, 
         nc.sync.dma_start(cw_sb, cw.rearrange("(o p t) one -> p o (t one)", o=PASSES, t=LANES))
         nc.sync.dma_start(rw_head[:], rw_chunks[:, 0:CHUNKS:3, :])
         load_x(0, 0)
-        load_x(0, 1)
         for q in range(QUADRANTS):
             load_wd_scales(nc.sync, q)
         for k in range(len(X_PIECES[1])):
@@ -141,12 +141,14 @@ def tile_attend_gml_sq_kernel(tc, xT, wd_words, wd_scales, wv_words, wv_scales, 
         load_wd(1)
         load_y(0, 0)
         load_y(0, 1)
-        nc.sync.dma_start(rw_mid[:], rw_chunks[:, 1:3, :])
+        nc.sync.dma_start(rw_mid[:], rw_chunks[:, 2, :])
         load_y(1, 0)
         for q in range(QUADRANTS):
             load_wv_scales(nc.sync, q)
         nc.sync.dma_start(wv_codes[:], wv_words.rearrange("o p d t -> p o (d t)").bitcast(I32))
-        load_y(1, 1)
+        for c in (3, 2):
+            nc.sync.dma_start(y_last[c][:], y_rows[1][:, :, c * CHUNK : (c + 1) * CHUNK])
+        nc.sync.dma_start(rw_col[:], rw[0, CHUNK : 2 * CHUNK].rearrange("(p one) -> p one", one=1))
 
         make_identity(nc, ident[:])
         for j in range(D_TILES - 1):
@@ -187,11 +189,6 @@ def tile_attend_gml_sq_kernel(tc, xT, wd_words, wd_scales, wv_words, wv_scales, 
                 MULT,
             )
 
-        def turn_rw(c, b):
-            col_bank = bank(b, [P, P], "col_bank")
-            nc.tensor.transpose(col_bank[:], rw_mid[:, c - 1, :], ident[:])
-            nc.scalar.copy(rw_col[:], col_bank[:, 0:1])
-
         def gather(dst, u, c0, c1):
             nc.vector.tensor_copy(dst, x_pairs[u][:].indirect(offsets[:, c0 * LIST_COLS : c1 * LIST_COLS]))
 
@@ -226,6 +223,8 @@ def tile_attend_gml_sq_kernel(tc, xT, wd_words, wd_scales, wv_words, wv_scales, 
 
         def y_of(c, o):
             h, within = divmod(c * CHUNK, HALF)
+            if h and o:
+                return y_last[c][:]
             return y_sb[h][o][:, :, within : within + CHUNK]
 
         def residual(c0, c1, o):
@@ -346,9 +345,8 @@ def tile_attend_gml_sq_kernel(tc, xT, wd_words, wd_scales, wv_words, wv_scales, 
             make_weight(0, o, rw_head[:, 0, :])
         for o in range(PASSES):
             make_weight_woven(o, rw_head[:, 1, :])
-        cast_x(0, 0, 0, 512, False)
-        cast_x(0, 1, 512, 704, True)
-        cast_x(0, 1, 704, 1024, False)
+        cast_x(0, 0, 0, 384, True)
+        cast_x(0, 0, 384, 1024, False)
         reorder_wd_scale()
         for c in range(2):
             gather(x_first[c][:, 0, :], 0, c, c + 1)
@@ -379,7 +377,6 @@ def tile_attend_gml_sq_kernel(tc, xT, wd_words, wd_scales, wv_words, wv_scales, 
         subtract_targets(0, 0, a00)
         subtract_targets(0, 1, a01)
         quantize_x(2, 4, listed_second[:])
-        turn_rw(1, 7)
         a30 = product(3, 0, 4)
         a20 = product(2, 0, 5)
         a31 = product(3, 1, 6)
@@ -396,7 +393,7 @@ def tile_attend_gml_sq_kernel(tc, xT, wd_words, wd_scales, wv_words, wv_scales, 
         res[2, 0] = front.tile([P, LANES, CHUNK], F32, name="res20", offset=2048)
         res[3, 1] = relay.tile([P, K_PASS], F32, name="res31", offset=2048)
         res[2, 1] = relay.tile([P, LANES, CHUNK], F32, name="res21", offset=6144)
-        rw_third = rw_mid[:, 1, :]
+        rw_third = rw_mid[:]
         weight[2, 0] = ys.tile([P, LANES, CHUNK], F32, name="weight20", offset=0)[:]
         make_weight(2, 0, rw_third)
         grad_second = grads.tile([P, V], BF16, name="grad_second", offset=0, align_bytes=64)
@@ -425,8 +422,8 @@ def tile_attend_gml_sq_kernel(tc, xT, wd_words, wd_scales, wv_words, wv_scales, 
         dx_early[0, 2] = part_c0[:, 0:CHUNK]
         dx_early[0, 3] = part_c0[:, CHUNK : 2 * CHUNK]
         grad_turned = {(1, o): relay.tile([P, K_PASS], BF16, name=f"grad_turned{o}", offset=(1088, 3648)[o]) for o in range(PASSES)}
-        turn_and_weigh(1, 0, 0)
-        turn_and_weigh(1, 1, 1)
+        turn_and_weigh(1, 0, 2)
+        turn_and_weigh(1, 1, 0)
         grad_late = grads.tile([P, 4 * K_PASS], BF16, name="grad_late", offset=0, align_bytes=64)
         weigh_side(2, 0, grad_late[:, K_PASS : 2 * K_PASS])
         weigh_side(2, 1, grad_late[:, 3 * K_PASS : 4 * K_PASS])
@@ -445,7 +442,7 @@ def tile_attend_gml_sq_kernel(tc, xT, wd_words, wd_scales, wv_words, wv_scales, 
         scatter_early(3, 0)
         quantize_grad(slice(G_COLS[1, 0] * CHUNK, (G_COLS[2, 1] + 1) * CHUNK), grad_late[:])
         for j in range(D_TILES):
-            back_rest(j, (6, 7, 4, 0)[j], (1, 0))
+            back_rest(j, (6, 7, 4, 1)[j], (1, 0))
         for j in range(1, D_TILES):
             scatter_early(3, j)
         for j in range(D_TILES):

@@ -141,14 +141,14 @@ def tile_attend_gml_sq_kernel(tc, xT, wd_words, wd_scales, wv_words, wv_scales, 
         load_wd(1)
         load_y(0, 0)
         load_y(0, 1)
-        nc.sync.dma_start(rw_mid[:], rw_chunks[:, 2, :])
+        nc.sync.dma_start(rw_col[:], rw[0, CHUNK : 2 * CHUNK].rearrange("(p one) -> p one", one=1))
         load_y(1, 0)
         for q in range(QUADRANTS):
             load_wv_scales(nc.sync, q)
         nc.sync.dma_start(wv_codes[:], wv_words.rearrange("o p d t -> p o (d t)").bitcast(I32))
-        for c in (3, 2):
-            nc.sync.dma_start(y_last[c][:], y_rows[1][:, :, c * CHUNK : (c + 1) * CHUNK])
-        nc.sync.dma_start(rw_col[:], rw[0, CHUNK : 2 * CHUNK].rearrange("(p one) -> p one", one=1))
+        nc.sync.dma_start(y_last[3][:], y_rows[1][:, :, 3 * CHUNK : 4 * CHUNK])
+        nc.sync.dma_start(y_last[2][:], y_rows[1][:, :, 2 * CHUNK : 3 * CHUNK])
+        nc.sync.dma_start(rw_mid[:], rw_chunks[:, 2, :])
 
         make_identity(nc, ident[:])
         for j in range(D_TILES - 1):
@@ -391,11 +391,11 @@ def tile_attend_gml_sq_kernel(tc, xT, wd_words, wd_scales, wv_words, wv_scales, 
             quantize_grad(g_cols(0, o, o + 1), grad_early[o][:])
         res[3, 0] = front.tile([P, K_PASS], F32, name="res30", offset=0)
         res[2, 0] = front.tile([P, LANES, CHUNK], F32, name="res20", offset=2048)
-        res[3, 1] = relay.tile([P, K_PASS], F32, name="res31", offset=2048)
-        res[2, 1] = relay.tile([P, LANES, CHUNK], F32, name="res21", offset=6144)
+        res[3, 1] = relay.tile([P, 2 * K_PASS], F32, name="res31", offset=2048)[:, 0:K_PASS]
+        res[2, 1] = relay.tile([P, LANES, CHUNK], F32, name="res21", offset=6656)
         rw_third = rw_mid[:]
-        weight[2, 0] = ys.tile([P, LANES, CHUNK], F32, name="weight20", offset=0)[:]
-        make_weight(2, 0, rw_third)
+        grad_turned = {(1, 0): keep.tile([P, K_PASS], BF16, name="grad_turned0")}
+        turn_and_weigh(1, 0, 2)
         grad_second = grads.tile([P, V], BF16, name="grad_second", offset=0, align_bytes=64)
         t0 = back_early(0, 0)
         copy_early(0, 0, 1, t0)
@@ -410,32 +410,33 @@ def tile_attend_gml_sq_kernel(tc, xT, wd_words, wd_scales, wv_words, wv_scales, 
         part_a = {c: keep.tile([P, CHUNK], F32, name=f"part_a{c}") for c in EARLY}
         fetch_early(0, 0, 1, e0a, part_a[0][:])
         e0b = turn_early(0, 1, 4, 4)
-        weight[2, 1] = dts.tile([P, LANES, CHUNK], F32, name="weight21", offset=0)[:]
-        make_weight(2, 1, rw_third)
+        weight[2, 0] = dts.tile([P, LANES, CHUNK], F32, name="weight20", offset=0)[:]
+        make_weight(2, 0, rw_third)
         scatter_early(0, 0)
         quantize_grad(g_cols(3, 0, 2), grad_second[:])
-        part_b0 = relay.tile([P, CHUNK], F32, name="part_b0", offset=2112)
-        part_c0 = relay.tile([P, 2 * CHUNK], F32, name="part_c0", offset=2624)
+        part_b0 = relay.tile([P, CHUNK], F32, name="part_b0", offset=2048)
+        part_c0 = relay.tile([P, 2 * CHUNK], F32, name="part_c0", offset=2560)
         nc.scalar.copy(part_b0[:], e0b[:, 0, :])
         nc.scalar.copy(part_c0[:], e0b[:, 1:3, :].rearrange("p j i -> p (j i)"))
         dx_early[0, 1] = part_b0[:]
         dx_early[0, 2] = part_c0[:, 0:CHUNK]
         dx_early[0, 3] = part_c0[:, CHUNK : 2 * CHUNK]
-        grad_turned = {(1, o): relay.tile([P, K_PASS], BF16, name=f"grad_turned{o}", offset=(1088, 3648)[o]) for o in range(PASSES)}
-        turn_and_weigh(1, 0, 2)
+        grad_turned[1, 1] = relay.tile([P, K_PASS], BF16, name="grad_turned1", offset=3584)
         turn_and_weigh(1, 1, 0)
+        weight[2, 1] = relay.tile([P, LANES, CHUNK], F32, name="weight21", offset=4608)[:]
+        make_weight(2, 1, rw_third)
         grad_late = grads.tile([P, 4 * K_PASS], BF16, name="grad_late", offset=0, align_bytes=64)
         weigh_side(2, 0, grad_late[:, K_PASS : 2 * K_PASS])
         weigh_side(2, 1, grad_late[:, 3 * K_PASS : 4 * K_PASS])
         t1 = back_early(3, 3)
         copy_early(3, 0, 1, t1)
         copy_early(3, 1, 4, t1)
+        turn_back(1, 0, 0, grad_late[:, 0:K_PASS])
         e1a = turn_early(3, 0, 1, 2)
         fetch_early(3, 0, 1, e1a, part_a[3][:])
         turn_back(1, 1, 3, grad_late[:, 2 * K_PASS : 3 * K_PASS])
-        turn_back(1, 0, 2, grad_late[:, 0:K_PASS])
         e1b = turn_early(3, 1, 4, 5)
-        part_b1 = relay.tile([P, 3 * CHUNK], F32, name="part_b1", offset=6144)
+        part_b1 = relay.tile([P, 3 * CHUNK], F32, name="part_b1", offset=6656)
         fetch_early(3, 1, 4, e1b, part_b1[:])
         for j in range(1, D_TILES):
             scatter_early(0, j)

@@ -51,6 +51,7 @@ def tile_attend_gml_sq_kernel(tc, xT, wd_words, wd_scales, wv_words, wv_scales, 
         neg = ctx.enter_context(tc.tile_pool(name="neg", bufs=1))
         ys = ctx.enter_context(tc.tile_pool(name="ys", bufs=1))
         dts = ctx.enter_context(tc.tile_pool(name="dts", bufs=1))
+        late = ctx.enter_context(tc.tile_pool(name="late", bufs=1))
         grads = ctx.enter_context(tc.tile_pool(name="grads", bufs=1))
         psum = ctx.enter_context(tc.psum_pool(name="psum", bufs=1))
 
@@ -60,7 +61,7 @@ def tile_attend_gml_sq_kernel(tc, xT, wd_words, wd_scales, wv_words, wv_scales, 
         offsets = keep.tile([P, N // 16], U16, name="offsets")
         wd_raw = [keep.tile([P, K_PASS], I32, name=f"wd_raw{o}", tag=f"wd_raw{o}", align_bytes=64) for o in range(PASSES)]
         wd_raw_scale = keep.tile([P, K_PASS], U8, name="wd_raw_scale", align_bytes=64)
-        wd_codes = [keep.tile([P, K_PASS], I32, name="wd_codes0", align_bytes=64)]
+        wd_codes = [keep.tile([P, K_PASS], I32, name=f"wd_codes{o}", align_bytes=64) for o in range(PASSES)]
         wv_codes = keep.tile([P, PASSES, D], I32, name="wv_codes", align_bytes=64)
         wv_scale = keep.tile([P, PASSES, D], U8, name="wv_scale", align_bytes=64)
         cw_sb = keep.tile([P, PASSES, 2 * LANES], F32, name="cw_sb")[:, :, 0:LANES]
@@ -78,7 +79,7 @@ def tile_attend_gml_sq_kernel(tc, xT, wd_words, wd_scales, wv_words, wv_scales, 
         rw_col = keep.tile([P, 1], F32, name="rw_col")
         x_pairs = [keep.tile([P, T], U32, name=f"x_pairs{u}") for u in range(PAIRS)]
         stage = mid.tile([P, 2 * HALF], U32, name="stage", offset=2048, align_bytes=64)
-        x_first = [keep.tile([P, PAIRS, CHUNK], U32, name=f"x_first{c}", tag=f"x_first{c}", align_bytes=64) for c in range(2)]
+        x_first = keep.tile([P, PAIRS, CHUNK], U32, name="x_first")
         wd_scale = keep.tile([P, K_PASS], U8, name="wd_scale", tag="x_raw0_0", align_bytes=64)
         x_second = stage[:].rearrange("p (u i) -> p u i", u=PAIRS)
         listed_first = [stage[:, HALF:].rearrange("p (i u) -> p i u", u=PAIRS), keep.tile([P, CHUNK, PAIRS], U32, name="listed1", align_bytes=64)]
@@ -91,9 +92,12 @@ def tile_attend_gml_sq_kernel(tc, xT, wd_words, wd_scales, wv_words, wv_scales, 
         weight_second = keep.tile([P, PASSES, K_PASS], F32, name="weight_second")
         a_scaled = {(1, o): mid.tile([P, LANES, CHUNK], F32, name=f"a_scaled{o}", offset=1024 + 2048 * o) for o in range(PASSES)}
         y_scaled = {(1, 0): keep.tile([P, LANES, CHUNK], F32, name="y_scaled0"), (1, 1): keep.tile([P, LANES, CHUNK], F32, name="y_scaled1")}
-        g_codes = keep.tile([P, PASSES * N], U32, name="g_codes", align_bytes=64)
+        y_part = {(o, t): y_scaled[1, o][:, t, :] for o in range(PASSES) for t in range(LANES)}
+        g_first = [keep.tile([P, CHUNK], U32, name=f"g_first{o}", tag=f"g_first{o}", align_bytes=64) for o in range(PASSES)]
+        part_a = {3: keep.tile([P, CHUNK], F32, name="part_a3")}
+        g_codes = late.tile([P, PASSES * N - HALF], U32, name="g_codes", offset=0, align_bytes=64)
         g_scale = keep.tile([P, PASSES * N], U8, name="g_scale", align_bytes=64)
-        dx_turned = {0: dts.tile([P, D], F32, name="dx_turned0", offset=0), 3: keep.tile([P, D], F32, name="dx_turned3")}
+        dx_turned = {0: dts.tile([P, D], F32, name="dx_turned0", offset=0), 3: keep.tile([P, D], F32, name="dx_turned3", tag="dx_turned3")}
         dx_early = {}
         dx_rest = [keep.tile([P, len(LATE) * CHUNK], F32, name=f"dx_rest{j}") for j in range(D_TILES)]
         windows = [keep.tile([P, T], F32, name=f"window{j}") for j in range(D_TILES)]
@@ -141,6 +145,7 @@ def tile_attend_gml_sq_kernel(tc, xT, wd_words, wd_scales, wv_words, wv_scales, 
         load_wd(1)
         load_y(0, 0)
         load_y(0, 1)
+        nc.sync.dma_start(rw_mid[:], rw_chunks[:, 2, :])
         nc.sync.dma_start(rw_col[:], rw[0, CHUNK : 2 * CHUNK].rearrange("(p one) -> p one", one=1))
         load_y(1, 0)
         for q in range(QUADRANTS):
@@ -148,7 +153,6 @@ def tile_attend_gml_sq_kernel(tc, xT, wd_words, wd_scales, wv_words, wv_scales, 
         nc.sync.dma_start(wv_codes[:], wv_words.rearrange("o p d t -> p o (d t)").bitcast(I32))
         nc.sync.dma_start(y_last[3][:], y_rows[1][:, :, 3 * CHUNK : 4 * CHUNK])
         nc.sync.dma_start(y_last[2][:], y_rows[1][:, :, 2 * CHUNK : 3 * CHUNK])
-        nc.sync.dma_start(rw_mid[:], rw_chunks[:, 2, :])
 
         make_identity(nc, ident[:])
         for j in range(D_TILES - 1):
@@ -252,20 +256,23 @@ def tile_attend_gml_sq_kernel(tc, xT, wd_words, wd_scales, wv_words, wv_scales, 
         def weigh_side(c, o, dst):
             weigh(dst, res[c, o][:], weight[c, o], nc.gpsimd, SIDE_RUN)
 
-        def scale_targets(c, o):
-            for t in range(LANES):
-                nc.scalar.activation(y_scaled[c, o][:, t, :], y_of(c, o)[:, t, :], COPY, scale=neg_col[o, t])
+        def scale_targets(c, o, lanes):
+            for t in lanes:
+                nc.scalar.activation(y_part[o, t], y_of(c, o)[:, t, :], COPY, scale=neg_col[o, t])
 
         def scale_product(c, o, a_bank):
             for t in range(LANES):
                 nc.scalar.activation(a_scaled[c, o][:, t, :], a_bank[:, t, :], COPY, scale=cw_sb[:, o, t : t + 1])
 
-        def turn_and_weigh(c, o, b):
+        def turn_and_add(c, o, b):
             sum_bank = bank(b, [P, LANES, P], f"sum_bank{c}{o}")
             for t in range(LANES):
-                nc.tensor.matmul(sum_bank[:, t, :], y_scaled[c, o][:, t, :], ident[:], start=(t == 0), stop=False, is_transpose=True)
+                nc.tensor.matmul(sum_bank[:, t, :], y_part[o, t], ident[:], start=(t == 0), stop=False, is_transpose=True)
             for t in range(LANES):
                 nc.tensor.matmul(sum_bank[:, t, :], a_scaled[c, o][:, t, :], ident[:], start=False, stop=(t == LANES - 1), is_transpose=True)
+            return sum_bank
+
+        def round_turned(c, o, sum_bank):
             nc.scalar.activation(
                 grad_turned[c, o][:].rearrange("i (u p e) -> i u p e", u=PAIRS, e=2),
                 sum_bank[:].rearrange("i (u e) p -> i u p e", u=PAIRS),
@@ -286,15 +293,18 @@ def tile_attend_gml_sq_kernel(tc, xT, wd_words, wd_scales, wv_words, wv_scales, 
         def g_cols(c, o0, o1):
             return slice(G_COLS[c, o0] * CHUNK, (G_COLS[c, o1 - 1] + 1) * CHUNK)
 
+        def g_words(cols):
+            return g_first[cols.start // CHUNK][:] if cols.start < HALF else g_codes[:, cols.start - HALF : cols.stop - HALF]
+
         def quantize_grad(cols, src):
-            nc.vector.quantize_mx(out=g_codes[:, cols].bitcast(E5M2), scales=g_scale[:, cols], in_=src)
+            nc.vector.quantize_mx(out=g_words(cols).bitcast(E5M2), scales=g_scale[:, cols], in_=src)
 
         def back_early(c, b0):
             turned_bank = bank(b0, [P, D], f"turned_bank{c}")
             for o in range(PASSES):
                 nc.tensor.matmul_mx(
                     out=turned_bank[:],
-                    lhsT=g_codes[:, g_cols(c, o, o + 1)].bitcast(E5M2),
+                    lhsT=g_words(g_cols(c, o, o + 1)).bitcast(E5M2),
                     lhsT_scale=g_scale[:, g_cols(c, o, o + 1)],
                     rhs=wv_codes[:, o, :].bitcast(E4M3),
                     rhs_scale=wv_scale[:, o, :],
@@ -324,7 +334,7 @@ def tile_attend_gml_sq_kernel(tc, xT, wd_words, wd_scales, wv_words, wv_scales, 
                     out=dx_bank[:],
                     lhsT=wv_codes[:, o, j * P : (j + 1) * P].bitcast(E4M3),
                     lhsT_scale=wv_scale[:, o, j * P : (j + 1) * P],
-                    rhs=g_codes[:, G_START[o] : G_START[o] + N].bitcast(E5M2),
+                    rhs=g_words(slice(G_START[o], G_START[o] + N)).bitcast(E5M2),
                     rhs_scale=g_scale[:, G_START[o] : G_START[o] + N],
                     start=(o == passes[0]),
                     stop=(o == passes[-1]),
@@ -348,21 +358,19 @@ def tile_attend_gml_sq_kernel(tc, xT, wd_words, wd_scales, wv_words, wv_scales, 
         cast_x(0, 0, 0, 384, True)
         cast_x(0, 0, 384, 1024, False)
         reorder_wd_scale()
-        for c in range(2):
-            gather(x_first[c][:, 0, :], 0, c, c + 1)
+        gather(listed_first[0][:, :, 0], 0, 0, 1)
+        gather(x_first[:, 0, :], 0, 1, 2)
         gather(x_second[:, 0, :], 0, 2, 4)
         cast_x(1, 0, 0, 512, True)
         cast_x(1, 1, 512, 704, True)
         cast_x(1, 1, 704, 1024, False)
 
-        gather(x_first[0][:, 1, :], 1, 0, 1)
-        weave(listed_first[0], x_first[0][:])
+        gather(listed_first[0][:, :, 1], 1, 0, 1)
         reorder_wd(0)
-        gather(x_first[1][:, 1, :], 1, 1, 2)
-        weave(listed_first[1][:], x_first[1][:])
+        gather(x_first[:, 1, :], 1, 1, 2)
+        weave(listed_first[1][:], x_first[:])
         quantize_x(0, 1, listed_first[0])
         a00 = product(0, 0, 0)
-        wd_codes.append(keep.tile([P, K_PASS], I32, name="wd_codes1", tag="x_first0", align_bytes=64))
         reorder_wd(1)
         a01 = product(0, 1, 1)
         gather(x_second[:, 1, :], 1, 2, 4)
@@ -371,7 +379,7 @@ def tile_attend_gml_sq_kernel(tc, xT, wd_words, wd_scales, wv_words, wv_scales, 
         a11 = product(1, 1, 3)
         res_first = keep.tile([P, LANES, PASSES, CHUNK], F32, name="res_first")
         res = {(0, o): res_first[:, :, o, :] for o in range(PASSES)}
-        scale_targets(1, 0)
+        scale_targets(1, 0, range(LANES))
         listed_second = neg.tile([P, HALF, PAIRS], U32, name="listed_second", offset=0, align_bytes=64)
         weave(listed_second[:], x_second)
         subtract_targets(0, 0, a00)
@@ -382,7 +390,7 @@ def tile_attend_gml_sq_kernel(tc, xT, wd_words, wd_scales, wv_words, wv_scales, 
         a31 = product(3, 1, 6)
         a21 = product(2, 1, 7)
         scale_product(1, 0, a10)
-        scale_targets(1, 1)
+        scale_targets(1, 1, range(LANES))
         scale_product(1, 1, a11)
         grad_early = [front.tile([P, K_PASS], BF16, name="grad_early0", offset=1536, align_bytes=64), keep.tile([P, K_PASS], BF16, name="grad_early1", align_bytes=64)]
         for o in range(PASSES):
@@ -392,51 +400,47 @@ def tile_attend_gml_sq_kernel(tc, xT, wd_words, wd_scales, wv_words, wv_scales, 
         res[3, 0] = front.tile([P, K_PASS], F32, name="res30", offset=0)
         res[2, 0] = front.tile([P, LANES, CHUNK], F32, name="res20", offset=2048)
         res[3, 1] = relay.tile([P, 2 * K_PASS], F32, name="res31", offset=2048)[:, 0:K_PASS]
-        res[2, 1] = relay.tile([P, LANES, CHUNK], F32, name="res21", offset=6656)
+        res[2, 1] = relay.tile([P, LANES, CHUNK], F32, name="res21", offset=8192)
         rw_third = rw_mid[:]
-        grad_turned = {(1, 0): keep.tile([P, K_PASS], BF16, name="grad_turned0")}
-        turn_and_weigh(1, 0, 2)
+        weight[2, 0] = ys.tile([P, LANES, CHUNK], F32, name="weight20", offset=0)[:]
+        make_weight(2, 0, rw_third)
         grad_second = grads.tile([P, V], BF16, name="grad_second", offset=0, align_bytes=64)
         t0 = back_early(0, 0)
         copy_early(0, 0, 1, t0)
         copy_early(0, 1, 4, t0)
         e0a = turn_early(0, 0, 1, 1)
+        sum_first = turn_and_add(1, 0, 2)
         subtract_woven(3, 0, a30)
         nc.gpsimd.tensor_tensor(grad_second[:, 0:K_PASS], res[3, 0][:], weight_second[:, 0, :], MULT)
         subtract_targets(2, 0, a20)
         subtract_woven(3, 1, a31)
-        nc.gpsimd.tensor_tensor(grad_second[:, K_PASS:V], res[3, 1][:], weight_second[:, 1, :], MULT)
         subtract_targets(2, 1, a21)
-        part_a = {c: keep.tile([P, CHUNK], F32, name=f"part_a{c}") for c in EARLY}
+        nc.vector.tensor_tensor(grad_second[:, K_PASS:V], res[3, 1][:], weight_second[:, 1, :], MULT)
+        quantize_grad(g_cols(3, 0, 2), grad_second[:])
+        part_a[0] = relay.tile([P, CHUNK], F32, name="part_a0", offset=2048)
         fetch_early(0, 0, 1, e0a, part_a[0][:])
         e0b = turn_early(0, 1, 4, 4)
-        weight[2, 0] = dts.tile([P, LANES, CHUNK], F32, name="weight20", offset=0)[:]
-        make_weight(2, 0, rw_third)
         scatter_early(0, 0)
-        quantize_grad(g_cols(3, 0, 2), grad_second[:])
-        part_b0 = relay.tile([P, CHUNK], F32, name="part_b0", offset=2048)
-        part_c0 = relay.tile([P, 2 * CHUNK], F32, name="part_c0", offset=2560)
-        nc.scalar.copy(part_b0[:], e0b[:, 0, :])
-        nc.scalar.copy(part_c0[:], e0b[:, 1:3, :].rearrange("p j i -> p (j i)"))
-        dx_early[0, 1] = part_b0[:]
-        dx_early[0, 2] = part_c0[:, 0:CHUNK]
-        dx_early[0, 3] = part_c0[:, CHUNK : 2 * CHUNK]
-        grad_turned[1, 1] = relay.tile([P, K_PASS], BF16, name="grad_turned1", offset=3584)
-        turn_and_weigh(1, 1, 0)
-        weight[2, 1] = relay.tile([P, LANES, CHUNK], F32, name="weight21", offset=4608)[:]
+        part_b0 = relay.tile([P, 3 * CHUNK], F32, name="part_b0", offset=2560)
+        fetch_early(0, 1, 4, e0b, part_b0[:])
+        grad_turned = {(1, o): relay.tile([P, K_PASS], BF16, name=f"grad_turned{o}", offset=(4096, 7168)[o]) for o in range(PASSES)}
+        round_turned(1, 0, sum_first)
+        weight[2, 1] = relay.tile([P, LANES, CHUNK], F32, name="weight21", offset=5120)[:]
         make_weight(2, 1, rw_third)
+        round_turned(1, 1, turn_and_add(1, 1, 1))
         grad_late = grads.tile([P, 4 * K_PASS], BF16, name="grad_late", offset=0, align_bytes=64)
         weigh_side(2, 0, grad_late[:, K_PASS : 2 * K_PASS])
         weigh_side(2, 1, grad_late[:, 3 * K_PASS : 4 * K_PASS])
         t1 = back_early(3, 3)
         copy_early(3, 0, 1, t1)
-        copy_early(3, 1, 4, t1)
-        turn_back(1, 0, 0, grad_late[:, 0:K_PASS])
-        e1a = turn_early(3, 0, 1, 2)
+        turn_back(1, 0, 2, grad_late[:, 0:K_PASS])
+        e1a = turn_early(3, 0, 1, 0)
         fetch_early(3, 0, 1, e1a, part_a[3][:])
-        turn_back(1, 1, 3, grad_late[:, 2 * K_PASS : 3 * K_PASS])
+        dx_turned[3] = keep.tile([P, D], F32, name="dx_turned3_rest", tag="dx_turned3")
+        copy_early(3, 1, 4, t1)
+        turn_back(1, 1, 2, grad_late[:, 2 * K_PASS : 3 * K_PASS])
         e1b = turn_early(3, 1, 4, 5)
-        part_b1 = relay.tile([P, 3 * CHUNK], F32, name="part_b1", offset=6656)
+        part_b1 = relay.tile([P, 3 * CHUNK], F32, name="part_b1", offset=7680)
         fetch_early(3, 1, 4, e1b, part_b1[:])
         for j in range(1, D_TILES):
             scatter_early(0, j)

@@ -152,7 +152,8 @@ def tile_attend_gml_sq_kernel(tc, xT, wd_words, wd_scales, wv_words, wv_scales, 
             load_wv_scales(nc.sync, q)
         nc.sync.dma_start(wv_codes[:], wv_words.rearrange("o p d t -> p o (d t)").bitcast(I32))
         nc.sync.dma_start(y_last[3][:], y_rows[1][:, :, 3 * CHUNK : 4 * CHUNK])
-        nc.sync.dma_start(y_last[2][:], y_rows[1][:, :, 2 * CHUNK : 3 * CHUNK])
+        for u in range(PAIRS):
+            nc.sync.dma_start(y_last[2][:, 2 * u : 2 * u + 2, :], y_rows[1][:, 2 * u : 2 * u + 2, 2 * CHUNK : 3 * CHUNK])
 
         make_identity(nc, ident[:])
         for j in range(D_TILES - 1):
@@ -404,18 +405,20 @@ def tile_attend_gml_sq_kernel(tc, xT, wd_words, wd_scales, wv_words, wv_scales, 
         rw_third = rw_mid[:]
         weight[2, 0] = ys.tile([P, LANES, CHUNK], F32, name="weight20", offset=0)[:]
         make_weight(2, 0, rw_third)
+        grad_turned = {(1, 0): keep.tile([P, K_PASS], BF16, name="grad_turned0"), (1, 1): relay.tile([P, K_PASS], BF16, name="grad_turned1", offset=7168)}
+        for o in range(PASSES):
+            round_turned(1, o, turn_and_add(1, o, 2 + o))
         grad_second = grads.tile([P, V], BF16, name="grad_second", offset=0, align_bytes=64)
         t0 = back_early(0, 0)
         copy_early(0, 0, 1, t0)
         copy_early(0, 1, 4, t0)
         e0a = turn_early(0, 0, 1, 1)
-        sum_first = turn_and_add(1, 0, 2)
         subtract_woven(3, 0, a30)
         nc.gpsimd.tensor_tensor(grad_second[:, 0:K_PASS], res[3, 0][:], weight_second[:, 0, :], MULT)
         subtract_targets(2, 0, a20)
         subtract_woven(3, 1, a31)
-        subtract_targets(2, 1, a21)
         nc.vector.tensor_tensor(grad_second[:, K_PASS:V], res[3, 1][:], weight_second[:, 1, :], MULT)
+        subtract_targets(2, 1, a21)
         quantize_grad(g_cols(3, 0, 2), grad_second[:])
         part_a[0] = relay.tile([P, CHUNK], F32, name="part_a0", offset=2048)
         fetch_early(0, 0, 1, e0a, part_a[0][:])
@@ -423,22 +426,18 @@ def tile_attend_gml_sq_kernel(tc, xT, wd_words, wd_scales, wv_words, wv_scales, 
         scatter_early(0, 0)
         part_b0 = relay.tile([P, 3 * CHUNK], F32, name="part_b0", offset=2560)
         fetch_early(0, 1, 4, e0b, part_b0[:])
-        grad_turned = {(1, o): relay.tile([P, K_PASS], BF16, name=f"grad_turned{o}", offset=(4096, 7168)[o]) for o in range(PASSES)}
-        round_turned(1, 0, sum_first)
         weight[2, 1] = relay.tile([P, LANES, CHUNK], F32, name="weight21", offset=5120)[:]
         make_weight(2, 1, rw_third)
-        round_turned(1, 1, turn_and_add(1, 1, 1))
         grad_late = grads.tile([P, 4 * K_PASS], BF16, name="grad_late", offset=0, align_bytes=64)
         weigh_side(2, 0, grad_late[:, K_PASS : 2 * K_PASS])
         weigh_side(2, 1, grad_late[:, 3 * K_PASS : 4 * K_PASS])
-        t1 = back_early(3, 3)
+        t1 = back_early(3, 0)
         copy_early(3, 0, 1, t1)
-        turn_back(1, 0, 2, grad_late[:, 0:K_PASS])
-        e1a = turn_early(3, 0, 1, 0)
-        fetch_early(3, 0, 1, e1a, part_a[3][:])
-        dx_turned[3] = keep.tile([P, D], F32, name="dx_turned3_rest", tag="dx_turned3")
         copy_early(3, 1, 4, t1)
-        turn_back(1, 1, 2, grad_late[:, 2 * K_PASS : 3 * K_PASS])
+        turn_back(1, 0, 4, grad_late[:, 0:K_PASS])
+        e1a = turn_early(3, 0, 1, 2)
+        fetch_early(3, 0, 1, e1a, part_a[3][:])
+        turn_back(1, 1, 0, grad_late[:, 2 * K_PASS : 3 * K_PASS])
         e1b = turn_early(3, 1, 4, 5)
         part_b1 = relay.tile([P, 3 * CHUNK], F32, name="part_b1", offset=7680)
         fetch_early(3, 1, 4, e1b, part_b1[:])
@@ -447,7 +446,7 @@ def tile_attend_gml_sq_kernel(tc, xT, wd_words, wd_scales, wv_words, wv_scales, 
         scatter_early(3, 0)
         quantize_grad(slice(G_COLS[1, 0] * CHUNK, (G_COLS[2, 1] + 1) * CHUNK), grad_late[:])
         for j in range(D_TILES):
-            back_rest(j, (6, 7, 4, 1)[j], (1, 0))
+            back_rest(j, (6, 7, 3, 1)[j], (1, 0))
         for j in range(1, D_TILES):
             scatter_early(3, j)
         for j in range(D_TILES):

@@ -68,11 +68,13 @@ def tile_attend_gml_sq_kernel(tc, xT, wd_words, wd_scales, wv_words, wv_scales, 
         cw_neg = [
             neg.tile([P, LANES], F32, name="cw_neg0", offset=0, align_bytes=64),
             front.tile([P, PAIRS], F32, name="cw_neg1", offset=1536),
-            ys.tile([P, PAIRS], F32, name="cw_neg2", offset=0),
+            ys.tile([P, 1], F32, name="cw_neg2", offset=0),
+            keep.tile([P, 1], F32, name="cw_neg3"),
         ]
         neg_col = {(0, t): cw_neg[0][:, t : t + 1] for t in range(LANES)}
-        for t in range(LANES):
-            neg_col[1, t] = cw_neg[1 + t // 2][:, t % 2 : t % 2 + 1]
+        for t in range(PAIRS):
+            neg_col[1, t] = cw_neg[1][:, t : t + 1]
+            neg_col[1, PAIRS + t] = cw_neg[2 + t][:]
         rw_head = keep.tile([P, 2, CHUNK], F32, name="rw_head")
         rw_mid = keep.tile([P, CHUNK], F32, name="rw_mid")
         x_raw = [[keep.tile([P, 2, b - a], F32, name=f"x_raw{u}_{a}", tag=f"x_raw{u}_{a}", align_bytes=64) for a, b in X_PIECES[u]] for u in range(PAIRS)]
@@ -132,11 +134,11 @@ def tile_attend_gml_sq_kernel(tc, xT, wd_words, wd_scales, wv_words, wv_scales, 
                 wv_scales[:, 4 * q : 4 * q + 4, :].rearrange("o f d -> f o d").bitcast(I32),
             )
 
-        nc.sync.dma_start(offsets[:], offs)
         rw_chunks = rw.rearrange("p (c i) -> p c i", c=CHUNKS)
         nc.sync.dma_start(cw_sb, cw.rearrange("(o p t) one -> p o (t one)", o=PASSES, t=LANES))
         nc.sync.dma_start(rw_head[:], rw_chunks[:, 0:CHUNKS:3, :])
         load_x(0, 0)
+        nc.sync.dma_start(offsets[:], offs)
         for q in range(QUADRANTS):
             load_wd_scales(nc.sync, q)
         for k in range(len(X_PIECES[1])):
@@ -267,8 +269,8 @@ def tile_attend_gml_sq_kernel(tc, xT, wd_words, wd_scales, wv_words, wv_scales, 
 
         def turn_and_add(c, o, b):
             sum_bank = bank(b, [P, LANES, P], f"sum_bank{c}{o}")
-            for t in range(LANES):
-                nc.tensor.matmul(sum_bank[:, t, :], y_part[o, t], ident[:], start=(t == 0), stop=False, is_transpose=True)
+            for t in reversed(range(LANES)):
+                nc.tensor.matmul(sum_bank[:, t, :], y_part[o, t], ident[:], start=(t == LANES - 1), stop=False, is_transpose=True)
             for t in range(LANES):
                 nc.tensor.matmul(sum_bank[:, t, :], a_scaled[c, o][:, t, :], ident[:], start=False, stop=(t == LANES - 1), is_transpose=True)
             return sum_bank
@@ -350,8 +352,9 @@ def tile_attend_gml_sq_kernel(tc, xT, wd_words, wd_scales, wv_words, wv_scales, 
             nc.sync.dma_start(out[j * P : (j + 1) * P, :], windows[j][:])
 
         nc.scalar.mul(cw_neg[0][:], cw_sb[:, 0, :], -1.0)
-        for u in range(PAIRS):
-            nc.scalar.mul(cw_neg[1 + u][:], cw_sb[:, 1, 2 * u : 2 * u + 2], -1.0)
+        nc.scalar.mul(cw_neg[1][:], cw_sb[:, 1, 0:2], -1.0)
+        for t in range(PAIRS, LANES):
+            nc.scalar.mul(cw_neg[t][:], cw_sb[:, 1, t : t + 1], -1.0)
         for o in range(PASSES):
             make_weight(0, o, rw_head[:, 0, :])
         for o in range(PASSES):
@@ -391,7 +394,7 @@ def tile_attend_gml_sq_kernel(tc, xT, wd_words, wd_scales, wv_words, wv_scales, 
         a31 = product(3, 1, 6)
         a21 = product(2, 1, 7)
         scale_product(1, 0, a10)
-        scale_targets(1, 1, range(LANES))
+        scale_targets(1, 1, range(LANES - 1))
         scale_product(1, 1, a11)
         grad_early = [front.tile([P, K_PASS], BF16, name="grad_early0", offset=1536, align_bytes=64), keep.tile([P, K_PASS], BF16, name="grad_early1", align_bytes=64)]
         for o in range(PASSES):
@@ -400,16 +403,19 @@ def tile_attend_gml_sq_kernel(tc, xT, wd_words, wd_scales, wv_words, wv_scales, 
             quantize_grad(g_cols(0, o, o + 1), grad_early[o][:])
         res[3, 0] = front.tile([P, K_PASS], F32, name="res30", offset=0)
         res[2, 0] = front.tile([P, LANES, CHUNK], F32, name="res20", offset=2048)
-        res[3, 1] = relay.tile([P, 2 * K_PASS], F32, name="res31", offset=2048)[:, 0:K_PASS]
-        res[2, 1] = relay.tile([P, LANES, CHUNK], F32, name="res21", offset=8192)
+        res[3, 1] = relay.tile([P, 2 * K_PASS + 16], F32, name="res31", offset=2048)[:, 0:K_PASS]
+        res[2, 1] = relay.tile([P, LANES, CHUNK], F32, name="res21", offset=7168)
         rw_third = rw_mid[:]
         weight[2, 0] = ys.tile([P, LANES, CHUNK], F32, name="weight20", offset=0)[:]
         make_weight(2, 0, rw_third)
-        grad_turned = {(1, 0): keep.tile([P, K_PASS], BF16, name="grad_turned0"), (1, 1): relay.tile([P, K_PASS], BF16, name="grad_turned1", offset=7168)}
-        for o in range(PASSES):
-            round_turned(1, o, turn_and_add(1, o, 2 + o))
+        grad_turned = {(1, 0): keep.tile([P, K_PASS], BF16, name="grad_turned0")}
+        round_turned(1, 0, turn_and_add(1, 0, 2))
         grad_second = grads.tile([P, V], BF16, name="grad_second", offset=0, align_bytes=64)
         t0 = back_early(0, 0)
+        y_lane = keep.tile([P, CHUNK], F32, name="y_lane", tag="g_first0", align_bytes=64)
+        y_part[1, LANES - 1] = y_lane[:]
+        scale_targets(1, 1, range(LANES - 1, LANES))
+        sum_second = turn_and_add(1, 1, 3)
         copy_early(0, 0, 1, t0)
         copy_early(0, 1, 4, t0)
         e0a = turn_early(0, 0, 1, 1)
@@ -426,8 +432,10 @@ def tile_attend_gml_sq_kernel(tc, xT, wd_words, wd_scales, wv_words, wv_scales, 
         scatter_early(0, 0)
         part_b0 = relay.tile([P, 3 * CHUNK], F32, name="part_b0", offset=2560)
         fetch_early(0, 1, 4, e0b, part_b0[:])
-        weight[2, 1] = relay.tile([P, LANES, CHUNK], F32, name="weight21", offset=5120)[:]
+        weight[2, 1] = relay.tile([P, LANES, CHUNK], F32, name="weight21", offset=4096)[:]
         make_weight(2, 1, rw_third)
+        grad_turned[1, 1] = relay.tile([P, K_PASS], BF16, name="grad_turned1", offset=6144)
+        round_turned(1, 1, sum_second)
         grad_late = grads.tile([P, 4 * K_PASS], BF16, name="grad_late", offset=0, align_bytes=64)
         weigh_side(2, 0, grad_late[:, K_PASS : 2 * K_PASS])
         weigh_side(2, 1, grad_late[:, 3 * K_PASS : 4 * K_PASS])
@@ -439,7 +447,7 @@ def tile_attend_gml_sq_kernel(tc, xT, wd_words, wd_scales, wv_words, wv_scales, 
         fetch_early(3, 0, 1, e1a, part_a[3][:])
         turn_back(1, 1, 0, grad_late[:, 2 * K_PASS : 3 * K_PASS])
         e1b = turn_early(3, 1, 4, 5)
-        part_b1 = relay.tile([P, 3 * CHUNK], F32, name="part_b1", offset=7680)
+        part_b1 = relay.tile([P, 3 * CHUNK], F32, name="part_b1", offset=6656)
         fetch_early(3, 1, 4, e1b, part_b1[:])
         for j in range(1, D_TILES):
             scatter_early(0, j)

@@ -1,7 +1,6 @@
 from contextlib import ExitStack
 
 import concourse.mybir as mybir
-from concourse.masks import make_identity
 
 N, T, D, V = 512, 1024, 512, 1024
 FLOPS = 2 * 2 * N * D * V
@@ -17,12 +16,13 @@ E5M2 = mybir.dt.float8_e5m2_x4
 COPY = mybir.ActivationFunctionType.Copy
 MULT = mybir.AluOpType.mult
 SUB = mybir.AluOpType.subtract
+ADD = mybir.AluOpType.add
+EQUAL = mybir.AluOpType.is_equal
 
 P = 128
 LANES = 4
 K_PASS = P * LANES
 PASSES = V // K_PASS
-PAIRS = 2
 QUADRANTS = 4
 D_TILES = D // P
 CHUNK = 128
@@ -30,137 +30,149 @@ CHUNKS = N // CHUNK
 HALF = N // 2
 LIST_COLS = CHUNK // 16
 RUN = 2
-X_PIECES = (((0, 1024),), ((0, 512), (512, 1024)))
-EARLY = (0, 3)
-LATE = (1, 2)
-TURNED = ((1, 0), (1, 1))
-WEIGHTED = (0, 2, 3)
-G_COLS = {(0, 0): 0, (0, 1): 1, (3, 0): 2, (3, 1): 3, (1, 0): 4, (2, 0): 5, (1, 1): 6, (2, 1): 7}
-SIDE_RUN = 4
-SIDE = 128
-G_START = (2 * CHUNK, N)
+WEAVE_RUN = 4
 
 
 def tile_attend_gml_sq_kernel(tc, xT, wd_words, wd_scales, wv_words, wv_scales, y, cw, rw, offs, out):
     nc = tc.nc
     with ExitStack() as ctx:
         keep = ctx.enter_context(tc.tile_pool(name="keep", bufs=1))
-        relay = ctx.enter_context(tc.tile_pool(name="relay", bufs=1))
-        front = ctx.enter_context(tc.tile_pool(name="front", bufs=1))
-        mid = ctx.enter_context(tc.tile_pool(name="mid", bufs=1))
-        neg = ctx.enter_context(tc.tile_pool(name="neg", bufs=1))
-        ys = ctx.enter_context(tc.tile_pool(name="ys", bufs=1))
-        dts = ctx.enter_context(tc.tile_pool(name="dts", bufs=1))
+        head = ctx.enter_context(tc.tile_pool(name="head", bufs=1))
         late = ctx.enter_context(tc.tile_pool(name="late", bufs=1))
-        grads = ctx.enter_context(tc.tile_pool(name="grads", bufs=1))
         psum = ctx.enter_context(tc.psum_pool(name="psum", bufs=1))
 
         def bank(b, shape, name):
             return psum.tile(shape, F32, name=name, tag=f"bank{b}")
 
         offsets = keep.tile([P, N // 16], U16, name="offsets")
-        wd_raw = [keep.tile([P, K_PASS], I32, name=f"wd_raw{o}", tag=f"wd_raw{o}", align_bytes=64) for o in range(PASSES)]
+        wd_raw = [keep.tile([P, K_PASS], I32, name=f"wd_raw{o}", align_bytes=64) for o in range(PASSES)]
         wd_raw_scale = keep.tile([P, K_PASS], U8, name="wd_raw_scale", align_bytes=64)
         wd_codes = [keep.tile([P, K_PASS], I32, name=f"wd_codes{o}", align_bytes=64) for o in range(PASSES)]
-        wv_codes = keep.tile([P, PASSES, D], I32, name="wv_codes", align_bytes=64)
+        wd_scale = keep.tile([P, K_PASS], U8, name="wd_scale", align_bytes=64)
+        wv_codes = [keep.tile([P, PASSES, D // 2], I32, name=f"wv_codes{h}", align_bytes=64) for h in range(2)]
         wv_scale = keep.tile([P, PASSES, D], U8, name="wv_scale", align_bytes=64)
         cw_sb = keep.tile([P, PASSES, 2 * LANES], F32, name="cw_sb")[:, :, 0:LANES]
-        cw_neg = [
-            neg.tile([P, LANES], F32, name="cw_neg0", offset=0, align_bytes=64),
-            front.tile([P, PAIRS], F32, name="cw_neg1", offset=1536),
-            ys.tile([P, 1], F32, name="cw_neg2", offset=0),
-            keep.tile([P, 1], F32, name="cw_neg3"),
-        ]
-        neg_col = {(0, t): cw_neg[0][:, t : t + 1] for t in range(LANES)}
-        for t in range(PAIRS):
-            neg_col[1, t] = cw_neg[1][:, t : t + 1]
-            neg_col[1, PAIRS + t] = cw_neg[2 + t][:]
-        rw_head = keep.tile([P, 2, CHUNK], F32, name="rw_head")
-        rw_mid = keep.tile([P, CHUNK], F32, name="rw_mid")
-        x_raw = [[keep.tile([P, 2, b - a], F32, name=f"x_raw{u}_{a}", tag=f"x_raw{u}_{a}", align_bytes=64) for a, b in X_PIECES[u]] for u in range(PAIRS)]
-        rw_col = keep.tile([P, 1], F32, name="rw_col")
-        x_pairs = [keep.tile([P, T], U32, name=f"x_pairs{u}") for u in range(PAIRS)]
-        stage = mid.tile([P, 2 * HALF], U32, name="stage", offset=2048, align_bytes=64)
-        x_first = keep.tile([P, PAIRS, CHUNK], U32, name="x_first")
-        wd_scale = keep.tile([P, K_PASS], U8, name="wd_scale", tag="x_raw0_0", align_bytes=64)
-        x_second = stage[:].rearrange("p (u i) -> p u i", u=PAIRS)
-        listed_first = [stage[:, HALF:].rearrange("p (i u) -> p i u", u=PAIRS), keep.tile([P, CHUNK, PAIRS], U32, name="listed1", align_bytes=64)]
-        x_codes = keep.tile([P, N], U32, name="x_codes", align_bytes=64)
-        x_scale = keep.tile([P, N], U8, name="x_scale", align_bytes=64)
-        y_sb = [[keep.tile([P, LANES, HALF], F32, name=f"y_sb{h}{o}", tag=f"y_sb{h}{o}", align_bytes=64) for o in range(PASSES - h)] for h in range(2)]
-        y_last = {c: keep.tile([P, LANES, CHUNK], F32, name=f"y_last{c}") for c in (2, 3)}
-        weight_first = keep.tile([P, LANES, PASSES, CHUNK], F32, name="weight_first")
-        weight = {(0, o): weight_first[:, :, o, :] for o in range(PASSES)}
-        weight_second = keep.tile([P, PASSES, K_PASS], F32, name="weight_second")
-        a_scaled = {(1, o): mid.tile([P, LANES, CHUNK], F32, name=f"a_scaled{o}", offset=1024 + 2048 * o) for o in range(PASSES)}
-        y_scaled = {(1, 0): keep.tile([P, LANES, CHUNK], F32, name="y_scaled0"), (1, 1): keep.tile([P, LANES, CHUNK], F32, name="y_scaled1")}
-        y_part = {(o, t): y_scaled[1, o][:, t, :] for o in range(PASSES) for t in range(LANES)}
-        g_first = [keep.tile([P, CHUNK], U32, name=f"g_first{o}", tag=f"g_first{o}", align_bytes=64) for o in range(PASSES)]
-        part_a = {3: keep.tile([P, CHUNK], F32, name="part_a3")}
-        g_codes = late.tile([P, PASSES * N - HALF], U32, name="g_codes", offset=0, align_bytes=64)
-        g_scale = keep.tile([P, PASSES * N], U8, name="g_scale", align_bytes=64)
-        dx_turned = {0: dts.tile([P, D], F32, name="dx_turned0", offset=0), 3: keep.tile([P, D], F32, name="dx_turned3", tag="dx_turned3")}
-        dx_early = {}
-        dx_rest = [keep.tile([P, len(LATE) * CHUNK], F32, name=f"dx_rest{j}") for j in range(D_TILES)]
+        rw_cols = head.tile([P, LANES], F32, name="rw_cols", offset=768, align_bytes=64)
+        rw_sb = keep.tile([P, N], F32, name="rw_sb")
+        x_planes = [keep.tile([P, T], F32, name=f"x_plane{t}") for t in range(LANES)]
+        x_first = keep.tile([P, CHUNK, LANES], BF16, name="x_first", align_bytes=64)
+        x_rest = head.tile([P, LANES, N - CHUNK], BF16, name="x_rest", offset=0, align_bytes=64)
+        x_second = keep.tile([P, CHUNK, LANES], BF16, name="x_second", align_bytes=64)
+        x_late = keep.tile([P, HALF, LANES], BF16, name="x_late", align_bytes=64)
+        x_groups = ((0, 1), (1, 2), (2, CHUNKS))
+        x_codes = {c0: keep.tile([P, (c1 - c0) * CHUNK], U32, name=f"x_codes{c0}", align_bytes=64) for c0, c1 in x_groups}
+        x_scale = {c0: keep.tile([P, (c1 - c0) * CHUNK], U8, name=f"x_scale{c0}", align_bytes=64) for c0, c1 in x_groups}
+        y_sb = {(c, o): keep.tile([P, LANES, CHUNK], F32, name=f"y_sb{c}{o}") for c in range(CHUNKS) for o in range(PASSES) if c < 2 or o == 1}
+        y_pair = keep.tile([P, LANES, HALF], F32, name="y_pair")
+        weight = [keep.tile([P, PASSES, LANES, HALF], F32, name="weight0")]
+        res = {}
+        grad = [keep.tile([P, PASSES, K_PASS], BF16, name=f"grad{c}", align_bytes=64) for c in range(CHUNKS)]
+        g_codes = [keep.tile([P, PASSES * CHUNK], U32, name=f"g_codes{c}", align_bytes=64) for c in range(CHUNKS)]
+        g_scale = [keep.tile([P, PASSES * CHUNK], U8, name=f"g_scale{c}", align_bytes=64) for c in range(CHUNKS)]
+        dx = keep.tile([P, D_TILES, N], F32, name="dx")
         windows = [keep.tile([P, T], F32, name=f"window{j}") for j in range(D_TILES)]
         ident = keep.tile([P, P], F32, name="ident")
 
         nc.gpsimd.memset(wd_raw_scale[:].bitcast(I32), 0)
         nc.gpsimd.memset(wv_scale[:].rearrange("p o d -> p (o d)").bitcast(I32), 0)
+        ones = keep.tile([P, 32], F32, name="ones")
+        by_column = keep.tile([P, 32], F32, name="by_column", align_bytes=64)
+        by_partition = keep.tile([P, 32], F32, name="by_partition", align_bytes=64)
+        nc.vector.memset(ones[:], 1.0)
+        nc.vector.memset(ident[:], 0.0)
+        nc.vector.tensor_tensor_scan(by_column[:], ones[:], ones[:], 0.0, MULT, ADD)
+        nc.vector.transpose(by_partition[:], by_column[:])
+        for q in range(QUADRANTS):
+            rows = slice(32 * q, 32 * q + 32)
+            nc.vector.tensor_tensor(ident[rows, rows], by_column[rows, :], by_partition[rows, :], EQUAL)
 
-        x_rows = xT.rearrange("(p u e) c -> u p e c", u=PAIRS, e=2)
+        x_rows = xT.rearrange("(p t) c -> t p c", t=LANES)
         y_rows = y.rearrange("(o p t) i -> o p t i", o=PASSES, t=LANES)
+        wd_rows = wd_words[0].rearrange("p v t -> p (v t)").bitcast(I32)
+        wv_rows = wv_words.rearrange("o p d t -> p o (d t)").bitcast(I32)
 
-        def load_x(u, k):
-            a, b = X_PIECES[u][k]
-            nc.sync.dma_start(x_raw[u][k][:], x_rows[u][:, :, a:b])
+        def load_x(t):
+            nc.sync.dma_start(x_planes[t][:], x_rows[t])
 
         def load_wd(o):
-            words = wd_words[0].rearrange("p v t -> p (v t)").bitcast(I32)
-            nc.sync.dma_start(wd_raw[o][:], words[:, o * K_PASS : (o + 1) * K_PASS])
+            nc.sync.dma_start(wd_raw[o][:], wd_rows[:, o * K_PASS : (o + 1) * K_PASS])
 
-        def load_y(h, o, queue=nc.sync):
-            queue.dma_start(y_sb[h][o][:], y_rows[o][:, :, h * HALF : (h + 1) * HALF])
+        def load_y(c, o):
+            nc.sync.dma_start(y_sb[c, o][:], y_rows[o][:, :, c * CHUNK : (c + 1) * CHUNK])
 
-        def load_wd_scales(queue, q):
-            queue.dma_start(
+        def load_wv(h):
+            nc.sync.dma_start(wv_codes[h][:], wv_rows[:, :, h * (D // 2) : (h + 1) * (D // 2)])
+
+        nc.sync.dma_start(rw_cols[:], rw[0, :].rearrange("(p j) -> p j", j=LANES))
+        load_x(0)
+        nc.sync.dma_start(cw_sb, cw.rearrange("(o p t) one -> p o (t one)", o=PASSES, t=LANES))
+        nc.sync.dma_start(offsets[:], offs)
+        load_x(1)
+        load_x(2)
+        for q in range(QUADRANTS):
+            nc.sync.dma_start(
                 wd_raw_scale[32 * q : 32 * q + 4 * PASSES, :].bitcast(I32),
                 wd_scales[0, 4 * q : 4 * q + 4, :].bitcast(I32).rearrange("f (o c) -> o f c", o=PASSES),
             )
-
-        def load_wv_scales(queue, q):
-            queue.dma_start(
+        load_x(3)
+        load_wd(0)
+        load_y(0, 0)
+        load_wd(1)
+        load_y(0, 1)
+        for q in range(QUADRANTS):
+            nc.sync.dma_start(
                 wv_scale[32 * q : 32 * q + 4, :, :].bitcast(I32),
                 wv_scales[:, 4 * q : 4 * q + 4, :].rearrange("o f d -> f o d").bitcast(I32),
             )
-
-        rw_chunks = rw.rearrange("p (c i) -> p c i", c=CHUNKS)
-        nc.sync.dma_start(cw_sb, cw.rearrange("(o p t) one -> p o (t one)", o=PASSES, t=LANES))
-        nc.sync.dma_start(rw_head[:], rw_chunks[:, 0:CHUNKS:3, :])
-        load_x(0, 0)
-        nc.sync.dma_start(offsets[:], offs)
-        for q in range(QUADRANTS):
-            load_wd_scales(nc.sync, q)
-        for k in range(len(X_PIECES[1])):
-            load_x(1, k)
-        load_wd(0)
-        load_wd(1)
-        load_y(0, 0)
-        load_y(0, 1)
-        nc.sync.dma_start(rw_mid[:], rw_chunks[:, 2, :])
-        nc.sync.dma_start(rw_col[:], rw[0, CHUNK : 2 * CHUNK].rearrange("(p one) -> p one", one=1))
+        load_wv(0)
         load_y(1, 0)
-        for q in range(QUADRANTS):
-            load_wv_scales(nc.sync, q)
-        nc.sync.dma_start(wv_codes[:], wv_words.rearrange("o p d t -> p o (d t)").bitcast(I32))
-        nc.sync.dma_start(y_last[3][:], y_rows[1][:, :, 3 * CHUNK : 4 * CHUNK])
-        for u in range(PAIRS):
-            nc.sync.dma_start(y_last[2][:, 2 * u : 2 * u + 2, :], y_rows[1][:, 2 * u : 2 * u + 2, 2 * CHUNK : 3 * CHUNK])
+        load_y(1, 1)
+        load_wv(1)
+        nc.sync.dma_start(y_pair[:], y_rows[0][:, :, HALF:N])
+        load_y(2, 1)
+        load_y(3, 1)
 
-        make_identity(nc, ident[:])
-        for j in range(D_TILES - 1):
+        for j in range(2):
             nc.vector.memset(windows[j][:].bitcast(I32), 0)
-        nc.gpsimd.memset(windows[D_TILES - 1][:].bitcast(I32), 0)
+
+        rw_bank = bank(7, [P, LANES, P], "rw_bank")
+        for j in range(LANES):
+            nc.tensor.transpose(rw_bank[:, j, :], rw_cols[:, j : j + 1].to_broadcast([P, P]), ident[:])
+        nc.scalar.activation(rw_sb[:].rearrange("p (m j) -> p m j", j=LANES), rw_bank[:].rearrange("p j m -> p m j"), COPY)
+
+        nc.gpsimd.tensor_copy(
+            wd_scale[:].rearrange("p (t m) -> p t m", t=LANES),
+            wd_raw_scale[:].rearrange("p (m t) -> p t m", t=LANES),
+        )
+        for j in range(2, D_TILES):
+            nc.gpsimd.memset(windows[j][:].bitcast(I32), 0)
+
+        def listed(c0, c1):
+            return offsets[:, c0 * LIST_COLS : c1 * LIST_COLS]
+
+        def gather_first(t):
+            nc.vector.tensor_copy(x_first[:, :, t], x_planes[t][:].indirect(listed(0, 1)))
+
+        def gather_rest(t, c0, c1):
+            dst = x_rest[:, t, (c0 - 1) * CHUNK : (c1 - 1) * CHUNK]
+            if t == 0:
+                nc.vector.tensor_copy(dst, x_planes[t][:].indirect(listed(c0, c1)))
+            else:
+                nc.scalar.activation(dst, x_planes[t][:].indirect(listed(c0, c1)), COPY)
+
+        def weave(dst, c0, c1):
+            nc.scalar.copy(
+                dst.rearrange("p (r i) t -> p r t i", i=WEAVE_RUN),
+                x_rest[:, :, (c0 - 1) * CHUNK : (c1 - 1) * CHUNK].rearrange("p t (r i) -> p r t i", i=WEAVE_RUN),
+            )
+
+        def make_weight(h, o, on_scalar):
+            src = rw_sb[:, h * HALF : (h + 1) * HALF]
+            for t in range(LANES):
+                if on_scalar:
+                    nc.scalar.activation(weight[h][:, o, t, :], src, COPY, scale=cw_sb[:, o, t : t + 1])
+                else:
+                    nc.vector.tensor_scalar(weight[h][:, o, t, :], src, cw_sb[:, o, t : t + 1], None, MULT)
 
         def reorder_wd(o):
             nc.vector.tensor_copy(
@@ -168,294 +180,155 @@ def tile_attend_gml_sq_kernel(tc, xT, wd_words, wd_scales, wv_words, wv_scales, 
                 wd_raw[o][:].rearrange("p (m t) -> p m t", t=LANES),
             )
 
-        def reorder_wd_scale():
-            nc.gpsimd.tensor_copy(
-                wd_scale[:].rearrange("p (t m) -> p t m", t=LANES),
-                wd_raw_scale[:].rearrange("p (m t) -> p t m", t=LANES),
-            )
-
-        def cast_x(u, k, a, b, on_scalar):
-            first = X_PIECES[u][k][0]
-            dst = x_pairs[u][:, a:b].bitcast(BF16).rearrange("p (c e) -> p c e", e=2)
-            src = x_raw[u][k][:, :, a - first : b - first].rearrange("p e c -> p c e")
-            if on_scalar:
-                nc.scalar.activation(dst, src, COPY)
-            else:
-                nc.vector.tensor_copy(dst, src)
-
-        def make_weight(c, o, src):
-            for t in range(LANES):
-                nc.scalar.activation(weight[c, o][:, t, :], src, COPY, scale=cw_sb[:, o, t : t + 1])
-
-        def make_weight_woven(o, src):
-            shape = [P, CHUNK, LANES]
-            nc.vector.tensor_tensor(
-                weight_second[:, o, :].rearrange("p (i t) -> p i t", t=LANES),
-                src.unsqueeze(2).broadcast_to(shape),
-                cw_sb[:, o, :].unsqueeze(1).broadcast_to(shape),
-                MULT,
-            )
-
-        def gather(dst, u, c0, c1):
-            nc.vector.tensor_copy(dst, x_pairs[u][:].indirect(offsets[:, c0 * LIST_COLS : c1 * LIST_COLS]))
-
-        def weave(dst, src, on_scalar=True):
-            if on_scalar:
-                nc.scalar.copy(dst, src.rearrange("p u i -> p i u"))
-            else:
-                nc.vector.tensor_copy(dst.bitcast(I32), src.bitcast(I32).rearrange("p u i -> p i u"))
-
-        def quantize_x(c0, c1, src):
-            cols = slice(c0 * CHUNK, c1 * CHUNK)
-            nc.vector.quantize_mx(
-                out=x_codes[:, cols].bitcast(E4M3),
-                scales=x_scale[:, cols],
-                in_=src.rearrange("p i u -> p (i u)").bitcast(BF16),
-            )
+        def quantize_x(c0, src):
+            nc.vector.quantize_mx(out=x_codes[c0][:].bitcast(E4M3), scales=x_scale[c0][:], in_=src.rearrange("p i t -> p (i t)"))
 
         def product(c, o, b):
-            cols = slice(c * CHUNK, (c + 1) * CHUNK)
+            c0 = min(c, 2)
+            cols = slice((c - c0) * CHUNK, (c - c0 + 1) * CHUNK)
             a_bank = bank(b, [P, LANES, CHUNK], f"a_bank{c}{o}")
             for t in range(LANES):
                 nc.tensor.matmul_mx(
                     out=a_bank[:, t, :],
                     lhsT=wd_codes[o][:, t * P : (t + 1) * P].bitcast(E4M3),
                     lhsT_scale=wd_scale[4 * o : P, t * P : (t + 1) * P],
-                    rhs=x_codes[:, cols].bitcast(E4M3),
-                    rhs_scale=x_scale[:, cols],
+                    rhs=x_codes[c0][:, cols].bitcast(E4M3),
+                    rhs_scale=x_scale[c0][:, cols],
                     start=True,
                     stop=True,
                 )
             return a_bank
 
         def y_of(c, o):
+            if (c, o) in y_sb:
+                return y_sb[c, o][:]
+            return y_pair[:, :, (c - 2) * CHUNK : (c - 1) * CHUNK]
+
+        def subtract(c, o, a_bank):
+            res[c, o] = late.tile([P, LANES, CHUNK], F32, name=f"res{c}{o}", offset=4096 * o)
+            nc.vector.tensor_tensor(res[c, o][:], a_bank[:], y_of(c, o), SUB)
+
+        def weigh(c, o):
             h, within = divmod(c * CHUNK, HALF)
-            if h and o:
-                return y_last[c][:]
-            return y_sb[h][o][:, :, within : within + CHUNK]
-
-        def residual(c0, c1, o):
-            return res[c0, o][:]
-
-        def subtract_targets(c, o, a_bank):
-            nc.vector.tensor_tensor(residual(c, c + 1, o), a_bank[:], y_of(c, o), SUB)
-
-        def subtract_woven(c, o, a_bank):
             nc.vector.tensor_tensor(
-                res[c, o][:].rearrange("p (r i t) -> p r t i", i=SIDE_RUN, t=LANES),
-                a_bank[:].rearrange("p t (r i) -> p r t i", i=SIDE_RUN),
-                y_of(c, o).rearrange("p t (r i) -> p r t i", i=SIDE_RUN),
-                SUB,
-            )
-
-        def weigh(dst, residuals, weights, engine, run):
-            engine.tensor_tensor(
-                dst.rearrange("p (r i t) -> p r t i", i=run, t=LANES),
-                residuals.rearrange("p t (r i) -> p r t i", i=run),
-                weights.rearrange("p t (r i) -> p r t i", i=run),
+                grad[c][:, o, :].rearrange("p (r i t) -> p r t i", i=RUN, t=LANES),
+                res[c, o][:].rearrange("p t (r i) -> p r t i", i=RUN),
+                weight[h][:, o, :, within : within + CHUNK].rearrange("p t (r i) -> p r t i", i=RUN),
                 MULT,
             )
 
-        def weigh_side(c, o, dst):
-            weigh(dst, res[c, o][:], weight[c, o], nc.gpsimd, SIDE_RUN)
+        def quantize_grad(c):
+            nc.vector.quantize_mx(out=g_codes[c][:].bitcast(E5M2), scales=g_scale[c][:], in_=grad[c][:].rearrange("p o k -> p (o k)"))
 
-        def scale_targets(c, o, lanes):
-            for t in lanes:
-                nc.scalar.activation(y_part[o, t], y_of(c, o)[:, t, :], COPY, scale=neg_col[o, t])
+        def back(c, h, b):
+            dx_bank = bank(b, [P, 2, CHUNK], f"dx_bank{c}{h}")
+            for jj in range(2):
+                j = 2 * h + jj
+                for o in range(PASSES):
+                    nc.tensor.matmul_mx(
+                        out=dx_bank[:, jj, :],
+                        lhsT=wv_codes[h][:, o, jj * P : (jj + 1) * P].bitcast(E4M3),
+                        lhsT_scale=wv_scale[:, o, j * P : (j + 1) * P],
+                        rhs=g_codes[c][:, o * CHUNK : (o + 1) * CHUNK].bitcast(E5M2),
+                        rhs_scale=g_scale[c][:, o * CHUNK : (o + 1) * CHUNK],
+                        start=(o == 0),
+                        stop=(o == PASSES - 1),
+                    )
+            return dx_bank
 
-        def scale_product(c, o, a_bank):
-            for t in range(LANES):
-                nc.scalar.activation(a_scaled[c, o][:, t, :], a_bank[:, t, :], COPY, scale=cw_sb[:, o, t : t + 1])
+        def fetch(dst, dx_bank, on_scalar):
+            if on_scalar:
+                nc.scalar.copy(dst, dx_bank[:])
+            else:
+                nc.vector.tensor_copy(dst, dx_bank[:])
 
-        def turn_and_add(c, o, b):
-            sum_bank = bank(b, [P, LANES, P], f"sum_bank{c}{o}")
-            for t in reversed(range(LANES)):
-                nc.tensor.matmul(sum_bank[:, t, :], y_part[o, t], ident[:], start=(t == LANES - 1), stop=False, is_transpose=True)
-            for t in range(LANES):
-                nc.tensor.matmul(sum_bank[:, t, :], a_scaled[c, o][:, t, :], ident[:], start=False, stop=(t == LANES - 1), is_transpose=True)
-            return sum_bank
+        def dx_cols(c, h):
+            return dx[:, 2 * h : 2 * h + 2, c * CHUNK : (c + 1) * CHUNK]
 
-        def round_turned(c, o, sum_bank):
-            nc.scalar.activation(
-                grad_turned[c, o][:].rearrange("i (u p e) -> i u p e", u=PAIRS, e=2),
-                sum_bank[:].rearrange("i (u e) p -> i u p e", u=PAIRS),
-                COPY,
-                scale=rw_col[:],
-            )
+        def scatter(j, c0, c1, src, on_scalar):
+            window = windows[j][:].indirect(listed(c0, c1))
+            if on_scalar:
+                nc.scalar.activation(window, src, COPY)
+            else:
+                nc.vector.tensor_copy(window, src)
 
-        def turn_back(c, o, b, dst):
-            word_bank = bank(b, [P, PAIRS, CHUNK], f"word_bank{c}{o}")
-            words = grad_turned[c, o][:].bitcast(F32)
-            for u in range(PAIRS):
-                nc.tensor.transpose(word_bank[:, u, :], words[:, u * P : (u + 1) * P], ident[:])
-            nc.scalar.copy(
-                dst.bitcast(F32).rearrange("p (i u) -> p i u", u=PAIRS),
-                word_bank[:].rearrange("p u i -> p i u"),
-            )
+        def scatter_dx(j, c0, c1, on_scalar):
+            scatter(j, c0, c1, dx[:, j, c0 * CHUNK : c1 * CHUNK], on_scalar)
 
-        def g_cols(c, o0, o1):
-            return slice(G_COLS[c, o0] * CHUNK, (G_COLS[c, o1 - 1] + 1) * CHUNK)
-
-        def g_words(cols):
-            return g_first[cols.start // CHUNK][:] if cols.start < HALF else g_codes[:, cols.start - HALF : cols.stop - HALF]
-
-        def quantize_grad(cols, src):
-            nc.vector.quantize_mx(out=g_words(cols).bitcast(E5M2), scales=g_scale[:, cols], in_=src)
-
-        def back_early(c, b0):
-            turned_bank = bank(b0, [P, D], f"turned_bank{c}")
-            for o in range(PASSES):
-                nc.tensor.matmul_mx(
-                    out=turned_bank[:],
-                    lhsT=g_words(g_cols(c, o, o + 1)).bitcast(E5M2),
-                    lhsT_scale=g_scale[:, g_cols(c, o, o + 1)],
-                    rhs=wv_codes[:, o, :].bitcast(E4M3),
-                    rhs_scale=wv_scale[:, o, :],
-                    start=(o == 0),
-                    stop=(o == PASSES - 1),
-                )
-            return turned_bank
-
-        def copy_early(c, j0, j1, turned_bank):
-            nc.scalar.copy(dx_turned[c][:, j0 * P : j1 * P], turned_bank[:, j0 * P : j1 * P])
-
-        def turn_early(c, j0, j1, b1):
-            early_bank = bank(b1, [P, j1 - j0, CHUNK], f"early_bank{c}{j0}")
-            for j in range(j0, j1):
-                nc.tensor.transpose(early_bank[:, j - j0, :], dx_turned[c][:, j * P : (j + 1) * P], ident[:])
-            return early_bank
-
-        def fetch_early(c, j0, j1, early_bank, part):
-            nc.scalar.copy(part, early_bank[:].rearrange("p j i -> p (j i)"))
-            for j in range(j0, j1):
-                dx_early[c, j] = part[:, (j - j0) * CHUNK : (j - j0 + 1) * CHUNK]
-
-        def back_rest(j, b, passes):
-            dx_bank = bank(b, [P, N], f"dx_bank{j}")
-            for o in passes:
-                nc.tensor.matmul_mx(
-                    out=dx_bank[:],
-                    lhsT=wv_codes[:, o, j * P : (j + 1) * P].bitcast(E4M3),
-                    lhsT_scale=wv_scale[:, o, j * P : (j + 1) * P],
-                    rhs=g_words(slice(G_START[o], G_START[o] + N)).bitcast(E5M2),
-                    rhs_scale=g_scale[:, G_START[o] : G_START[o] + N],
-                    start=(o == passes[0]),
-                    stop=(o == passes[-1]),
-                )
-            nc.scalar.copy(dx_rest[j][:], dx_bank[:, N - len(LATE) * CHUNK : N])
-
-        def scatter_early(c, j):
-            nc.vector.tensor_copy(windows[j][:].indirect(offsets[:, c * LIST_COLS : (c + 1) * LIST_COLS]), dx_early[c, j])
-
-        def scatter_rest_and_store(j):
-            nc.vector.tensor_copy(windows[j][:].indirect(offsets[:, LATE[0] * LIST_COLS : (LATE[-1] + 1) * LIST_COLS]), dx_rest[j][:])
+        def store(j):
             nc.sync.dma_start(out[j * P : (j + 1) * P, :], windows[j][:])
 
-        nc.scalar.mul(cw_neg[0][:], cw_sb[:, 0, :], -1.0)
-        nc.scalar.mul(cw_neg[1][:], cw_sb[:, 1, 0:2], -1.0)
-        for t in range(PAIRS, LANES):
-            nc.scalar.mul(cw_neg[t][:], cw_sb[:, 1, t : t + 1], -1.0)
-        for o in range(PASSES):
-            make_weight(0, o, rw_head[:, 0, :])
-        for o in range(PASSES):
-            make_weight_woven(o, rw_head[:, 1, :])
-        cast_x(0, 0, 0, 384, True)
-        cast_x(0, 0, 384, 1024, False)
-        reorder_wd_scale()
-        gather(listed_first[0][:, :, 0], 0, 0, 1)
-        gather(x_first[:, 0, :], 0, 1, 2)
-        gather(x_second[:, 0, :], 0, 2, 4)
-        cast_x(1, 0, 0, 512, True)
-        cast_x(1, 1, 512, 704, True)
-        cast_x(1, 1, 704, 1024, False)
-
-        gather(listed_first[0][:, :, 1], 1, 0, 1)
+        for t in range(LANES - 1):
+            gather_first(t)
+            gather_rest(t, 1, CHUNKS)
+            if t < PASSES:
+                make_weight(0, t, False)
+        gather_first(LANES - 1)
         reorder_wd(0)
-        gather(x_first[:, 1, :], 1, 1, 2)
-        weave(listed_first[1][:], x_first[:])
-        quantize_x(0, 1, listed_first[0])
+        quantize_x(0, x_first[:])
         a00 = product(0, 0, 0)
         reorder_wd(1)
         a01 = product(0, 1, 1)
-        gather(x_second[:, 1, :], 1, 2, 4)
-        quantize_x(1, 2, listed_first[1][:])
+        gather_rest(LANES - 1, 1, 2)
+        weave(x_second[:], 1, 2)
+        gather_rest(LANES - 1, 2, CHUNKS)
+        weave(x_late[:], 2, CHUNKS)
+        weight.append(head.tile([P, PASSES, LANES, HALF], F32, name="weight1", offset=0, align_bytes=64))
+        for o in range(PASSES):
+            make_weight(1, o, True)
+        subtract(0, 0, a00)
+        quantize_x(1, x_second[:])
         a10 = product(1, 0, 2)
         a11 = product(1, 1, 3)
-        res_first = keep.tile([P, LANES, PASSES, CHUNK], F32, name="res_first")
-        res = {(0, o): res_first[:, :, o, :] for o in range(PASSES)}
-        scale_targets(1, 0, range(LANES))
-        listed_second = neg.tile([P, HALF, PAIRS], U32, name="listed_second", offset=0, align_bytes=64)
-        weave(listed_second[:], x_second)
-        subtract_targets(0, 0, a00)
-        subtract_targets(0, 1, a01)
-        quantize_x(2, 4, listed_second[:])
-        a30 = product(3, 0, 4)
-        a20 = product(2, 0, 5)
-        a31 = product(3, 1, 6)
-        a21 = product(2, 1, 7)
-        scale_product(1, 0, a10)
-        scale_targets(1, 1, range(LANES - 1))
-        scale_product(1, 1, a11)
-        grad_early = [front.tile([P, K_PASS], BF16, name="grad_early0", offset=1536, align_bytes=64), keep.tile([P, K_PASS], BF16, name="grad_early1", align_bytes=64)]
-        for o in range(PASSES):
-            weigh(grad_early[o][:], res[0, o], weight[0, o], nc.vector, RUN)
-        for o in range(PASSES):
-            quantize_grad(g_cols(0, o, o + 1), grad_early[o][:])
-        res[3, 0] = front.tile([P, K_PASS], F32, name="res30", offset=0)
-        res[2, 0] = front.tile([P, LANES, CHUNK], F32, name="res20", offset=2048)
-        res[3, 1] = relay.tile([P, 2 * K_PASS + 16], F32, name="res31", offset=2048)[:, 0:K_PASS]
-        res[2, 1] = relay.tile([P, LANES, CHUNK], F32, name="res21", offset=7168)
-        rw_third = rw_mid[:]
-        weight[2, 0] = ys.tile([P, LANES, CHUNK], F32, name="weight20", offset=0)[:]
-        make_weight(2, 0, rw_third)
-        grad_turned = {(1, 0): keep.tile([P, K_PASS], BF16, name="grad_turned0")}
-        round_turned(1, 0, turn_and_add(1, 0, 2))
-        grad_second = grads.tile([P, V], BF16, name="grad_second", offset=0, align_bytes=64)
-        t0 = back_early(0, 0)
-        y_lane = keep.tile([P, CHUNK], F32, name="y_lane", tag="g_first0", align_bytes=64)
-        y_part[1, LANES - 1] = y_lane[:]
-        scale_targets(1, 1, range(LANES - 1, LANES))
-        sum_second = turn_and_add(1, 1, 3)
-        copy_early(0, 0, 1, t0)
-        copy_early(0, 1, 4, t0)
-        e0a = turn_early(0, 0, 1, 1)
-        subtract_woven(3, 0, a30)
-        nc.gpsimd.tensor_tensor(grad_second[:, 0:K_PASS], res[3, 0][:], weight_second[:, 0, :], MULT)
-        subtract_targets(2, 0, a20)
-        subtract_woven(3, 1, a31)
-        nc.vector.tensor_tensor(grad_second[:, K_PASS:V], res[3, 1][:], weight_second[:, 1, :], MULT)
-        subtract_targets(2, 1, a21)
-        quantize_grad(g_cols(3, 0, 2), grad_second[:])
-        part_a[0] = relay.tile([P, CHUNK], F32, name="part_a0", offset=2048)
-        fetch_early(0, 0, 1, e0a, part_a[0][:])
-        e0b = turn_early(0, 1, 4, 4)
-        scatter_early(0, 0)
-        part_b0 = relay.tile([P, 3 * CHUNK], F32, name="part_b0", offset=2560)
-        fetch_early(0, 1, 4, e0b, part_b0[:])
-        weight[2, 1] = relay.tile([P, LANES, CHUNK], F32, name="weight21", offset=4096)[:]
-        make_weight(2, 1, rw_third)
-        grad_turned[1, 1] = relay.tile([P, K_PASS], BF16, name="grad_turned1", offset=6144)
-        round_turned(1, 1, sum_second)
-        grad_late = grads.tile([P, 4 * K_PASS], BF16, name="grad_late", offset=0, align_bytes=64)
-        weigh_side(2, 0, grad_late[:, K_PASS : 2 * K_PASS])
-        weigh_side(2, 1, grad_late[:, 3 * K_PASS : 4 * K_PASS])
-        t1 = back_early(3, 0)
-        copy_early(3, 0, 1, t1)
-        copy_early(3, 1, 4, t1)
-        turn_back(1, 0, 4, grad_late[:, 0:K_PASS])
-        e1a = turn_early(3, 0, 1, 2)
-        fetch_early(3, 0, 1, e1a, part_a[3][:])
-        turn_back(1, 1, 0, grad_late[:, 2 * K_PASS : 3 * K_PASS])
-        e1b = turn_early(3, 1, 4, 5)
-        part_b1 = relay.tile([P, 3 * CHUNK], F32, name="part_b1", offset=6656)
-        fetch_early(3, 1, 4, e1b, part_b1[:])
-        for j in range(1, D_TILES):
-            scatter_early(0, j)
-        scatter_early(3, 0)
-        quantize_grad(slice(G_COLS[1, 0] * CHUNK, (G_COLS[2, 1] + 1) * CHUNK), grad_late[:])
-        for j in range(D_TILES):
-            back_rest(j, (6, 7, 3, 1)[j], (1, 0))
-        for j in range(1, D_TILES):
-            scatter_early(3, j)
-        for j in range(D_TILES):
-            scatter_rest_and_store(j)
+        subtract(0, 1, a01)
+        weigh(0, 0)
+        quantize_x(2, x_late[:])
+        a20 = product(2, 0, 0)
+        a21 = product(2, 1, 1)
+        weigh(0, 1)
+        subtract(1, 0, a10)
+        quantize_grad(0)
+        for h in range(2):
+            fetch(dx_cols(0, h), back(0, h, 4 + h), True)
+            for jj in range(2):
+                scatter_dx(2 * h + jj, 0, 1, True)
+        subtract(1, 1, a11)
+        a30 = product(3, 0, 2)
+        a31 = product(3, 1, 3)
+        weigh(1, 0)
+        weigh(1, 1)
+        subtract(2, 0, a20)
+        quantize_grad(1)
+        fetch(dx_cols(1, 0), back(1, 0, 6), True)
+        for j in range(2):
+            scatter_dx(j, 1, 2, True)
+        b1 = back(1, 1, 7)
+        subtract(2, 1, a21)
+        weigh(2, 0)
+        weigh(2, 1)
+        subtract(3, 0, a30)
+        quantize_grad(2)
+        fetch(dx_cols(2, 0), back(2, 0, 4), True)
+        for j in range(2):
+            scatter_dx(j, 2, 3, True)
+        b2 = back(2, 1, 5)
+        subtract(3, 1, a31)
+        weigh(3, 0)
+        weigh(3, 1)
+        dx_late = late.tile([P, 2, N - CHUNK], F32, name="dx_late", offset=0)
+        fetch(dx_late[:, :, 0:CHUNK], b1, False)
+        quantize_grad(3)
+        a3 = back(3, 0, 6)
+        b3 = back(3, 1, 0)
+        scatter(2, 1, 2, dx_late[:, 0, 0:CHUNK], False)
+        fetch(dx_late[:, :, CHUNK : 2 * CHUNK], b2, True)
+        fetch(dx_cols(3, 0), a3, False)
+        scatter_dx(1, 3, 4, False)
+        store(1)
+        scatter_dx(0, 3, 4, True)
+        store(0)
+        fetch(dx_late[:, :, 2 * CHUNK : 3 * CHUNK], b3, True)
+        scatter(2, 2, 4, dx_late[:, 0, CHUNK : 3 * CHUNK], True)
+        store(2)
+        scatter(3, 1, 4, dx_late[:, 1, :], False)
+        store(3)

from contextlib import ExitStack

import concourse.mybir as mybir

N, T, D, V = 512, 1024, 512, 1024
FLOPS = 2 * 2 * N * D * V

F32 = mybir.dt.float32
BF16 = mybir.dt.bfloat16
I32 = mybir.dt.int32
U32 = mybir.dt.uint32
U16 = mybir.dt.uint16
U8 = mybir.dt.uint8
E4M3 = mybir.dt.float8_e4m3fn_x4
E5M2 = mybir.dt.float8_e5m2_x4
COPY = mybir.ActivationFunctionType.Copy
MULT = mybir.AluOpType.mult
SUB = mybir.AluOpType.subtract
ADD = mybir.AluOpType.add
EQUAL = mybir.AluOpType.is_equal

P = 128
LANES = 4
K_PASS = P * LANES
PASSES = V // K_PASS
QUADRANTS = 4
D_TILES = D // P
CHUNK = 128
CHUNKS = N // CHUNK
HALF = N // 2
LIST_COLS = CHUNK // 16
RUN = 2
WEAVE_RUN = 4


def tile_attend_gml_sq_kernel(tc, xT, wd_words, wd_scales, wv_words, wv_scales, y, cw, rw, offs, out):
    nc = tc.nc
    with ExitStack() as ctx:
        keep = ctx.enter_context(tc.tile_pool(name="keep", bufs=1))
        head = ctx.enter_context(tc.tile_pool(name="head", bufs=1))
        late = ctx.enter_context(tc.tile_pool(name="late", bufs=1))
        psum = ctx.enter_context(tc.psum_pool(name="psum", bufs=1))

        def bank(b, shape, name):
            return psum.tile(shape, F32, name=name, tag=f"bank{b}")

        offsets = keep.tile([P, N // 16], U16, name="offsets")
        wd_raw = [keep.tile([P, K_PASS], I32, name=f"wd_raw{o}", align_bytes=64) for o in range(PASSES)]
        wd_raw_scale = keep.tile([P, K_PASS], U8, name="wd_raw_scale", align_bytes=64)
        wd_codes = [keep.tile([P, K_PASS], I32, name=f"wd_codes{o}", align_bytes=64) for o in range(PASSES)]
        wd_scale = keep.tile([P, K_PASS], U8, name="wd_scale", align_bytes=64)
        wv_codes = [keep.tile([P, PASSES, D // 2], I32, name=f"wv_codes{h}", align_bytes=64) for h in range(2)]
        wv_scale = keep.tile([P, PASSES, D], U8, name="wv_scale", align_bytes=64)
        cw_sb = keep.tile([P, PASSES, 2 * LANES], F32, name="cw_sb")[:, :, 0:LANES]
        rw_cols = head.tile([P, LANES], F32, name="rw_cols", offset=768, align_bytes=64)
        rw_sb = keep.tile([P, N], F32, name="rw_sb")
        x_planes = [keep.tile([P, T], F32, name=f"x_plane{t}") for t in range(LANES)]
        x_first = keep.tile([P, CHUNK, LANES], BF16, name="x_first", align_bytes=64)
        x_rest = head.tile([P, LANES, N - CHUNK], BF16, name="x_rest", offset=0, align_bytes=64)
        x_second = keep.tile([P, CHUNK, LANES], BF16, name="x_second", align_bytes=64)
        x_late = keep.tile([P, HALF, LANES], BF16, name="x_late", align_bytes=64)
        x_groups = ((0, 1), (1, 2), (2, CHUNKS))
        x_codes = {c0: keep.tile([P, (c1 - c0) * CHUNK], U32, name=f"x_codes{c0}", align_bytes=64) for c0, c1 in x_groups}
        x_scale = {c0: keep.tile([P, (c1 - c0) * CHUNK], U8, name=f"x_scale{c0}", align_bytes=64) for c0, c1 in x_groups}
        y_sb = {(c, o): keep.tile([P, LANES, CHUNK], F32, name=f"y_sb{c}{o}") for c in range(CHUNKS) for o in range(PASSES) if c < 2 or o == 1}
        y_pair = keep.tile([P, LANES, HALF], F32, name="y_pair")
        weight = [keep.tile([P, PASSES, LANES, HALF], F32, name="weight0")]
        res = {}
        grad = [keep.tile([P, PASSES, K_PASS], BF16, name=f"grad{c}", align_bytes=64) for c in range(CHUNKS)]
        g_codes = [keep.tile([P, PASSES * CHUNK], U32, name=f"g_codes{c}", align_bytes=64) for c in range(CHUNKS)]
        g_scale = [keep.tile([P, PASSES * CHUNK], U8, name=f"g_scale{c}", align_bytes=64) for c in range(CHUNKS)]
        dx = keep.tile([P, D_TILES, N], F32, name="dx")
        windows = [keep.tile([P, T], F32, name=f"window{j}") for j in range(D_TILES)]
        ident = keep.tile([P, P], F32, name="ident")

        nc.gpsimd.memset(wd_raw_scale[:].bitcast(I32), 0)
        nc.gpsimd.memset(wv_scale[:].rearrange("p o d -> p (o d)").bitcast(I32), 0)
        ones = keep.tile([P, 32], F32, name="ones")
        by_column = keep.tile([P, 32], F32, name="by_column", align_bytes=64)
        by_partition = keep.tile([P, 32], F32, name="by_partition", align_bytes=64)
        nc.vector.memset(ones[:], 1.0)
        nc.vector.memset(ident[:], 0.0)
        nc.vector.tensor_tensor_scan(by_column[:], ones[:], ones[:], 0.0, MULT, ADD)
        nc.vector.transpose(by_partition[:], by_column[:])
        for q in range(QUADRANTS):
            rows = slice(32 * q, 32 * q + 32)
            nc.vector.tensor_tensor(ident[rows, rows], by_column[rows, :], by_partition[rows, :], EQUAL)

        x_rows = xT.rearrange("(p t) c -> t p c", t=LANES)
        y_rows = y.rearrange("(o p t) i -> o p t i", o=PASSES, t=LANES)
        wd_rows = wd_words[0].rearrange("p v t -> p (v t)").bitcast(I32)
        wv_rows = wv_words.rearrange("o p d t -> p o (d t)").bitcast(I32)

        def load_x(t):
            nc.sync.dma_start(x_planes[t][:], x_rows[t])

        def load_wd(o):
            nc.sync.dma_start(wd_raw[o][:], wd_rows[:, o * K_PASS : (o + 1) * K_PASS])

        def load_y(c, o):
            nc.sync.dma_start(y_sb[c, o][:], y_rows[o][:, :, c * CHUNK : (c + 1) * CHUNK])

        def load_wv(h):
            nc.sync.dma_start(wv_codes[h][:], wv_rows[:, :, h * (D // 2) : (h + 1) * (D // 2)])

        nc.sync.dma_start(rw_cols[:], rw[0, :].rearrange("(p j) -> p j", j=LANES))
        load_x(0)
        nc.sync.dma_start(cw_sb, cw.rearrange("(o p t) one -> p o (t one)", o=PASSES, t=LANES))
        nc.sync.dma_start(offsets[:], offs)
        load_x(1)
        load_x(2)
        for q in range(QUADRANTS):
            nc.sync.dma_start(
                wd_raw_scale[32 * q : 32 * q + 4 * PASSES, :].bitcast(I32),
                wd_scales[0, 4 * q : 4 * q + 4, :].bitcast(I32).rearrange("f (o c) -> o f c", o=PASSES),
            )
        load_x(3)
        load_wd(0)
        load_y(0, 0)
        load_wd(1)
        load_y(0, 1)
        for q in range(QUADRANTS):
            nc.sync.dma_start(
                wv_scale[32 * q : 32 * q + 4, :, :].bitcast(I32),
                wv_scales[:, 4 * q : 4 * q + 4, :].rearrange("o f d -> f o d").bitcast(I32),
            )
        load_wv(0)
        load_y(1, 0)
        load_y(1, 1)
        load_wv(1)
        nc.sync.dma_start(y_pair[:], y_rows[0][:, :, HALF:N])
        load_y(2, 1)
        load_y(3, 1)

        for j in range(2):
            nc.vector.memset(windows[j][:].bitcast(I32), 0)

        rw_bank = bank(7, [P, LANES, P], "rw_bank")
        for j in range(LANES):
            nc.tensor.transpose(rw_bank[:, j, :], rw_cols[:, j : j + 1].to_broadcast([P, P]), ident[:])
        nc.scalar.activation(rw_sb[:].rearrange("p (m j) -> p m j", j=LANES), rw_bank[:].rearrange("p j m -> p m j"), COPY)

        nc.gpsimd.tensor_copy(
            wd_scale[:].rearrange("p (t m) -> p t m", t=LANES),
            wd_raw_scale[:].rearrange("p (m t) -> p t m", t=LANES),
        )
        for j in range(2, D_TILES):
            nc.gpsimd.memset(windows[j][:].bitcast(I32), 0)

        def listed(c0, c1):
            return offsets[:, c0 * LIST_COLS : c1 * LIST_COLS]

        def gather_first(t):
            nc.vector.tensor_copy(x_first[:, :, t], x_planes[t][:].indirect(listed(0, 1)))

        def gather_rest(t, c0, c1):
            dst = x_rest[:, t, (c0 - 1) * CHUNK : (c1 - 1) * CHUNK]
            if t == 0:
                nc.vector.tensor_copy(dst, x_planes[t][:].indirect(listed(c0, c1)))
            else:
                nc.scalar.activation(dst, x_planes[t][:].indirect(listed(c0, c1)), COPY)

        def weave(dst, c0, c1):
            nc.scalar.copy(
                dst.rearrange("p (r i) t -> p r t i", i=WEAVE_RUN),
                x_rest[:, :, (c0 - 1) * CHUNK : (c1 - 1) * CHUNK].rearrange("p t (r i) -> p r t i", i=WEAVE_RUN),
            )

        def make_weight(h, o, on_scalar):
            src = rw_sb[:, h * HALF : (h + 1) * HALF]
            for t in range(LANES):
                if on_scalar:
                    nc.scalar.activation(weight[h][:, o, t, :], src, COPY, scale=cw_sb[:, o, t : t + 1])
                else:
                    nc.vector.tensor_scalar(weight[h][:, o, t, :], src, cw_sb[:, o, t : t + 1], None, MULT)

        def reorder_wd(o):
            nc.vector.tensor_copy(
                wd_codes[o][:].rearrange("p (t m) -> p m t", t=LANES),
                wd_raw[o][:].rearrange("p (m t) -> p m t", t=LANES),
            )

        def quantize_x(c0, src):
            nc.vector.quantize_mx(out=x_codes[c0][:].bitcast(E4M3), scales=x_scale[c0][:], in_=src.rearrange("p i t -> p (i t)"))

        def product(c, o, b):
            c0 = min(c, 2)
            cols = slice((c - c0) * CHUNK, (c - c0 + 1) * CHUNK)
            a_bank = bank(b, [P, LANES, CHUNK], f"a_bank{c}{o}")
            for t in range(LANES):
                nc.tensor.matmul_mx(
                    out=a_bank[:, t, :],
                    lhsT=wd_codes[o][:, t * P : (t + 1) * P].bitcast(E4M3),
                    lhsT_scale=wd_scale[4 * o : P, t * P : (t + 1) * P],
                    rhs=x_codes[c0][:, cols].bitcast(E4M3),
                    rhs_scale=x_scale[c0][:, cols],
                    start=True,
                    stop=True,
                )
            return a_bank

        def y_of(c, o):
            if (c, o) in y_sb:
                return y_sb[c, o][:]
            return y_pair[:, :, (c - 2) * CHUNK : (c - 1) * CHUNK]

        def subtract(c, o, a_bank):
            res[c, o] = late.tile([P, LANES, CHUNK], F32, name=f"res{c}{o}", offset=4096 * o)
            nc.vector.tensor_tensor(res[c, o][:], a_bank[:], y_of(c, o), SUB)

        def weigh(c, o):
            h, within = divmod(c * CHUNK, HALF)
            nc.vector.tensor_tensor(
                grad[c][:, o, :].rearrange("p (r i t) -> p r t i", i=RUN, t=LANES),
                res[c, o][:].rearrange("p t (r i) -> p r t i", i=RUN),
                weight[h][:, o, :, within : within + CHUNK].rearrange("p t (r i) -> p r t i", i=RUN),
                MULT,
            )

        def quantize_grad(c):
            nc.vector.quantize_mx(out=g_codes[c][:].bitcast(E5M2), scales=g_scale[c][:], in_=grad[c][:].rearrange("p o k -> p (o k)"))

        def back(c, h, b):
            dx_bank = bank(b, [P, 2, CHUNK], f"dx_bank{c}{h}")
            for jj in range(2):
                j = 2 * h + jj
                for o in range(PASSES):
                    nc.tensor.matmul_mx(
                        out=dx_bank[:, jj, :],
                        lhsT=wv_codes[h][:, o, jj * P : (jj + 1) * P].bitcast(E4M3),
                        lhsT_scale=wv_scale[:, o, j * P : (j + 1) * P],
                        rhs=g_codes[c][:, o * CHUNK : (o + 1) * CHUNK].bitcast(E5M2),
                        rhs_scale=g_scale[c][:, o * CHUNK : (o + 1) * CHUNK],
                        start=(o == 0),
                        stop=(o == PASSES - 1),
                    )
            return dx_bank

        def fetch(dst, dx_bank, on_scalar):
            if on_scalar:
                nc.scalar.copy(dst, dx_bank[:])
            else:
                nc.vector.tensor_copy(dst, dx_bank[:])

        def dx_cols(c, h):
            return dx[:, 2 * h : 2 * h + 2, c * CHUNK : (c + 1) * CHUNK]

        def scatter(j, c0, c1, src, on_scalar):
            window = windows[j][:].indirect(listed(c0, c1))
            if on_scalar:
                nc.scalar.activation(window, src, COPY)
            else:
                nc.vector.tensor_copy(window, src)

        def scatter_dx(j, c0, c1, on_scalar):
            scatter(j, c0, c1, dx[:, j, c0 * CHUNK : c1 * CHUNK], on_scalar)

        def store(j):
            nc.sync.dma_start(out[j * P : (j + 1) * P, :], windows[j][:])

        for t in range(LANES - 1):
            gather_first(t)
            gather_rest(t, 1, CHUNKS)
            if t < PASSES:
                make_weight(0, t, False)
        gather_first(LANES - 1)
        reorder_wd(0)
        quantize_x(0, x_first[:])
        a00 = product(0, 0, 0)
        reorder_wd(1)
        a01 = product(0, 1, 1)
        gather_rest(LANES - 1, 1, 2)
        weave(x_second[:], 1, 2)
        gather_rest(LANES - 1, 2, CHUNKS)
        weave(x_late[:], 2, CHUNKS)
        weight.append(head.tile([P, PASSES, LANES, HALF], F32, name="weight1", offset=0, align_bytes=64))
        for o in range(PASSES):
            make_weight(1, o, True)
        subtract(0, 0, a00)
        quantize_x(1, x_second[:])
        a10 = product(1, 0, 2)
        a11 = product(1, 1, 3)
        subtract(0, 1, a01)
        weigh(0, 0)
        quantize_x(2, x_late[:])
        a20 = product(2, 0, 0)
        a21 = product(2, 1, 1)
        weigh(0, 1)
        subtract(1, 0, a10)
        quantize_grad(0)
        for h in range(2):
            fetch(dx_cols(0, h), back(0, h, 4 + h), True)
            for jj in range(2):
                scatter_dx(2 * h + jj, 0, 1, True)
        subtract(1, 1, a11)
        a30 = product(3, 0, 2)
        a31 = product(3, 1, 3)
        weigh(1, 0)
        weigh(1, 1)
        subtract(2, 0, a20)
        quantize_grad(1)
        fetch(dx_cols(1, 0), back(1, 0, 6), True)
        for j in range(2):
            scatter_dx(j, 1, 2, True)
        b1 = back(1, 1, 7)
        subtract(2, 1, a21)
        weigh(2, 0)
        weigh(2, 1)
        subtract(3, 0, a30)
        quantize_grad(2)
        fetch(dx_cols(2, 0), back(2, 0, 4), True)
        for j in range(2):
            scatter_dx(j, 2, 3, True)
        b2 = back(2, 1, 5)
        subtract(3, 1, a31)
        weigh(3, 0)
        weigh(3, 1)
        dx_late = late.tile([P, 2, N - CHUNK], F32, name="dx_late", offset=0)
        fetch(dx_late[:, :, 0:CHUNK], b1, False)
        quantize_grad(3)
        a3 = back(3, 0, 6)
        b3 = back(3, 1, 0)
        scatter(2, 1, 2, dx_late[:, 0, 0:CHUNK], False)
        fetch(dx_late[:, :, CHUNK : 2 * CHUNK], b2, True)
        fetch(dx_cols(3, 0), a3, False)
        scatter_dx(1, 3, 4, False)
        store(1)
        scatter_dx(0, 3, 4, True)
        store(0)
        fetch(dx_late[:, :, 2 * CHUNK : 3 * CHUNK], b3, True)
        scatter(2, 2, 4, dx_late[:, 0, CHUNK : 3 * CHUNK], True)
        store(2)
        scatter(3, 1, 4, dx_late[:, 1, :], False)
        store(3)
